import numpy as np, ml_dtypes
CORES = [1,5,17,21,33,37,49,53]
N = 8
BF = ml_dtypes.bfloat16
W, VI, CR, S, EV = 1536, 256, 16, 2, 1
V = W - VI
R, NEED, DT, DL = 0.75, 9, 0.0625, 0.1875
def invol(rng, lone):
    o = np.argsort(rng.random((N, 8, CR, W)), axis=-1); x, y = o[..., 0::2], o[..., 1::2]; m = rng.random(x.shape) < lone
    c = np.empty((N, 8, CR, W), np.int64)
    np.put_along_axis(c, x, np.where(m, x, y), -1); np.put_along_axis(c, y, np.where(m, y, x), -1)
    return c
def join(row, x, y):
    p, s = int(row[x]), int(row[y])
    if p == y: return
    row[x] = y; row[y] = x
    if p != x and s != y: row[p] = s; row[s] = p
    elif p != x: row[p] = p
    elif s != y: row[s] = s
def signs(rng, shape): return np.where(rng.random(shape) < 0.5, -1.0, 1.0)
def parts(rng):
    sh = (N, 8, 16, W)
    q = 2.0 * rng.random(sh) - 1.0; v = signs(rng, sh) * (0.5 + 1.5 * rng.random(sh)); k = 0.125 + 0.375 * rng.random(sh)
    a = 2.0 * rng.random((N, 8, W)) - 1.0; con = invol(rng, 0.02)
    u = rng.random((N, 8, W)); far = rng.integers(0, CR, (N, 8, W))
    cur = (rng.integers(0, CR, (N, 8, 1)) + np.where(u < 0.7, 0, np.where(u < 0.8, 1, np.where(u < 0.9, 2, far)))) & (CR - 1)
    return q, v, k, a, con, cur
def small(x, least):
    return np.where(np.abs(x) < least, 0.0, x).astype(np.float32).astype(BF)
def camps(rng, near):
    o = rng.permutation(W); h = W // 2; side = np.empty(W); side[o[:h]] = 1.0; side[o[h:]] = -1.0
    rows = np.empty((CR, W), np.int64)
    for m in range(CR):
        x, y = rng.permutation(o[:h]), rng.permutation(o[h:])
        if near[m]: x, y = np.concatenate([x[0::2], y[0::2]]), np.concatenate([x[1::2], y[1::2]])
        rows[m, x] = y; rows[m, y] = x
    return side, rows
def brink(rng):
    F = np.float32; n = 2 ** 18
    ki = (rng.integers(160, 256, n) * 2.0 ** -9).astype(F); kj = (rng.integers(160, 256, n) * 2.0 ** -9).astype(F)
    vi = (rng.integers(128, 256, n) * 2.0 ** -7).astype(F); vj = (rng.integers(-255, -127, n) * 2.0 ** -21).astype(F)
    dv = vi - vj; kk = ki * kj; p = kk * dv; x = kk.astype(np.float64) * dv.astype(np.float64)
    t = DT * ((vi - p).astype(np.float64) - (vj + p).astype(np.float64))
    hi = small(t, 2.0 ** -20).astype(F); lo = small(t - hi, 2.0 ** -20).astype(F)
    def behind(a, b): return (F(DT) * a - hi) - (lo + F(DT) * b) < 0
    right = behind(vi - p, vj + p)
    wrong = (behind(vi - ki * (kj * dv), vj + kj * (ki * dv)), behind(vi - x, vj + x), behind((vi - x).astype(F), (vj + x).astype(F)))
    best = np.stack([np.argsort(right == w, kind="stable")[:96] for w in wrong])
    return np.stack([-hi, lo, vi, vj, ki, kj])[:, best]
def pack(q, v, k, a, con, cur):
    return {"q0": small(q, 2.0 ** -20).reshape(N, 128, W), "v0": small(v, 2.0 ** -16).reshape(N, 128, W), "kap": k.astype(np.float32).astype(BF).reshape(N, 128, W), "aim": small(a, 2.0 ** -20),
            "con": np.ascontiguousarray(con.reshape(N, 8 * CR, W)).astype(np.int32), "cur": np.ascontiguousarray(cur).astype(np.int32)}
def setup_inputs(rng):
    return pack(*parts(rng))
def setup_inputs_calm(rng):
    q, v, k, a, con, cur = parts(rng); v = v * 0.5
    g = np.arange(8)[None, :, None]; r = np.arange(N)[:, None, None]
    cur = (np.where(r % 2 == 0, g - 2, CR - 3 - g) & (CR - 1)) + np.zeros((N, 8, W), np.int64)
    return pack(q, v, k, a, con, cur)
def setup_inputs_corners(rng):
    q, v, k, a, con, cur = parts(rng); s = int(rng.integers(0, 8)); here = np.arange(W)
    for r in range(N):
        for g in range(8):
            z = (g + 3 * r + s) % 8
            if z == 0: con[r, g] = here
            elif z == 1:
                join(con[r, g, 0], 0, W - 1); con[r, g] = con[r, g, 0].copy(); q[r, g] = q[r, g] * 0.25
            elif z == 2: k[r, g] = np.where(rng.random((16, W)) < 0.5, 0.0625, 0.5)
            elif z == 3: q[r, g] = q[r, g, :, :1].copy()
            elif z == 4:
                side, rows = camps(rng, [m % 2 == 1 for m in range(CR)])
                con[r, g] = rows; q[r, g] = side[None, :] * (0.75 + 0.25 * rng.random((16, W))); cur[r, g] = 2 * int(rng.integers(0, CR // 2))
            elif z == 5:
                for m in range(CR):
                    x, y = 1 + m, W - 2 - m
                    join(con[r, g, m], 0, x); join(con[r, g, m], W - 1, y)
                    q[r, g, :, x] = q[r, g, :, 0]; q[r, g, :, y] = q[r, g, :, W - 1]; cur[r, g, x] = m; cur[r, g, y] = m
            elif z == 6:
                for m in range(CR):
                    o = rng.permutation(V); row = con[r, g, m]; h = (V - VI) // 2
                    row[V:] = o[:VI]; row[o[:VI]] = V + np.arange(VI)
                    x, y = o[VI:VI + h], o[VI + h:]
                    row[x] = y; row[y] = x
            else:
                side, rows = camps(rng, [1 <= m <= CR - 3 for m in range(CR)])
                con[r, g] = rows; q[r, g] = side[None, :] * (0.75 + 0.25 * rng.random((16, W))); cur[r, g] = CR - 1 - rng.integers(0, 2, W)
    return pack(q, v, k, a, con, cur)
def setup_inputs_ends(rng):
    q, v, k, a, con, cur = parts(rng); q = signs(rng, q.shape)
    for r in range(N):
        for g in range(8):
            for m in (0, CR - 1):
                join(con[r, g, m], 0, W - 1); join(con[r, g, m], 1, W - 2)
            e = 1.0 if (r + g) % 2 == 0 else -1.0
            q[r, g, :, W - 1] = e * q[r, g, :, 0]; q[r, g, :, W - 2] = -e * q[r, g, :, 1]
    v = np.where(rng.random(q.shape) < 0.875, -2.0, 2.0) * q
    k = np.where(rng.random(q.shape) < 0.8, 0.5, 0.0625); a = signs(rng, a.shape)
    cur = np.where(rng.random(cur.shape) < 0.75, 0, CR - 1)
    return pack(q, v, k, a, con, cur)
def setup_inputs_spread(rng):
    q, v, k, a, con, cur = parts(rng); sh = (N, 8, 16, W); one = (N, 8, 1, W)
    q = q * np.exp2(-rng.random(one)); v = signs(rng, sh) * (0.5 + 0.5 * rng.random(sh)) * np.exp2(2.0 * rng.random(one) - 1.0)
    k = (0.25 + 0.25 * rng.random(sh)) * np.exp2(-2.0 * rng.random(one)); a = a * np.exp2(-2.0 * rng.random(a.shape))
    cur = np.where(rng.random((N, 8, 1)) < 0.5, rng.integers(0, CR, cur.shape), cur)
    return pack(q, v, k, a, con, cur)
def setup_inputs_ties(rng):
    q, v, k, a, con, cur = parts(rng); edge = brink(rng)
    q = rng.integers(-8, 9, q.shape) * 0.125; v = rng.integers(-1, 2, v.shape) * 2.0; k = np.where(rng.random(k.shape) < 0.9, 0.5, 0.0625); a = rng.integers(-8, 9, a.shape) * 0.125
    for r in range(N):
        for g in range(8):
            b = int(rng.integers(0, CR)); row = con[r, g, b]; x = np.flatnonzero(np.arange(W) < row); x = rng.permutation(x)[:len(x) // 4]; y = row[x]
            n = rng.integers(NEED - 1, NEED + 1, len(x)); low = rng.integers(-8, 2, (16, len(x))); place = np.argsort(rng.random((16, len(x))), axis=0)
            q[r, g][:, x] = low * 0.125; q[r, g][:, y] = (low + np.where(place < n[None, :], 6, 7)) * 0.125; v[r, g][:, y] = v[r, g][:, x]
            cur[r, g] = (cur[r, g] - cur[r, g, 0] + b) & (CR - 1); cur[r, g, x] = b; cur[r, g, y] = b
            o = rng.permutation(V)
            for p in range(4):
                x, y = int(o[2 * p]), int(o[2 * p + 1]); e = signs(rng, 16)
                for m in range(CR): join(con[r, g, m], x, y)
                a[r, g, x] = 0.25; a[r, g, y] = -0.25
                if p < 2: z = edge[:, np.arange(16) % 3, rng.integers(0, 96, 16)].astype(np.float64)
                else:
                    lane = rng.permutation(16); near = lane < 8; one = lane == 8
                    z = np.stack([np.where(near, -0.25, np.where(one, 0.75, -0.875)), np.where(near, 0.25, np.where(one, 2.0 ** -20, 0.875)),
                                  np.where(near, 1.0, 0.0), np.where(near, -1.0, np.where(one, -129.0 * 2.0 ** -23, 0.0)), np.full(16, 0.375), np.full(16, 0.375)])
                q[r, g, :, x] = e * z[0]; q[r, g, :, y] = e * z[1]; v[r, g, :, x] = e * z[2]; v[r, g, :, y] = e * z[3]; k[r, g, :, x] = z[4]; k[r, g, :, y] = z[5]
    return pack(q, v, k, a, con, cur)
def check_ranges(d):
    bad = []
    for n, lo, hi, least in (("q0", -1.0, 1.0, 2.0 ** -20), ("v0", -2.0, 2.0, 2.0 ** -16), ("kap", 0.0625, 0.5, 0.0625), ("aim", -1.0, 1.0, 2.0 ** -20)):
        x = np.asarray(d[n]).astype(np.float64); s = np.abs(x)
        if not np.all((x >= lo) & (x <= hi) & ((s == 0) | (s >= least))): bad.append("range of " + n)
    for n, hi in (("con", W - 1), ("cur", CR - 1)):
        if np.min(d[n]) < 0 or np.max(d[n]) > hi: bad.append("range of " + n)
    if "range of con" not in bad:
        c = np.asarray(d["con"]).astype(np.int64)
        if np.any(np.take_along_axis(c, c, 2) != np.arange(W)): bad.append("a row of con is no involution")
    return bad
def pick(x, j):
    y = np.empty_like(x)
    for r in range(N):
        for g in range(8): y[r, g] = np.take(x[r, g], j[r, g], axis=1)
    return y
def travel(x, d):
    y = x.copy(); H = V + VI // 2
    y[..., V:H] = np.roll(x[..., V:H], (d, d), axis=(0, 1)); y[..., H:] = np.roll(x[..., H:], (d, 4 * d), axis=(0, 1))
    return y
def reference(q0, v0, kap, aim, con, cur):
    F = np.float32; sh = (N, 8, 16, W)
    qs = q0.astype(F).reshape(sh); vs = v0.astype(F).reshape(sh); ks = kap.astype(F).reshape(sh); target = aim.astype(F).reshape(N, 8, 1, W)
    ct = con.astype(np.int64).reshape(N, 8, CR, W); cs = cur.astype(np.int64).reshape(N, 8, W); here = np.arange(W)[None, None, :]
    total = ks.astype(np.float64)
    for shot in range(2):
        q, v, k, c, log = qs, vs, ks, cs, []
        for t in range(1, S + 1):
            j0 = np.take_along_axis(ct, c[:, :, None, :], 2)[:, :, 0]; j1 = np.take_along_axis(ct, ((c + 1) & (CR - 1))[:, :, None, :], 2)[:, :, 0]
            d0 = q - pick(q, j0); d1 = q - pick(q, j1)
            o0 = np.sum(np.abs(d0) <= F(R), axis=2) >= NEED; o1 = np.sum(np.abs(d1) <= F(R), axis=2) >= NEED
            some = o0 | o1; j = np.where(o0, j0, np.where(o1, j1, here)); choice = np.where(some, j, -1)
            mutual = some & (np.take_along_axis(choice, j, 2) == here)
            dq = np.where(o0[:, :, None], d0, d1); dv = v - pick(v, j); kj = pick(k, j)
            hit = mutual[:, :, None] & (dq * dv < F(0))
            kk = np.where(hit, k * kj, F(0)); w = np.where(hit, kj.astype(np.float64) * dv, 0.0); log.append((j, kk, w))
            v = v - kk * dv
            c = np.where(mutual & o0, c + 1, c + 2) & (CR - 1)
            q = q + F(DT) * v
            if t % EV == 0 and t < S: q, v, k = travel(q, 1), travel(v, 1), travel(k, 1)
        aq = q - target; av = np.zeros(sh, F); gain = np.zeros(sh, np.float64)
        for t in range(S, 0, -1):
            if t % EV == 0 and t < S: aq, av, gain = travel(aq, -1), travel(av, -1), travel(gain, -1)
            av = av + F(DT) * aq
            j, kk, w = log[t - 1]; da = av - pick(av, j)
            gain = gain - w * da.astype(np.float64)
            av = av - kk * da
        total = total + gain
        vs = vs - np.clip(av, F(-DL), F(DL))
    return {"yg": total.reshape(N, 128, W).astype(np.float32), "yv": vs.reshape(N, 128, W).astype(np.float32)}

def check_inputs(d):
    bad = list(check_ranges(d))
    if not bad:
        for name, y in reference(**d).items():
            for q in range(N):
                v = np.abs(np.asarray(y[q], np.float64)); s = np.sqrt(np.mean(v * v))
                if v.max() > 14 * s or s < 2.0 ** -4: bad.append('%s of rank %d is uneven or too small' % (name, q))
    return bad

@@ -1,0 +1,721 @@
+from concourse.mybir import AluOpType, ActivationFunctionType
+
+W, V = 1536, 1280
+H = V + 128
+L1, L2 = 16.0, 4096.0
+EPS = 2.0 ** -11
+SQ = 0.5625 + 2.0 ** -24
+
+F, B, HF, I, U = "float32", "bfloat16", "float16", "int32", "uint16"
+SCRATCH = {}
+for _n in ("V1a", "V1b", "CP", "q1", "CQ", "D0", "D1", "E1a", "E1b", "E2", "Wn", "io2", "A", "A2a", "A2b", "DA", "KS", "KH1",
+           "S1", "Y2a", "Y2b", "V0p", "V0q", "ZZ", "R0"):
+    SCRATCH[_n] = ("sbuf", [128, W], F)
+for _n in ("q0s", "q0c", "v0s", "K1", "v0c", "V0b", "OH", "F0", "F1", "QB", "KM", "AM1", "AM2"):
+    SCRATCH[_n] = ("sbuf", [128, W], B)
+SCRATCH.update({
+    "cons": ("sbuf", [128, W], I), "X": ("sbuf", [128, W], HF), "K2": ("sbuf", [128, W + 256], B),
+    "aims": ("sbuf", [128, W], B), "curs": ("sbuf", [128, 96], I), "curh": ("sbuf", [128, 96], HF),
+    "R": ("sbuf", [128, 2048], HF), "io3": ("sbuf", [128, 128], B), "vv": ("sbuf", [128, 256], I),
+    "v15": ("sbuf", [128, 144], I), "v127": ("sbuf", [128, 256], I), "pc": ("sbuf", [128, 4], I), "pm": ("sbuf", [128, 4], I),
+    "col": ("sbuf", [128, 16], F), "Bm": ("sbuf", [128, 128], B), "U0": ("sbuf", [128, 144], B), "U1": ("sbuf", [128, 144], B),
+    "U2": ("sbuf", [128, 144], B), "C01": ("sbuf", [128, 128], B), "C23": ("sbuf", [128, 128], B),
+    "Zb": ("sbuf", [128, 144], B), "Zh": ("sbuf", [128, 144], HF), "IIf": ("sbuf", [128, 256], F), "IIb": ("sbuf", [128, 256], B),
+    "NIb": ("sbuf", [128, 128], B), "NIf": ("sbuf", [128, 128], F), "L1b": ("sbuf", [128, 128], B), "L2b": ("sbuf", [128, 128], B),
+    "B8": ("sbuf", [128, 128], B), "B8a": ("sbuf", [128, 128], B), "B8b": ("sbuf", [128, 128], B), "N256": ("sbuf", [128, 128], B),
+    "iwr": ("sbuf", [128, 96], F), "iw": ("sbuf", [128, 96], F),
+    "Si": ("sbuf", [128, 192], I), "J": ("sbuf", [128, 384], I), "J2": ("sbuf", [128, 192], F),
+    "Ju": ("sbuf", [128, 192], U), "J2u": ("sbuf", [128, 192], U), "dJ": ("sbuf", [128, 192], F), "dJ2": ("sbuf", [128, 192], F),
+    "o0": ("sbuf", [128, 96], F), "o0k": ("sbuf", [128, 96], F), "s1": ("sbuf", [128, 96], F), "s2": ("sbuf", [128, 96], F), "s3": ("sbuf", [128, 96], F),
+    "s4": ("sbuf", [128, 96], F), "s5": ("sbuf", [128, 192], F), "s6": ("sbuf", [128, 192], F), "jf": ("sbuf", [128, 96], F),
+    "jh": ("sbuf", [128, 96], HF), "j1u": ("sbuf", [128, 96], U), "j2u": ("sbuf", [128, 96], U),
+    "V1v": ("sbuf", [128, 256], F), "A2v": ("sbuf", [128, 256], F), "Yv": ("sbuf", [128, 256], F),
+    "t0": ("sbuf", [128, 512], B), "t1": ("sbuf", [128, 256], F), "t2": ("sbuf", [128, 256], F),
+    "t3": ("sbuf", [128, 256], F), "t4": ("sbuf", [128, 256], F), "t5": ("sbuf", [128, 256], F),
+    "PA": ("psum", [128, W], F), "PB": ("psum", [128, W], F), "PC": ("psum", [128, 512], F), "PD": ("psum", [128, 512], F),
+})
+SEMAPHORES = ["pe", "dve", "act", "pool", "sent"] + ["d%d" % _i for _i in range(40)] + ["r%d" % _i for _i in range(6)]
+
+OPT = {"lea": 1, "leb": 2, "le0": 1, "st2": 2.5, "st1": 1.5, "look": 60, "heat": 300, "tries": 5000, "fold": 0,
+       "q1pe": 0, "cqdma": 0, "rk": 1, "c4": 0, "aqpe": 0, "v0pe": 0}
+CASES = [(1.56, 0.45, 150, 4000), (1.9, 0.42, 200, 5000), (1.3, 0.7, 120, 3500)]
+KEPT = {}
+
+
+def rank_program(g, core, T, topo):
+    rank = T.rank_of(core)
+    if rank is None:
+        return
+    op, fn = AluOpType, ActivationFunctionType
+    n = len(T.cores)
+    nxt, prv = T.cores[(rank + 1) % n], T.cores[(rank - 1) % n]
+    Q = {"pe": g.tensor, "dve": g.vector, "act": g.scalar, "pool": g, "sp": g.sync}
+    count = {"pe": 0, "dve": 0, "act": 0, "pool": 0, "dma": 0, "sent": 0}
+    seen = {q: {} for q in Q}
+    hist = {}
+    dmas = []
+    opened = {}
+
+    def S(name, a=0, b=None, step=1, parts=128):
+        b = T[name].shape[1] if b is None else b
+        ap = T[name][0:parts, a:b:step] if step > 1 else T[name][0:parts, a:b]
+        return (name, a, b, ap)
+
+    def G(win, off, a, b, o=0):
+        return (win, 0, W, T[win][:, 0:W].indirect(T[off][:, o + a // 16:o + b // 16]), (off, o + a // 16, o + b // 16, None))
+
+    def deps(q, reads, writes):
+        need = {}
+        for xs, wr in ((reads, False), (writes, True)):
+            for x in xs:
+                ps = SCRATCH.get(x[0], ("",))[0] == "psum"
+                for lo, hi, q2, tok, w2 in hist.get(x[0], []):
+                    if q == "pe" and q2 == "pe":
+                        continue
+                    if ps and q2 != q:
+                        hit = lo // 512 <= (x[2] - 1) // 512 and x[1] // 512 <= (hi - 1) // 512
+                    else:
+                        hit = (wr or w2) and lo < x[2] and x[1] < hi
+                    if hit:
+                        need[tok[0]] = max(need.get(tok[0], 0), tok[1])
+        for s, c in need.items():
+            if seen[q].get(s, 0) < c:
+                Q[q].wait_ge(T.sem[s], c)
+                seen[q][s] = c
+
+    def note(q, reads, writes, tok):
+        for x in writes:
+            hist[x[0]] = [h for h in hist.get(x[0], []) if not (x[1] <= h[0] and h[1] <= x[2])]
+        for xs, wr in ((reads, False), (writes, True)):
+            for x in xs:
+                hist.setdefault(x[0], []).append((x[1], x[2], q, tok, wr))
+
+    calls = []
+
+    def run(q, make, reads, writes, cost):
+        reads = list(reads) + [x[4] for x in reads if len(x) > 4]
+
+        def emit():
+            deps(q, reads, writes)
+            count[q] += 1
+            make().then_inc(T.sem[q], 1)
+            note(q, reads, writes, (q, count[q]))
+        calls.append((q, emit, reads, writes, cost, "lat"))
+
+    def size(x):
+        return int(SCRATCH[x[0]][2][-2:]) // 8 if x[0] in SCRATCH else 4
+
+    def price(out, a, m, more=0):
+        if len(a) > 4:
+            return (50, (out[2] - out[1]) * 0.83, 0)
+        return (max(64, (out[2] - out[1]) * m) * 0.83 + more, 0, 0)
+
+    def half(out, a):
+        return 0.5 if size(out) == 2 and size(a) == 2 else 1
+
+    def tt(out, a, b, o):
+        both = SCRATCH[a[0]][0] == SCRATCH[b[0]][0]
+        run("dve", lambda: g.vector.tensor_tensor(out[3], a[3], b[3], o), [a, b], [out], price(out, a, 2 if both else 1))
+
+    def ts(out, a, s1, o0, s2=None, o1=None):
+        cols = [s for s in (s1, s2) if isinstance(s, tuple)]
+        x1, x2 = [s[3] if isinstance(s, tuple) else s for s in (s1, s2)]
+        if o1 is None:
+            run("dve", lambda: g.vector.tensor_scalar(out[3], a[3], x1, None, o0), [a] + cols, [out], price(out, a, half(out, a)))
+        else:
+            run("dve", lambda: g.vector.tensor_scalar(out[3], a[3], x1, x2, o0, o1), [a] + cols, [out], price(out, a, half(out, a)))
+
+    def cp(out, a):
+        run("dve", lambda: g.vector.tensor_copy(out[3], a[3]), [a], [out], price(out, a, half(out, a)))
+
+    def act(out, a, f, bias=0.0, scale=1.0):
+        run("act", lambda: g.scalar.activation(out[3], a[3], f, bias=bias, scale=scale), [a], [out],
+            price(out, a, 1, 1400 if f in (fn.Ln, fn.Exp) else 0))
+
+    def act3(out, a, f, bias=0.0, scale=1.0):
+        for k in range(0, W, 512):
+            act(S(out, k, k + 512), S(a, k, k + 512), f, bias, scale)
+
+    def mm(items, wide=None):
+        items = [list(it) for it in items]
+        for it in items:
+            key = (it[0][0], it[0][1] // 512)
+            if not it[3]:
+                opened[key][4] = False
+            opened[key] = it
+
+        def make():
+            for o, l, r, s0, s1 in items:
+                ins = g.tensor.matmul(o[3], l[3], r[3], s0, s1)
+            return ins
+        cost = (0, 0, sum(max(64, wide or it[0][2] - it[0][1]) * (4 if size(it[2]) == 4 else 1) for it in items))
+        run("pe", make, [x for it in items for x in it[1:3]], [it[0] for it in items], cost)
+
+    def iota(out, pat, base, cm, small=True):
+        cost = (130 + 1.66 * (out[2] - out[1]), 0, 0)
+        if small:
+            run("pool", lambda: g.iota(out[3], pat, base, cm, allow_small_or_imprecise_dtypes=True), [], [out], cost)
+        else:
+            run("pool", lambda: g.iota(out[3], pat, base, cm), [], [out], cost)
+
+    def dma(q, out, a, add=False):
+        def emit():
+            deps(q, [a], [out])
+            s = "d%d" % count["dma"]
+            count["dma"] += 1
+            ins = g.dma_start(out[3], a[3], accum_op=op.add) if add else Q[q].dma_start(out[3], a[3])
+            ins.then_inc(T.sem[s], 16)
+            note("dma", [a], [out], (s, 16))
+            dmas.append(s)
+        calls.append((q, emit, [a], [out], (1000 if add else 60, 0, 0), 2000 + (out[2] - out[1]) * size(out) * (0.5 if add else 0.25)))
+
+    def D(name, a=0, b=W):
+        return (name, a, b, T[name][:, a:b])
+
+    def send(k, dst, src, land):
+        def emit():
+            deps("pool", [src], [])
+            eng = topo.engines(core, dst)[:8]
+            rid, pid, _ = topo.addr(dst)
+            g.remote_dma(land[3], src[3], T.sem["r%d" % k], T.sem.sent, pid, rid, sum(1 << e for e in eng))
+            count["sent"] += len(eng)
+            other = prv if dst == nxt else nxt
+            note("dma", [], [land], ("r%d" % k, len(topo.engines(other, core)[:8])))
+        calls.append(("pool", emit, [src], [land], (500, 0, 0), "rem"))
+
+    def banks(x):
+        return [(x[0], k) for k in range(x[1] // 512, (x[2] - 1) // 512 + 1)] if SCRATCH.get(x[0], ("",))[0] == "psum" else []
+
+    def issue():
+        m = len(calls)
+        pred = [set() for _ in range(m)]
+        log, lastpe = {}, {}
+        for i, (q, _, reads, writes, _, _) in enumerate(calls):
+            for xs, wr in ((reads, False), (writes, True)):
+                for x in xs:
+                    for lo, hi, j, w2 in log.get(x[0], []):
+                        if (wr or w2) and lo < x[2] and x[1] < hi and j != i:
+                            pred[i].add(j)
+            for x in writes:
+                log[x[0]] = [h for h in log.get(x[0], []) if not (x[1] <= h[0] and h[1] <= x[2])]
+                if q == "pe":
+                    for bk in banks(x):
+                        if lastpe.get(bk, i) != i:
+                            pred[i].add(lastpe[bk])
+                        lastpe[bk] = i
+            for xs, wr in ((reads, False), (writes, True)):
+                for x in xs:
+                    log.setdefault(x[0], []).append((x[1], x[2], i, wr))
+        succ = [[] for _ in range(m)]
+        for i in range(m):
+            for j in pred[i]:
+                succ[j].append(i)
+        qs = [c[0] for c in calls]
+        bk = [list(set(b for x in c[2] + c[3] for b in banks(x))) for c in calls]
+        cases = []
+        for gat, pe, lat, rem in CASES:
+            cases.append(([c[4][0] + c[4][1] * gat + c[4][2] * pe for c in calls], [{"lat": lat, "rem": rem}.get(c[5], c[5]) for c in calls]))
+
+        def walk(case, order=None, rank_of=None):
+            cost, late = case
+            left = [len(p) for p in pred]
+            at = [0.0] * m
+            free = {q: 0.0 for q in Q}
+            held = {}
+            ready = {q: [i for i in range(m) if not left[i] and qs[i] == q] for q in Q}
+            made, end = [], 0.0
+
+            def start(i, q):
+                t = max(at[i], free[q])
+                for b in bk[i]:
+                    if b in held and held[b][0] != q and held[b][1] > t:
+                        t = held[b][1]
+                return t
+            for step in range(m):
+                if order:
+                    i = order[step]
+                    q = qs[i]
+                    t = start(i, q)
+                else:
+                    t0 = 1e18
+                    for z in Q:
+                        if ready[z] and free[z] < t0:
+                            ts0 = [(start(i, z), i) for i in ready[z]]
+                            t1 = min(ts0)[0]
+                            if t1 < t0:
+                                t0, q, pick = t1, z, ts0
+                    t, i = max((z for z in pick if z[0] <= t0 + OPT["look"]), key=lambda z: rank_of[z[1]])
+                    ready[q].remove(i)
+                    made.append(i)
+                free[q] = t + cost[i]
+                done = free[q] + late[i]
+                end = max(end, done)
+                for b in bk[i]:
+                    held[b] = (q, done)
+                for j in succ[i]:
+                    d = free[q] if q == "pe" and qs[j] == "pe" else done
+                    if d > at[j]:
+                        at[j] = d
+                    left[j] -= 1
+                    if not left[j] and not order:
+                        ready[qs[j]].append(j)
+            return made, end
+
+        if "order" not in KEPT:
+            rest = [0.0] * m
+            for i in range(m - 1, -1, -1):
+                rest[i] = cases[0][0][i] + cases[0][1][i] + max([rest[j] for j in succ[i]] + [0.0])
+            seed = [12345]
+
+            def rnd():
+                seed[0] = (seed[0] * 1103515245 + 12345) % 2 ** 31
+                return seed[0] / 2.0 ** 31
+
+            def score(r):
+                o, e = walk(cases[0], rank_of=r)
+                return e + sum(walk(c, o)[1] for c in cases[1:]), o
+            best, order = score(rest)
+            top = (best, order)
+            for it in range(OPT["tries"]):
+                r = list(rest)
+                k = int(rnd() * m)
+                amp = 300 + 2500 * rnd() ** 2
+                if rnd() < 0.5:
+                    for i in order[k:k + 2 + int(rnd() * 14)]:
+                        r[i] += amp * (rnd() - 0.5)
+                else:
+                    up, c = amp * (rnd() - 0.5) * 2, calls[order[k]][3][0][1] // 512
+                    for i in order[k:k + 5 + int(rnd() * 50)]:
+                        if calls[i][3][0][1] // 512 == c:
+                            r[i] += up
+                s, o = score(r)
+                if s <= best + OPT["heat"] * (1 - it / OPT["tries"]) ** 2 * rnd() ** 3:
+                    best, order, rest = s, o, r
+                    if s < top[0]:
+                        top = (s, o)
+            KEPT["order"], KEPT["best"] = top[1], top[0] / len(cases)
+        for i in list(range(loads)) + [i for i in KEPT["order"] if i >= loads]:
+            calls[i][1]()
+
+    C3 = [(0, 512), (512, 1024), (1024, W)]
+    CL = [C3[2], C3[0], C3[1]]
+    CV = [(V, W), (0, 512), (512, 1024), (1024, V)]
+    cv, c0, c1, c2 = CV
+
+    def wrap(bank, z, src, chunks=((0, W),)):
+        for a, b in chunks:
+            mm([(S(bank, a // 16, b // 16), S(z, 15 - l, 143 - l), S(src, a + l, b, 16), l == 0, l == 15) for l in range(16)])
+
+    def wrap2(bank, z, src, a, b):
+        if b >= 1024:
+            wrap(bank, z, src, [(0, 1024) if b == 1024 else (a, b)])
+
+    def shift(bank, ii, src, a, back, o=0):
+        k = 16 if back else 112
+        mm([(S(bank, o, o + 128), S(ii, k, k + 128), S(src, a, a + 128), True, True),
+            (S(bank, o + 128, o + 256), S(ii, 64, 192), S(src, a + 128, a + 256), True, True)])
+
+    def stagger(steps, chunks, lag):
+        for _, c, k in sorted((k + lag * c, c, k) for c in range(len(chunks)) for k in range(len(steps))):
+            steps[k](*chunks[c])
+
+    dma("sp", S("curs"), ("cur", 0, W, T.cur[:]))
+    for a, b in C3:
+        dma("sp", S("cons", a, b), D("con", a, b))
+    dma("sp", S("q0s"), D("q0"))
+    dma("sp", S("q0c"), D("q0"))
+    dma("sp", S("K1"), D("kap"))
+    dma("sp", S("v0s"), D("v0"))
+    dma("sp", S("v0c"), D("v0"))
+    dma("sp", S("K2", 0, V), D("kap", 0, V))
+    dma("sp", S("aims", parts=8), ("aim", 0, W, T.aim[:]))
+    loads = len(calls)
+    for i in range(loads):
+        calls[i] = calls[i][:5] + (2000 + sum((c[3][0][2] - c[3][0][1]) * size(c[3][0]) * 0.22 for c in calls[:i + 1]),)
+
+    iota(S("io3"), [[16, 8], [0, 16]], 0, -1)
+    iota(S("pc", 0, 1), [[0, 1]], 0, 1, False)
+    iota(S("vv"), [[1, 256]], 128, -1, False)
+    iota(S("iwr"), [[16, 96]], 0, 0)
+    for l in range(16):
+        ts(S("R", 128 * l, 128 * l + 128), S("io3"), float(-l), op.is_equal, 2.0, op.mult)
+    ts(S("pm", 0, 1), S("pc", 0, 1), 15, op.bitwise_and)
+    ts(S("v15"), S("vv", 0, 144), 15, op.bitwise_and)
+    cp(S("col", 0, 1), S("pm", 0, 1))
+    ts(S("col", 1, 2), S("pm", 0, 1), 2.0, op.mult)
+    ts(S("col", 2, 3), S("pm", 0, 1), -1.0, op.mult, 143.0, op.add)
+    ts(S("U0"), S("v15"), 0.0, op.is_equal)
+    ts(S("U1"), S("v15"), 1.0, op.is_equal, EPS, op.mult)
+    ts(S("Bm"), S("io3"), S("col", 0, 1), op.add, 0.0, op.is_equal)
+    ts(S("v127"), S("vv"), 127, op.bitwise_and)
+    tt(S("U2"), S("U0"), S("U1"), op.add)
+    ts(S("Zh"), S("vv", 0, 144), S("col", 2, 3), op.is_equal)
+    cp(S("curh"), S("curs"))
+    tt(S("C01"), S("Bm"), S("U2", 0, 128), op.mult)
+    ts(S("Zb"), S("vv", 0, 144), S("col", 2, 3), op.is_equal)
+    tt(S("C23"), S("Bm"), S("U2", 14, 142), op.mult)
+    ts(S("iw"), S("iwr"), S("col", 0, 1), op.add)
+    iota(S("io2"), [[2, W]], -1, 0)
+
+    spots = [("PA", 0), ("PA", 512), ("PA", 1024), ("PC", 0)]
+    for k, (bk, o) in enumerate(spots):
+        mm([(S(bk, o + 96 * s, o + 96 * s + 96), S("R", 128 * (4 * k + s), 128 * (4 * k + s) + 128), S("curh"), True, True) for s in range(4)])
+    act(S("R0"), S("K1"), fn.Ln)
+    act(S("R0"), S("R0"), fn.Exp, scale=-1.0)
+
+    def onehot(k):
+        bk, o = spots[k]
+        ts(S("OH", 384 * k, 384 * k + 384), S(bk, o, o + 384), S("col", 1, 2), op.is_equal)
+
+    def weigh(bank, c, a, b):
+        mm([(S(bank, a, b), S(c), S("OH", a, b), True, True)])
+
+    def unpack(o):
+        ts(S("Si", o // 2, o // 2 + 96), S("PD", 0, 96), 2048.0, op.mult)
+        ts(S("J", o, o + 96), S("Si", o // 2, o // 2 + 96), 11, op.logical_shift_right)
+        ts(S("J", o + 96, o + 192), S("Si", o // 2, o // 2 + 96), 2047, op.bitwise_and)
+
+    onehot(0)
+    onehot(1)
+    weigh("PB", "C01", 0, 512)
+    onehot(2)
+    weigh("PB", "C01", 512, 1024)
+    onehot(3)
+    weigh("PB", "C01", 1024, W)
+    for a, b in C3:
+        tt(S("X", a, b), S("PB", a, b), S("cons", a, b), op.mult)
+        wrap2("PD", "Zh", "X", a, b)
+    ts(S("IIb"), S("v127"), 0.0, op.is_equal)
+    ts(S("NIb"), S("v127", 0, 128), 0.0, op.is_equal, -1.0, op.mult)
+    ts(S("IIf"), S("v127"), 0.0, op.is_equal)
+    ts(S("L1b"), S("v127", 0, 128), 0.0, op.is_equal, L1, op.mult)
+    for a, b in C3:
+        weigh("PA", "C23", a, b)
+    unpack(0)
+    cp(S("Ju"), S("J", 0, 192))
+
+    shift("PC", "IIb", "K1", V, False)
+    shift("PC", "IIb", "q0s", V, False, o=256)
+    act(S("t0"), S("PC"), fn.Copy)
+    send(0, nxt, S("t0"), S("K2", V, W + 256))
+
+    def decide(q, qc, lam, lists, dj, ju, o0, le1, fill, pre):
+        for k, (dd, ff, bank) in enumerate((("D0", "F0", "PC"), ("D1", "F1", "PD"))):
+            for a, b in C3:
+                tt(S(dd, a, b), G(q, lists, a, b, 96 * k), S(qc, a, b), op.subtract)
+                act(S(dd, a, b), S(dd, a, b), fn.Square, scale=1.0 / lam)
+                if k == 0 or a // 512 < 3 - le1:
+                    act(S(ff, a, b), S(dd, a, b), fn.Sign, bias=SQ, scale=-1.0)
+                    wrap2(bank, "Zb", ff, a, b)
+            if k == 0:
+                pre()
+        fill()
+        for a, b in C3[3 - le1:]:
+            ts(S("F1", a, b), S("D1", a, b), SQ, op.is_lt, 0.5, op.subtract)
+            wrap2("PD", "Zb", "F1", a, b)
+        p1, p2, p3 = S("PC", 96, 192), S("PC", 192, 288), S("PD", 96, 192)
+        if o0:
+            ts(S(o0), S("PC", 0, 96), 1.0, op.is_ge)
+        ts(p1, S("PC", 0, 96), 1.0, op.is_ge)
+        ts(p2, S("PC", 0, 96), 1.0, op.is_lt)
+        tt(p1, p1, S(dj, 0, 96), op.mult)
+        tt(S("s3"), p2, S(dj, 96, 192), op.mult)
+        tt(S("s4"), p1, S("iw"), op.add)
+        ts(p3, S("PD", 0, 96), 0.25, op.is_ge)
+        tt(p3, p3, S("s3"), op.mult)
+        tt(S("jf"), p3, S("s4"), op.add)
+        cp(S(ju), S("jf"))
+        cp(S("jh"), S("jf"))
+
+    def spread_pre(k):
+        for a, b in C3:
+            mm([(S("PB", a, b), S("NIb"), S(k, a, b), True, False)])
+
+    def spread():
+        for a, b in C3:
+            mm([(S("PB", a + l, b, 16), S("R", 128 * l, 128 * l + 128), S("jh", a // 16, b // 16), False, l == 15) for l in range(16)], 32)
+            act(S("Wn", a, b), S("PB", a, b), fn.Copy)
+
+    def partner_k(a, b):
+        act(S("D1", a, b), S("D1", a, b), fn.Abs)
+        act(S("KM", a, b), S("D1", a, b), fn.Relu, bias=1.0, scale=-1.0)
+
+    def pre1():
+        tt(S("dJ", 0, 96), S("J", 0, 96), S("iw"), op.subtract)
+        tt(S("dJ", 96, 192), S("J", 96, 192), S("iw"), op.subtract)
+        spread_pre("K1")
+
+    def fill1():
+        for a, b in C3:
+            tt(S("X", a, b), S("PA", a, b), S("cons", a, b), op.mult)
+            mm([(S("PA", a, b), S("NIb"), S("q0s", a, b), True, False)])
+
+    decide("q0s", "q0c", 1.0, "Ju", "dJ", "j1u", "o0k", OPT["le0"], fill1, pre1)
+    spread()
+    for a, b in CV:
+        tt(S("E1a", a, b), G("v0s", "j1u", a, b), S("v0c", a, b), op.subtract)
+    for a, b in CL:
+        act(S("QB", a, b), G("q0s", "j1u", a, b), fn.Copy)
+        mm([(S("PA", a, b), S("IIb", 0, 128), S("QB", a, b), False, True)])
+    wrap("PD", "Zh", "X")
+    for a, b in CL:
+        tt(S("D1", a, b), G("Wn", "j1u", a, b), S("io2", a, b), op.subtract)
+        act(S("PB", a, b), S("PA", a, b), fn.Sign)
+        partner_k(a, b)
+        act(S("PA", a, b), S("E1a", a, b), fn.Sign)
+    unpack(192)
+    ts(S("NIf"), S("v127", 0, 128), 0.0, op.is_equal, -1.0, op.mult)
+    ts(S("L2b"), S("v127", 0, 128), 0.0, op.is_equal, L2, op.mult)
+    ts(S("col", 3, 4), S("pc", 0, 1), 15.0, op.mult)
+    if OPT["aqpe"]:
+        ts(S("B8a", parts=8), S("io3", parts=8), S("col", 3, 4, parts=8), op.is_equal, -L1, op.mult)
+        ts(S("B8b", parts=8), S("io3", parts=8), S("col", 3, 4, parts=8), op.is_equal, -L2, op.mult)
+    else:
+        ts(S("B8", parts=8), S("io3", parts=8), S("col", 3, 4, parts=8), op.is_equal)
+    if OPT["v0pe"]:
+        ts(S("N256"), S("v127", 0, 128), 0.0, op.is_equal, -L2 / 16, op.mult)
+
+    def lists2():
+        wrap("PD", "Zb", "KM")
+        tt(S("s5"), S("J", 96, 288), S("J", 192, 384), op.subtract)
+        ts(S("PD", 0, 96), S("PD", 0, 96), 0.0, op.is_gt)
+        tt(S("PD", 0, 96), S("PD", 0, 96), S("o0k"), op.mult)
+        tt(S("PD", 96, 192), S("PD", 0, 96), S("s5", 0, 96), op.mult)
+        tt(S("PD", 192, 288), S("PD", 0, 96), S("s5", 96, 192), op.mult)
+        tt(S("PD", 96, 288), S("PD", 96, 288), S("J", 192, 384), op.add)
+        cp(S("J2u"), S("PD", 96, 288))
+        tt(S("dJ2", 0, 96), S("PD", 96, 192), S("iw"), op.subtract)
+        tt(S("dJ2", 96, 192), S("PD", 192, 288), S("iw"), op.subtract)
+
+    def aims():
+        for a, b in C3:
+            mm([(S("PD"), S("B8", parts=8), S("aims", a, b, parts=8), True, True)])
+            act(S("AM1", a, b), S("PD"), fn.Copy, scale=L1)
+
+    def newton(two):
+        for k, (a, b) in enumerate(C3):
+            act(S(two[k % 2]), S("S1", a, b), fn.Copy)
+            tt(S("R0", a, b), S(two[k % 2]), S("R0", a, b), op.mult)
+
+    def shot(x):
+        lam, lb, v0, v0c, base = ((L1, "L1b", "v0s", "v0c", "V0b"), (L2, "L2b", "V0p", "CQ", "V0q"))[x]
+        v1, a2, am, y2, e1, vout = (("V1a", "A2a", "AM1", "Y2a", "E1a", "V0p"), ("V1b", "A2b", "AM2", "Y2b", "E1b", "Wn"))[x]
+        dl = 0.1875 * 16 * lam
+
+        def one(a, b):
+            tt(S("PB", a, b), S("KM", a, b), S("PB", a, b), op.mult)
+
+        def two(a, b):
+            tt(S("KS", a, b), S("PB", a, b), S("K1", a, b), op.mult)
+
+        def ee(a, b):
+            tt(S(e1, a, b), G(v0, "j1u", a, b), S(v0c, a, b), op.subtract)
+            act(S("PA", a, b), S(e1, a, b), fn.Sign)
+
+        def hh(a, b):
+            tt(S("PA", a, b), S("PA", a, b), S("KS", a, b), op.mult)
+            act(S("PA", a, b), S("PA", a, b), fn.Relu, scale=-1.0)
+
+        def tv(a, b):
+            tt(S("PB", a, b), S("PA", a, b), S(e1, a, b), op.mult)
+
+        def vnew(a, b):
+            if a < V and OPT["q1pe"] & (1 << x):
+                tt(S(v1, a, b), S("PB", a, b), S(v0, a, b), op.add)
+                mm([(S("PB", a, b), S("IIf", 0, 128), S(v1, a, b), True, False), (S("PB", a, b), S(lb), S("q0s", a, b), False, True)])
+                return
+            out = S("V1v") if a == V else S(v1, a, b)
+            tt(out, S("PB", a, b), S(v0, a, b), op.add)
+            if a == V:
+                shift("PC", "IIf", "V1v", 0, False)
+                act(S(("t1", "t3")[x]), S("PC", 0, 256), fn.Copy)
+                send(1 + 2 * x, nxt, S(("t1", "t3")[x]), S(v1, V, W))
+                mm([(S("PC", 256, 512), S(lb), S("K2", W, W + 256), True, True)])
+            else:
+                mm([(S("PB", a, b), S(lb), S("q0s", a, b), True, True)])
+
+        def qnew(a, b):
+            if a < V and OPT["q1pe"] & (1 << x):
+                act(S("q1", a, b), S("PB", a, b), fn.Copy)
+                if OPT["cqdma"]:
+                    dma("sp", S("CQ", a, b), S("q1", a, b))
+                else:
+                    act(S("CQ", a, b), S("PB", a, b), fn.Copy)
+                return
+            tt(S("q1", a, b), S("PC", 256, 512) if a == V else S("PB", a, b), S(v1, a, b), op.add)
+            act(S("CQ", a, b), S("q1", a, b), fn.Copy)
+
+        if x == 0:
+            one(*C3[2]); two(*C3[2]); one(*c0); hh(*cv); two(*c0); one(*c1); tv(*cv); hh(*c0); vnew(*cv)
+            two(*c1); hh(*c2); hh(*c1)
+            lists2()
+            if not OPT["aqpe"]:
+                aims()
+        else:
+            ee(*cv); ee(*c0); hh(*cv); ee(*c1); tv(*cv); hh(*c0); vnew(*cv); ee(*c2); hh(*c1); hh(*c2)
+        stagger([tv, vnew], [c0, c1, c2], 0.5)
+        for a, b in C3:
+            act(S("KH1", a, b), S("PA", a, b), fn.Copy)
+        dma("sp", S("CP", 0, V), S(v1, 0, V))
+        for c in (c0, c1, c2):
+            qnew(*c)
+        for a, b in (c0, c1):
+            mm([(S("PA", a, b), S("NIf"), S("q1", a, b), True, False)])
+        if x == 0:
+            for a, b in C3:
+                mm([(S("PB", a, b), S("IIb", 0, 128), S("K1", a, b), True, True)])
+        elif OPT["rk"]:
+            newton(("PD", "PD"))
+        qnew(*cv)
+        dma("sp", S("CP", V, W), S(v1, V, W))
+        mm([(S("PA", *C3[2]), S("NIf"), S("q1", *C3[2]), True, False)])
+
+        def fill2():
+            for a, b in C3:
+                if x == 0:
+                    tt(S("S1", a, b), S("PB", a, b), S("R0", a, b), op.mult)
+            spread_pre("K2")
+
+        decide("q1", "CQ", lam, "J2u", "dJ2", "j2u", None, OPT[("lea", "leb")[x]], fill2, lambda: None)
+        spread()
+        for a, b in CL:
+            tt(S("E2", a, b), G(v1, "j2u", a, b), S("CP", a, b), op.subtract)
+        for a, b in CL:
+            act(S("D0", a, b), G("q1", "j2u", a, b), fn.Copy)
+            mm([(S("PA", a, b), S("IIf", 0, 128), S("D0", a, b), False, True)])
+        for a, b in CL:
+            tt(S("D1", a, b), G("Wn", "j2u", a, b), S("io2", a, b), op.subtract)
+        for a, b in CL:
+            tt(S("PA", a, b), S("PA", a, b), S("E2", a, b), op.mult)
+            act(S("F0", a, b), S("PA", a, b), fn.Sign)
+            if OPT["fold"]:
+                act(S("D1", a, b), S("D1", a, b), fn.Abs)
+                mm([(S("PA", a, b), S("IIf", 0, 128), S("D1", a, b), True, False), (S("PA", a, b), S("IIb", 0, 128), S("F0", a, b), False, True)])
+                act(S("PA", a, b), S("PA", a, b), fn.Relu, scale=-1.0)
+                continue
+            partner_k(a, b)
+            mm([(S("PA", a, b), S("NIb"), S("F0", a, b), True, False), (S("PA", a, b), S("IIb", 0, 128), S("KM", a, b), False, True)])
+            act(S("PA", a, b), S("PA", a, b), fn.Relu, bias=-1.0)
+        if x == 0:
+            act3("S1", "S1", fn.Identity, bias=-2.0 / L2 ** 2, scale=1.0 / L2 ** 2)
+            if not OPT["v0pe"]:
+                act3("V0b", "v0s", fn.Copy, scale=L2 / 16)
+        else:
+            act3("V0q", "V0p", fn.Copy, scale=256.0)
+
+        def aq(a, b):
+            if OPT["aqpe"]:
+                mm([(S("PA", a, b), S("IIf", 0, 128), S("DA", a, b), True, False),
+                    (S("PA", a, b), S(("B8a", "B8b")[x], parts=8), S("aims", a, b, parts=8), False, True)])
+                act(S("A", a, b), S("PA", a, b), fn.Copy)
+                act(S("CQ", a, b), S("PA", a, b), fn.Copy)
+                return
+            tt(S("A", a, b), S("PA", a, b), S(am, a, b), op.subtract)
+            act(S("CQ", a, b), S("A", a, b), fn.Copy)
+
+        stagger([lambda a, b: tt(S("PB", a, b), S("PA", a, b), S("K2", a, b), op.mult),
+                 lambda a, b: tt(S("PA", a, b), S("PB", a, b), S("E2", a, b), op.mult),
+                 lambda a, b: tt(S("PA", a, b), S("PA", a, b), S(v1, a, b), op.add),
+                 lambda a, b: tt(S("DA" if OPT["aqpe"] else "PA", a, b), S("PA", a, b), S("q1", a, b), op.add),
+                 aq], CV if OPT["c4"] & 2 else CL, OPT["st2"])
+
+        def da2(a, b):
+            tt(S("DA", a, b), G("A", "j2u", a, b), S("CQ", a, b), op.subtract)
+
+        def b1(a, b):
+            tt(S("PB", a, b), S("PB", a, b), S("DA", a, b), op.mult)
+
+        def b2(a, b):
+            tt(S("PA", a, b), S("PB", a, b), S("A", a, b), op.add)
+
+        def b3(a, b):
+            tt(S("A2v") if a == V else S(a2, a, b), S("PA", a, b), S("A", a, b), op.add)
+            if a == V:
+                shift("PC", "IIf", "A2v", 0, True)
+                act(S(("t2", "t4")[x]), S("PC", 0, 256), fn.Copy)
+                send(2 + 2 * x, prv, S(("t2", "t4")[x]), S(a2, V, W))
+            else:
+                dma("sp", S("CP", a, b), S(a2, a, b))
+                act(S("PA", a, W if b == V else b), S("KH1", a, W if b == V else b), fn.Copy)
+
+        def zz(a, b):
+            tt(S("Yv") if (a == V and x == 1) else S(y2, a, b), S("PB", a, b), S("E2", a, b), op.mult)
+
+        da2(*cv); da2(*c0); b1(*cv); da2(*c1); b2(*cv); b1(*c0); b3(*cv); da2(*c2)
+        if x == 1:
+            zz(*cv)
+            mm([(S("PD", 0, 128), S("IIf", 16, 144), S("Y2a", V, H), True, False),
+                (S("PD", 0, 128), S("IIf", 16, 144), S("Yv", 0, 128), False, True),
+                (S("PD", 128, 256), S("IIf", 64, 192), S("Y2a", H, W), True, False),
+                (S("PD", 128, 256), S("IIf", 64, 192), S("Yv", 128, 256), False, True)])
+            act(S("t5"), S("PD", 0, 256), fn.Copy)
+            send(5, prv, S("t5"), S("Y2b", V, W))
+        else:
+            if not OPT["aqpe"]:
+                act3("AM2", "AM1", fn.Copy, scale=L2 / L1)
+            act3("ZZ", "K1", fn.Square, scale=L2)
+        b1(*c1); b2(*c0); b1(*c2); b2(*c1); b3(*c0); b2(*c2); b3(*c1); b3(*c2)
+        for c in ((c0, c1, C3[2]) if x == 0 else (c0, c1, c2)):
+            zz(*c)
+        if x == 0 and not OPT["rk"]:
+            newton(("PD", "PC"))
+        act(S("CP", V, W), S(a2, V, W), fn.Copy)
+
+        sums = [S("PC"), S("PD"), S("PA", 1024, W)]
+        if x == 0:
+            act3("ZZ", "ZZ", fn.Copy, scale=-1.0)
+            act3("Y2a", "Y2a", fn.Copy, scale=(L2 / L1) ** 2)
+            dma("pool", S("ZZ", 0, V), S("Y2a", 0, V), True)
+        else:
+            for (a, b), bank in list(zip(C3, sums))[:2]:
+                mm([(bank, S("IIf", 0, 128), S("ZZ", a, b), True, False)])
+                mm([(bank, S("IIf", 0, 128), S("Y2b", a, b), False, False)])
+        for a, b in C3:
+            tt(S("DA", a, b), G(a2, "j1u", a, b), S("CP", a, b), op.subtract)
+        for a, b in C3:
+            tt(S("PA", a, b), S("PA", a, b), S("DA", a, b), op.mult)
+        if x == 1:
+            for (a, b), bank in zip(C3, sums):
+                tt(S("D1", a, b), S("PA", a, b), S("E1b", a, b), op.mult)
+                if a < 1024:
+                    mm([(bank, S("IIf", 0, 128), S("D1", a, b), False, True)])
+
+        def f1(a, b):
+            tt(S("PB", a, b), S("PA", a, b), S(a2, a, b), op.add)
+            if x == 0:
+                tt(S("D1", a, b), S("PA", a, b), S("E1a", a, b), op.mult)
+                act(S("D1", a, b), S("D1", a, b), fn.Copy, scale=(L2 / L1) ** 2)
+            elif a == 1024:
+                mm([(sums[2], S("IIf", 0, 128), S(z, a, b), z == "ZZ", z == "D1") for z in ("ZZ", "Y2b", "D1")])
+
+        def f3(a, b):
+            if x == 0 and OPT["v0pe"]:
+                mm([(S("PB", a, b), S("IIf", 0, 128), S("D0", a, b), True, False), (S("PB", a, b), S("N256"), S("v0s", a, b), False, True)])
+                act(S(vout, a, b), S("PB", a, b), fn.Copy, scale=-1.0)
+                act(S("CQ", a, b), S("PB", a, b), fn.Copy, scale=-1.0)
+                return
+            tt(S(vout, a, b), S(base, a, b), S("PB", a, b), op.subtract)
+            if x == 0:
+                act(S("CQ", a, b), S(vout, a, b), fn.Copy)
+            else:
+                act(S(vout, a, b), S(vout, a, b), fn.Copy, scale=1.0 / (16 * L2))
+                dma("sp", D("yv", a, b), S(vout, a, b))
+
+        stagger([f1, lambda a, b: ts(S("D0" if x == 0 and OPT["v0pe"] else "PB", a, b), S("PB", a, b), dl, op.min, -dl, op.max), f3],
+                CV if x == 0 and OPT["c4"] & 1 else CL, OPT["st1"])
+        if x == 0:
+            dma("pool", S("ZZ"), S("D1"), True)
+        else:
+            for (a, b), bank in zip(C3, sums):
+                tt(S("D0", a, b), bank, S("R0", a, b), op.mult)
+                dma("act", D("yg", a, b), S("D0", a, b))
+
+    shot(0)
+    shot(1)
+    issue()
+
+    g.wait_ge(T.sem.sent, count["sent"])
+    for q in ("pe", "dve", "act", "pool"):
+        g.wait_ge(T.sem[q], count[q])
+    for s in dmas:
+        g.wait_ge(T.sem[s], 16)

@@ -2,44 +2,50 @@ from concourse.mybir import AluOpType, ActivationFunctionType
 
 W, V = 1536, 1280
 H = V + 128
-L1, L2 = 16.0, 4096.0
-EPS = 2.0 ** -11
-SQ = 0.5625 + 2.0 ** -24
+L = 16.0
+BIG = 16 * L
+EPS = 2.0 ** -12
+WHOLE = 1.5 * 2.0 ** 23
+TWO = 2.0 ** 24
+SIXTEEN = 1.5 * 2.0 ** 27
+NEAR = 0x150aaaa / 2.0 ** 24
+
+OPT = {"r0": "aaaaaa", "fast": 1, "q1pe": 0, "ra1": 15, "ra2": 7, "fa1": 3, "fa2": 7, "h1": 0, "dq1": "d", "p5": "dmm", "v1pe": 0, "p4": "fad",
+       "cqdma": 3, "ga2": 0, "ta2": 7, "nw": 1, "yvacc": 0, "c6": 1, "turns": 12, "span": 60, "moves": 2000, "warm": 1500, "free": 0.3, "soon": 1.0, "hint": 1.0, "seed": 12345, "ks": "3333", "look": 60, "heat": 300, "tries": 0}
+CASES = [(1.56, 0.45, 150, 4000), (1.9, 0.42, 200, 5000), (1.3, 0.6, 120, 3500)]
+KEPT = {}
 
 F, B, HF, I, U = "float32", "bfloat16", "float16", "int32", "uint16"
+SAME = {"DA": "DD", "DQ2": "QB", "FH": "F0", "HB": "F1", "RK2": "AB0", "DK2": "AB1"}
 SCRATCH = {}
-for _n in ("V1a", "V1b", "CP", "q1", "CQ", "D0", "D1", "E1a", "E1b", "E2", "Wn", "io2", "A", "A2a", "A2b", "DA", "KS", "KH1",
-           "S1", "Y2a", "Y2b", "V0p", "V0q", "ZZ", "R0"):
+for _n in ("V1a", "V1b", "q1", "CQ", "Wn", "io2", "A", "A2a", "A2b", "VG", "KH1", "E2", "DL1",
+           "Y2a", "Y2b", "V0p", "ZZ", "R0", "RR", "Y1", "CP", "KS", "SQ"):
     SCRATCH[_n] = ("sbuf", [128, W], F)
-for _n in ("q0s", "q0c", "v0s", "K1", "v0c", "V0b", "OH", "F0", "F1", "QB", "KM", "AM1", "AM2"):
+for _n in ("q0s", "q0c", "v0s", "K1", "OH", "F0", "F1", "QB", "AM", "AB0", "AB1", "DK1", "RK1", "DQ1"):
     SCRATCH[_n] = ("sbuf", [128, W], B)
 SCRATCH.update({
+    "DD": ("sbuf", [128, 2 * W], F),
     "cons": ("sbuf", [128, W], I), "X": ("sbuf", [128, W], HF), "K2": ("sbuf", [128, W + 256], B),
     "aims": ("sbuf", [128, W], B), "curs": ("sbuf", [128, 96], I), "curh": ("sbuf", [128, 96], HF),
     "R": ("sbuf", [128, 2048], HF), "io3": ("sbuf", [128, 128], B), "vv": ("sbuf", [128, 256], I),
-    "v15": ("sbuf", [128, 144], I), "v127": ("sbuf", [128, 256], I), "pc": ("sbuf", [128, 4], I), "pm": ("sbuf", [128, 4], I),
+    "v15": ("sbuf", [128, 144], I), "pc": ("sbuf", [128, 4], I), "pm": ("sbuf", [128, 4], I),
     "col": ("sbuf", [128, 16], F), "Bm": ("sbuf", [128, 128], B), "U0": ("sbuf", [128, 144], B), "U1": ("sbuf", [128, 144], B),
     "U2": ("sbuf", [128, 144], B), "C01": ("sbuf", [128, 128], B), "C23": ("sbuf", [128, 128], B),
     "Zb": ("sbuf", [128, 144], B), "Zh": ("sbuf", [128, 144], HF), "IIf": ("sbuf", [128, 256], F), "IIb": ("sbuf", [128, 256], B),
-    "NIb": ("sbuf", [128, 128], B), "NIf": ("sbuf", [128, 128], F), "L1b": ("sbuf", [128, 128], B), "L2b": ("sbuf", [128, 128], B),
-    "B8": ("sbuf", [128, 128], B), "B8a": ("sbuf", [128, 128], B), "B8b": ("sbuf", [128, 128], B), "N256": ("sbuf", [128, 128], B),
-    "iwr": ("sbuf", [128, 96], F), "iw": ("sbuf", [128, 96], F),
-    "Si": ("sbuf", [128, 192], I), "J": ("sbuf", [128, 384], I), "J2": ("sbuf", [128, 192], F),
+    "NIb": ("sbuf", [128, 128], B), "NIf": ("sbuf", [128, 256], F), "Lb": ("sbuf", [128, 128], B), "Zero": ("sbuf", [128, 128], B),
+    "Is": ("sbuf", [128, 128], F), "B8s": ("sbuf", [128, 128], B),
+    "B8": ("sbuf", [128, 128], B), "B4": ("sbuf", [128, 128], B), "N8": ("sbuf", [128, 128], B),
+    "iwr": ("sbuf", [128, 96], F), "iw": ("sbuf", [128, 96], F), "J": ("sbuf", [128, 384], F),
     "Ju": ("sbuf", [128, 192], U), "J2u": ("sbuf", [128, 192], U), "dJ": ("sbuf", [128, 192], F), "dJ2": ("sbuf", [128, 192], F),
-    "o0": ("sbuf", [128, 96], F), "o0k": ("sbuf", [128, 96], F), "s1": ("sbuf", [128, 96], F), "s2": ("sbuf", [128, 96], F), "s3": ("sbuf", [128, 96], F),
-    "s4": ("sbuf", [128, 96], F), "s5": ("sbuf", [128, 192], F), "s6": ("sbuf", [128, 192], F), "jf": ("sbuf", [128, 96], F),
+    "o0k": ("sbuf", [128, 96], F), "s3": ("sbuf", [128, 96], F), "selu": ("sbuf", [128, 96], U),
+    "s4": ("sbuf", [128, 96], F), "s5": ("sbuf", [128, 192], F), "jf": ("sbuf", [128, 96], F),
     "jh": ("sbuf", [128, 96], HF), "j1u": ("sbuf", [128, 96], U), "j2u": ("sbuf", [128, 96], U),
-    "V1v": ("sbuf", [128, 256], F), "A2v": ("sbuf", [128, 256], F), "Yv": ("sbuf", [128, 256], F),
+    "tv": ("sbuf", [128, 256], F), "YL": ("sbuf", [128, 256], F),
     "t0": ("sbuf", [128, 512], B), "t1": ("sbuf", [128, 256], F), "t2": ("sbuf", [128, 256], F),
     "t3": ("sbuf", [128, 256], F), "t4": ("sbuf", [128, 256], F), "t5": ("sbuf", [128, 256], F),
     "PA": ("psum", [128, W], F), "PB": ("psum", [128, W], F), "PC": ("psum", [128, 512], F), "PD": ("psum", [128, 512], F),
 })
 SEMAPHORES = ["pe", "dve", "act", "pool", "sent"] + ["d%d" % _i for _i in range(40)] + ["r%d" % _i for _i in range(6)]
-
-OPT = {"lea": 1, "leb": 2, "le0": 1, "st2": 2.5, "st1": 1.5, "look": 60, "heat": 300, "tries": 5000, "fold": 0,
-       "q1pe": 0, "cqdma": 0, "rk": 1, "c4": 0, "aqpe": 0, "v0pe": 0}
-CASES = [(1.56, 0.45, 150, 4000), (1.9, 0.42, 200, 5000), (1.3, 0.7, 120, 3500)]
-KEPT = {}
 
 
 def rank_program(g, core, T, topo):
@@ -57,12 +63,14 @@ def rank_program(g, core, T, topo):
     opened = {}
 
     def S(name, a=0, b=None, step=1, parts=128):
+        name = SAME.get(name, name)
         b = T[name].shape[1] if b is None else b
         ap = T[name][0:parts, a:b:step] if step > 1 else T[name][0:parts, a:b]
         return (name, a, b, ap)
 
     def G(win, off, a, b, o=0):
-        return (win, 0, W, T[win][:, 0:W].indirect(T[off][:, o + a // 16:o + b // 16]), (off, o + a // 16, o + b // 16, None))
+        w = T[win].shape[1]
+        return (win, 0, w, T[win][:, 0:w].indirect(T[off][:, o + a // 16:o + b // 16]), (off, o + a // 16, o + b // 16, None))
 
     def deps(q, reads, writes):
         need = {}
@@ -91,6 +99,17 @@ def rank_program(g, core, T, topo):
                 hist.setdefault(x[0], []).append((x[1], x[2], q, tok, wr))
 
     calls = []
+
+    gates, hints = [], []
+
+    def urgent(up, f, *args):
+        a = len(calls)
+        f(*args)
+        hints.append((a, len(calls), up * OPT["hint"]))
+
+    def behind(j, f, *args):
+        gates.append((len(calls), j))
+        f(*args)
 
     def run(q, make, reads, writes, cost):
         reads = list(reads) + [x[4] for x in reads if len(x) > 4]
@@ -130,13 +149,13 @@ def rank_program(g, core, T, topo):
 
     def act(out, a, f, bias=0.0, scale=1.0):
         run("act", lambda: g.scalar.activation(out[3], a[3], f, bias=bias, scale=scale), [a], [out],
-            price(out, a, 1, 1400 if f in (fn.Ln, fn.Exp) else 0))
+            price(out, a, 1, 1400 if f in (fn.Ln, fn.Exp) and out[1] == 0 else 0))
 
     def act3(out, a, f, bias=0.0, scale=1.0):
         for k in range(0, W, 512):
             act(S(out, k, k + 512), S(a, k, k + 512), f, bias, scale)
 
-    def mm(items, wide=None):
+    def mm(items, wide=None, more=()):
         items = [list(it) for it in items]
         for it in items:
             key = (it[0][0], it[0][1] // 512)
@@ -149,7 +168,7 @@ def rank_program(g, core, T, topo):
                 ins = g.tensor.matmul(o[3], l[3], r[3], s0, s1)
             return ins
         cost = (0, 0, sum(max(64, wide or it[0][2] - it[0][1]) * (4 if size(it[2]) == 4 else 1) for it in items))
-        run("pe", make, [x for it in items for x in it[1:3]], [it[0] for it in items], cost)
+        run("pe", make, [x for it in items for x in it[1:3]], [it[0] for it in items] + list(more), cost)
 
     def iota(out, pat, base, cm, small=True):
         cost = (130 + 1.66 * (out[2] - out[1]), 0, 0)
@@ -206,6 +225,8 @@ def rank_program(g, core, T, topo):
             for xs, wr in ((reads, False), (writes, True)):
                 for x in xs:
                     log.setdefault(x[0], []).append((x[1], x[2], i, wr))
+        for i, j in gates:
+            pred[i].add(j)
         succ = [[] for _ in range(m)]
         for i in range(m):
             for j in pred[i]:
@@ -265,7 +286,10 @@ def rank_program(g, core, T, topo):
             rest = [0.0] * m
             for i in range(m - 1, -1, -1):
                 rest[i] = cases[0][0][i] + cases[0][1][i] + max([rest[j] for j in succ[i]] + [0.0])
-            seed = [12345]
+            for a, b, up in hints:
+                for i in range(a, b):
+                    rest[i] += up
+            seed = [OPT["seed"]]
 
             def rnd():
                 seed[0] = (seed[0] * 1103515245 + 12345) % 2 ** 31
@@ -293,6 +317,123 @@ def rank_program(g, core, T, topo):
                     best, order, rest = s, o, r
                     if s < top[0]:
                         top = (s, o)
+            qn = [list(Q).index(q) for q in qs]
+            names = sorted(set(b for x in bk for b in x))
+            bn = [[names.index(b) for b in x] for x in bk]
+            soft = [[j for j in pred[i] if qs[i] == "pe" and qs[j] == "pe"] for i in range(m)]
+            hard = [[j for j in pred[i] if j not in soft[i]] for i in range(m)]
+
+            qn.append(-1)
+
+            def frame(case, o, a, b):
+                cost, late = case
+                state = [0.0] * (m + 1), [0.0] * (m + 1), [m] * (m + 1), [m] * len(Q), [m] * len(names)
+                lay(case, o[:a], state)
+                tail, nextq, nextb = [0.0] * (m + 1), [m] * len(Q), [m] * len(names)
+                for i in reversed(o[b:]):
+                    t = max([late[i], tail[nextq[qn[i]]]] + [tail[j] + (0 if i in soft[j] else late[i]) for j in succ[i]]
+                            + [tail[nextb[z]] + late[i] for z in bn[i] if qn[nextb[z]] != qn[i]])
+                    tail[i] = t + cost[i]
+                    nextq[qn[i]] = i
+                    for z in bn[i]:
+                        nextb[z] = i
+                after = [max([late[i]] + [tail[j] + (0 if i in soft[j] else late[i]) for j in succ[i]]) for i in range(m)]
+                least = max([0.0] + [state[0][i] + after[i] for i in o[:a]])
+                return state, after, tail, nextq, nextb, least
+
+            def weigh(case, part, fr):
+                state, after, tail, nextq, nextb, end = fr
+                fin, done, why, lastq, lastb = state[0], state[1], state[2], list(state[3]), list(state[4])
+                lay(case, part, (fin, done, why, lastq, lastb))
+                last, total = m, 0.0
+                for i in part:
+                    total += fin[i]
+                    if fin[i] + after[i] > end:
+                        end, last = fin[i] + after[i], i
+                for i, j in zip(lastq, nextq):
+                    if fin[i] + tail[j] > end:
+                        end, last = fin[i] + tail[j], i
+                for i, j in zip(lastb, nextb):
+                    if qn[i] != qn[j] and done[i] + tail[j] > end:
+                        end, last = done[i] + tail[j], i
+                pairs, inside = [], set(part)
+                while last in inside:
+                    if why[last] in inside and why[last] not in pred[last]:
+                        pairs.append((last, why[last]))
+                    last = why[last]
+                return end + OPT["soon"] * total / m, pairs, end
+
+            def lay(case, o, state):
+                cost, late = case
+                fin, done, why, lastq, lastb = state
+                for i in o:
+                    q = qn[i]
+                    w = lastq[q]
+                    t = fin[w]
+                    for j in hard[i]:
+                        if done[j] > t:
+                            t, w = done[j], j
+                    for j in soft[i]:
+                        if fin[j] > t:
+                            t, w = fin[j], j
+                    for b in bn[i]:
+                        j = lastb[b]
+                        if done[j] > t and qn[j] != q:
+                            t, w = done[j], j
+                        lastb[b] = i
+                    why[i] = w
+                    lastq[q] = i
+                    fin[i] = t = t + cost[i]
+                    done[i] = t + late[i]
+
+            def moved(o, i, j):
+                a, b = o.index(j), o.index(i)
+                part, link = o[a:b + 1], pred
+                back = rnd() < 0.5
+                if back:
+                    part, link, i, j = part[::-1], succ, j, i
+                take = {i}
+                for z in reversed(part):
+                    if z in take:
+                        take.update(link[z])
+                if j in take:
+                    return None
+                part = [z for z in part if z in take] + [z for z in part if z not in take]
+                return o[:a] + (part[::-1] if back else part) + o[b + 1:]
+
+            def by_time(case, o):
+                state = [0.0] * (m + 1), [0.0] * (m + 1), [m] * (m + 1), [m] * len(Q), [m] * len(names)
+                lay(case, o, state)
+                return sorted(o, key=lambda i: state[0][i] - case[0][i])
+
+            order, span = top[1], OPT["span"]
+            for turn in range(OPT["turns"]):
+                for a in range(-int(rnd() * span / 2), m - 10, span // 2):
+                    order = by_time(cases[0], order)
+                    a, b = max(a, 0), min(a + span, m)
+                    frames = [frame(c, order, a, b) for c in cases]
+                    part = order[a:b]
+                    laid = [weigh(c, part, f) for c, f in zip(cases, frames)]
+                    best = sum(z[0] for z in laid)
+                    keep = (best, part, laid)
+                    for it in range(OPT["moves"]):
+                        pairs = laid[int(rnd() * len(cases))][1]
+                        if rnd() < OPT["free"] or not pairs:
+                            k = int(rnd() * (b - a - 1))
+                            near = [z for z in part[k:k + 40] if qs[z] == qs[part[k]]][:2 + int(rnd() * 5)]
+                            i, j = near[-1], near[0]
+                        else:
+                            i, j = pairs[int(rnd() * len(pairs))]
+                        o = moved(part, i, j) if i != j else None
+                        if o:
+                            new = [weigh(c, o, f) for c, f in zip(cases, frames)]
+                            s = sum(z[0] for z in new)
+                            if s <= best + OPT["warm"] * (1 - it / OPT["moves"]) ** 2 * rnd() ** 2:
+                                best, part, laid = s, o, new
+                                if s < keep[0]:
+                                    keep = (s, o, new)
+                    order = order[:a] + keep[1] + order[b:]
+                top = (sum(z[2] for z in keep[2]), order)
             KEPT["order"], KEPT["best"] = top[1], top[0] / len(cases)
         for i in list(range(loads)) + [i for i in KEPT["order"] if i >= loads]:
             calls[i][1]()
@@ -300,33 +441,35 @@ def rank_program(g, core, T, topo):
     C3 = [(0, 512), (512, 1024), (1024, W)]
     CL = [C3[2], C3[0], C3[1]]
     CV = [(V, W), (0, 512), (512, 1024), (1024, V)]
-    cv, c0, c1, c2 = CV
+    CN = [(1024, V), (0, 512), (512, 1024), (V, W)]
 
-    def wrap(bank, z, src, chunks=((0, W),)):
+    def wrap(bank, z, src, chunks=((0, W),), o=0):
         for a, b in chunks:
-            mm([(S(bank, a // 16, b // 16), S(z, 15 - l, 143 - l), S(src, a + l, b, 16), l == 0, l == 15) for l in range(16)])
+            mm([(S(bank, o + a // 16, o + b // 16), S(z, 15 - l, 143 - l), S(src, a + l, b, 16), l == 0, l == 15) for l in range(16)])
 
     def wrap2(bank, z, src, a, b):
         if b >= 1024:
             wrap(bank, z, src, [(0, 1024) if b == 1024 else (a, b)])
 
-    def shift(bank, ii, src, a, back, o=0):
+    def shift(bank, ii, src, a, back, o=0, start=True):
         k = 16 if back else 112
-        mm([(S(bank, o, o + 128), S(ii, k, k + 128), S(src, a, a + 128), True, True),
-            (S(bank, o + 128, o + 256), S(ii, 64, 192), S(src, a + 128, a + 256), True, True)])
+        mm([(S(bank, o, o + 128), S(ii, k, k + 128), S(src, a, a + 128), start, True),
+            (S(bank, o + 128, o + 256), S(ii, 64, 192), S(src, a + 128, a + 256), start, True)])
 
-    def stagger(steps, chunks, lag):
-        for _, c, k in sorted((k + lag * c, c, k) for c in range(len(chunks)) for k in range(len(steps))):
-            steps[k](*chunks[c])
+    def clear(bank):
+        mm([(S(bank), S("Zero"), S("OH", 0, 512), True, True)])
+
+    def put(out, w, src, start=True, whole=False):
+        mm([(out, S(w, 0, 128), src, start, True)], more=[S(out[0], out[2], out[1] // 512 * 512 + 512)] if whole else [])
 
     dma("sp", S("curs"), ("cur", 0, W, T.cur[:]))
     for a, b in C3:
         dma("sp", S("cons", a, b), D("con", a, b))
     dma("sp", S("q0s"), D("q0"))
-    dma("sp", S("q0c"), D("q0"))
     dma("sp", S("K1"), D("kap"))
     dma("sp", S("v0s"), D("v0"))
-    dma("sp", S("v0c"), D("v0"))
+    if OPT["dq1"] == "d":
+        dma("sp", S("q0c"), D("q0"))
     dma("sp", S("K2", 0, V), D("kap", 0, V))
     dma("sp", S("aims", parts=8), ("aim", 0, W, T.aim[:]))
     loads = len(calls)
@@ -335,7 +478,7 @@ def rank_program(g, core, T, topo):
 
     iota(S("io3"), [[16, 8], [0, 16]], 0, -1)
     iota(S("pc", 0, 1), [[0, 1]], 0, 1, False)
-    iota(S("vv"), [[1, 256]], 128, -1, False)
+    iota(S("vv", 0, 144), [[1, 144]], 128, -1, False)
     iota(S("iwr"), [[16, 96]], 0, 0)
     for l in range(16):
         ts(S("R", 128 * l, 128 * l + 128), S("io3"), float(-l), op.is_equal, 2.0, op.mult)
@@ -347,7 +490,6 @@ def rank_program(g, core, T, topo):
     ts(S("U0"), S("v15"), 0.0, op.is_equal)
     ts(S("U1"), S("v15"), 1.0, op.is_equal, EPS, op.mult)
     ts(S("Bm"), S("io3"), S("col", 0, 1), op.add, 0.0, op.is_equal)
-    ts(S("v127"), S("vv"), 127, op.bitwise_and)
     tt(S("U2"), S("U0"), S("U1"), op.add)
     ts(S("Zh"), S("vv", 0, 144), S("col", 2, 3), op.is_equal)
     cp(S("curh"), S("curs"))
@@ -355,363 +497,396 @@ def rank_program(g, core, T, topo):
     ts(S("Zb"), S("vv", 0, 144), S("col", 2, 3), op.is_equal)
     tt(S("C23"), S("Bm"), S("U2", 14, 142), op.mult)
     ts(S("iw"), S("iwr"), S("col", 0, 1), op.add)
-    iota(S("io2"), [[2, W]], -1, 0)
+    iota(S("IIb"), [[0, 2], [1, 128]], 0, -1)
+    iota(S("io2"), [[2, W]], 0, 0)
+    act(S("IIb"), S("IIb"), fn.Abs)
+    act(S("IIb"), S("IIb"), fn.Relu, bias=1.0, scale=-1.0)
+    act(S("IIf"), S("IIb"), fn.Copy)
+    act(S("NIf"), S("IIb"), fn.Copy, scale=-1.0)
+    for name, w in (("NIb", -1.0), ("Lb", L), ("Zero", 0.0), ("N8", -8.0), ("Is", 1.0 / BIG)):
+        act(S(name), S("IIb", 0, 128), fn.Copy, scale=w)
+    act(S("B4"), S("Bm"), fn.Copy, scale=0.25)
+    ts(S("col", 3, 4), S("pc", 0, 1), 15.0, op.mult)
+    ts(S("B8", parts=8), S("io3", parts=8), S("col", 3, 4, parts=8), op.is_equal, -L, op.mult)
+    act(S("B8s", parts=8), S("B8", parts=8), fn.Copy, scale=1.0 / BIG)
 
     spots = [("PA", 0), ("PA", 512), ("PA", 1024), ("PC", 0)]
     for k, (bk, o) in enumerate(spots):
         mm([(S(bk, o + 96 * s, o + 96 * s + 96), S("R", 128 * (4 * k + s), 128 * (4 * k + s) + 128), S("curh"), True, True) for s in range(4)])
-    act(S("R0"), S("K1"), fn.Ln)
-    act(S("R0"), S("R0"), fn.Exp, scale=-1.0)
-
-    def onehot(k):
-        bk, o = spots[k]
         ts(S("OH", 384 * k, 384 * k + 384), S(bk, o, o + 384), S("col", 1, 2), op.is_equal)
 
-    def weigh(bank, c, a, b):
-        mm([(S(bank, a, b), S(c), S("OH", a, b), True, True)])
+    def unpack(src, rest, o, lists):
+        if lists:
+            ts(S(lists, 0, 96), src, WHOLE, op.add, WHOLE, op.subtract)
+        ts(S("J", o, o + 96), src, WHOLE, op.add, WHOLE, op.subtract)
+        tt(rest, src, S("J", o, o + 96), op.subtract)
+        if lists:
+            ts(S(lists, 96, 192), rest, 1.0 / EPS, op.mult)
+        ts(S("J", o + 96, o + 192), rest, 1.0 / EPS, op.mult)
 
-    def unpack(o):
-        ts(S("Si", o // 2, o // 2 + 96), S("PD", 0, 96), 2048.0, op.mult)
-        ts(S("J", o, o + 96), S("Si", o // 2, o // 2 + 96), 11, op.logical_shift_right)
-        ts(S("J", o + 96, o + 192), S("Si", o // 2, o // 2 + 96), 2047, op.bitwise_and)
-
-    onehot(0)
-    onehot(1)
-    weigh("PB", "C01", 0, 512)
-    onehot(2)
-    weigh("PB", "C01", 512, 1024)
-    onehot(3)
-    weigh("PB", "C01", 1024, W)
     for a, b in C3:
+        put(S("PB", a, b), "C01", S("OH", a, b))
         tt(S("X", a, b), S("PB", a, b), S("cons", a, b), op.mult)
         wrap2("PD", "Zh", "X", a, b)
-    ts(S("IIb"), S("v127"), 0.0, op.is_equal)
-    ts(S("NIb"), S("v127", 0, 128), 0.0, op.is_equal, -1.0, op.mult)
-    ts(S("IIf"), S("v127"), 0.0, op.is_equal)
-    ts(S("L1b"), S("v127", 0, 128), 0.0, op.is_equal, L1, op.mult)
     for a, b in C3:
-        weigh("PA", "C23", a, b)
-    unpack(0)
-    cp(S("Ju"), S("J", 0, 192))
+        put(S("PA", a, b), "C23", S("OH", a, b))
+    unpack(S("PD", 0, 96), S("PD", 96, 192), 0, "Ju")
 
-    shift("PC", "IIb", "K1", V, False)
-    shift("PC", "IIb", "q0s", V, False, o=256)
-    act(S("t0"), S("PC"), fn.Copy)
+    urgent(9000, shift, "PC", "IIb", "K1", V, False)
+    urgent(9000, shift, "PC", "IIb", "q0s", V, False, 256)
+    urgent(9000, act, S("t0"), S("PC"), fn.Copy)
     send(0, nxt, S("t0"), S("K2", V, W + 256))
 
-    def decide(q, qc, lam, lists, dj, ju, o0, le1, fill, pre):
-        for k, (dd, ff, bank) in enumerate((("D0", "F0", "PC"), ("D1", "F1", "PD"))):
-            for a, b in C3:
-                tt(S(dd, a, b), G(q, lists, a, b, 96 * k), S(qc, a, b), op.subtract)
-                act(S(dd, a, b), S(dd, a, b), fn.Square, scale=1.0 / lam)
-                if k == 0 or a // 512 < 3 - le1:
-                    act(S(ff, a, b), S(dd, a, b), fn.Sign, bias=SQ, scale=-1.0)
-                    wrap2(bank, "Zb", ff, a, b)
-            if k == 0:
-                pre()
-        fill()
-        for a, b in C3[3 - le1:]:
-            ts(S("F1", a, b), S("D1", a, b), SQ, op.is_lt, 0.5, op.subtract)
-            wrap2("PD", "Zb", "F1", a, b)
+    def choose(least, dj, ju, o0, sel):
         p1, p2, p3 = S("PC", 96, 192), S("PC", 192, 288), S("PD", 96, 192)
         if o0:
-            ts(S(o0), S("PC", 0, 96), 1.0, op.is_ge)
-        ts(p1, S("PC", 0, 96), 1.0, op.is_ge)
-        ts(p2, S("PC", 0, 96), 1.0, op.is_lt)
+            ts(S(o0), S("PC", 0, 96), least, op.is_ge)
+        ts(p1, S("PC", 0, 96), least, op.is_ge)
+        ts(p2, S("PC", 0, 96), least, op.is_lt)
+        if sel:
+            p4 = S("PC", 288, 384)
+            ts(p4, S("PC", 0, 96), least, op.is_lt, float(W), op.mult)
+            tt(p4, p4, S("iw"), op.add)
+            cp(S("selu"), p4)
         tt(p1, p1, S(dj, 0, 96), op.mult)
         tt(S("s3"), p2, S(dj, 96, 192), op.mult)
         tt(S("s4"), p1, S("iw"), op.add)
-        ts(p3, S("PD", 0, 96), 0.25, op.is_ge)
+        ts(p3, S("PD", 0, 96), least, op.is_ge)
         tt(p3, p3, S("s3"), op.mult)
+        urgent(2000, tt, S("jh"), p3, S("s4"), op.add)
         tt(S("jf"), p3, S("s4"), op.add)
         cp(S(ju), S("jf"))
-        cp(S("jh"), S("jf"))
 
-    def spread_pre(k):
+    def partner(bank, k, ju, dk, rk, ract, chunks):
         for a, b in C3:
-            mm([(S("PB", a, b), S("NIb"), S(k, a, b), True, False)])
+            urgent(2000, mm, [(S(bank, a + l, b, 16), S("R", 128 * l, 128 * l + 128), S("jh", a // 16, b // 16), False, l == 15) for l in range(16)], 32)
+            urgent(2000, act, S("Wn", a, b), S(bank, a, b), fn.Copy)
+        for c, (a, b) in enumerate(chunks):
+            tt(S(dk, a, b), G("Wn", ju, a, b), S("io2", a, b), op.subtract)
+            if ract >> c & 1:
+                act(S(rk, a, b), S(dk, a, b), fn.Relu, bias=-1.0)
+            else:
+                ts(S(rk, a, b), S(dk, a, b), 1.0, op.subtract, 0.0, op.max)
 
-    def spread():
-        for a, b in C3:
-            mm([(S("PB", a + l, b, 16), S("R", 128 * l, 128 * l + 128), S("jh", a // 16, b // 16), False, l == 15) for l in range(16)], 32)
-            act(S("Wn", a, b), S("PB", a, b), fn.Copy)
+    def differ(x, win, ju, to, w, a, b):
+        act(S(to, a, b), G(win, ju, a, b), fn.Copy)
+        put(x, w, S(to, a, b), False)
 
-    def partner_k(a, b):
-        act(S("D1", a, b), S("D1", a, b), fn.Abs)
-        act(S("KM", a, b), S("D1", a, b), fn.Relu, bias=1.0, scale=-1.0)
+    def hits(x, y, dq, dk, rk, k, kh, how, a, b, h):
+        least = 1.0
+        if how == 2:
+            least = 2.0
+            act(S("HB", a, b), x, fn.Sign)
+            mm([(y, S("IIb", 0, 128), S(dq, a, b), True, False), (y, S("IIb", 0, 128), S("HB", a, b), False, True)])
+            act(S("FH", a, b), y, fn.Abs)
+        elif how == 1:
+            tt(h, x, S(dq, a, b), op.mult)
+            act(S("FH", a, b), h, fn.Sign)
+        else:
+            tt(S("HB", a, b), x, S(dq, a, b), op.mult)
+            ts(S("FH", a, b), S("HB", a, b), 0.0, op.is_gt)
+        mm([(y, S("IIb", 0, 128), S(dk, a, b), True, False), (y, S("N8"), S(rk, a, b), False, False),
+            (y, S("IIb", 0, 128), S("FH", a, b), False, True)])
+        act(y, y, fn.Relu, bias=-least)
+        tt(kh, y, S(k, a, b), op.mult)
 
-    def pre1():
-        tt(S("dJ", 0, 96), S("J", 0, 96), S("iw"), op.subtract)
-        tt(S("dJ", 96, 192), S("J", 96, 192), S("iw"), op.subtract)
-        spread_pre("K1")
-
-    def fill1():
-        for a, b in C3:
-            tt(S("X", a, b), S("PA", a, b), S("cons", a, b), op.mult)
-            mm([(S("PA", a, b), S("NIb"), S("q0s", a, b), True, False)])
-
-    decide("q0s", "q0c", 1.0, "Ju", "dJ", "j1u", "o0k", OPT["le0"], fill1, pre1)
-    spread()
+    for a, b in C3:
+        tt(S("X", a, b), S("PA", a, b), S("cons", a, b), op.mult)
+    for c, (a, b) in enumerate(C3):
+        if "d" in OPT["r0"][c::3]:
+            act(S("A", a, b), S("q0s", a, b), fn.Identity, bias=-0.25)
+    for k, (bank, ff, cnt, qb) in enumerate((("PB", "F0", "PC", "QB"), ("PA", "F1", "PD", "HB"))):
+        for c, (a, b) in enumerate(C3):
+            if OPT["r0"][3 * k + c] == "d":
+                src = S("DD", W * k + a, W * k + b)
+                tt(src, G("q0s", "Ju", a, b, 96 * k), S("A", a, b), op.subtract)
+            else:
+                src = S(bank, a, b)
+                mm([(src, S("NIb"), S("q0s", a, b), True, False), (src, S("B4"), S("OH", a, b), False, False)])
+                act(S(qb, a, b), G("q0s", "Ju", a, b, 96 * k), fn.Copy)
+                put(src, "IIb", S(qb, a, b), False)
+            ts(S(ff, a, b), src, TWO, op.add, TWO, op.is_equal)
+            wrap2(cnt, "Zb", ff, a, b)
+    tt(S("dJ", 0, 96), S("J", 0, 96), S("iw"), op.subtract)
+    tt(S("dJ", 96, 192), S("J", 96, 192), S("iw"), op.subtract)
+    for a, b in C3:
+        put(S("PB", a, b), "IIb", S("K1", a, b))
+    choose(8.5, "dJ", "j1u", "o0k", False)
+    spread = len(calls) + 4
+    partner("PB", "K1", "j1u", "DK1", "RK1", OPT["ra1"], CV)
+    behind(spread, wrap, "PC", "Zh", "X", ((0, W),), 288)
+    unpack(S("PC", 288, 384), S("PC", 384, 480), 192, None)
     for a, b in CV:
-        tt(S("E1a", a, b), G("v0s", "j1u", a, b), S("v0c", a, b), op.subtract)
-    for a, b in CL:
-        act(S("QB", a, b), G("q0s", "j1u", a, b), fn.Copy)
-        mm([(S("PA", a, b), S("IIb", 0, 128), S("QB", a, b), False, True)])
-    wrap("PD", "Zh", "X")
-    for a, b in CL:
-        tt(S("D1", a, b), G("Wn", "j1u", a, b), S("io2", a, b), op.subtract)
-        act(S("PB", a, b), S("PA", a, b), fn.Sign)
-        partner_k(a, b)
-        act(S("PA", a, b), S("E1a", a, b), fn.Sign)
-    unpack(192)
-    ts(S("NIf"), S("v127", 0, 128), 0.0, op.is_equal, -1.0, op.mult)
-    ts(S("L2b"), S("v127", 0, 128), 0.0, op.is_equal, L2, op.mult)
-    ts(S("col", 3, 4), S("pc", 0, 1), 15.0, op.mult)
-    if OPT["aqpe"]:
-        ts(S("B8a", parts=8), S("io3", parts=8), S("col", 3, 4, parts=8), op.is_equal, -L1, op.mult)
-        ts(S("B8b", parts=8), S("io3", parts=8), S("col", 3, 4, parts=8), op.is_equal, -L2, op.mult)
-    else:
-        ts(S("B8", parts=8), S("io3", parts=8), S("col", 3, 4, parts=8), op.is_equal)
-    if OPT["v0pe"]:
-        ts(S("N256"), S("v127", 0, 128), 0.0, op.is_equal, -L2 / 16, op.mult)
+        if OPT["dq1"] == "d":
+            tt(S("DQ1", a, b), G("q0s", "j1u", a, b), S("q0c", a, b), op.subtract)
+        else:
+            y = S("PD", 0, 256) if a == V else S("PB", a, b)
+            put(y, "NIb", S("q0s", a, b))
+            differ(y, "q0s", "j1u", "AB0", "IIb", a, b)
+            act(S("DQ1", a, b), y, fn.Sign)
 
     def lists2():
-        wrap("PD", "Zb", "KM")
+        flag, t = S("PC", 256, 352), S("PC", 352, 448)
+        wrap("PC", "Zb", "DK1", o=256)
         tt(S("s5"), S("J", 96, 288), S("J", 192, 384), op.subtract)
-        ts(S("PD", 0, 96), S("PD", 0, 96), 0.0, op.is_gt)
-        tt(S("PD", 0, 96), S("PD", 0, 96), S("o0k"), op.mult)
-        tt(S("PD", 96, 192), S("PD", 0, 96), S("s5", 0, 96), op.mult)
-        tt(S("PD", 192, 288), S("PD", 0, 96), S("s5", 96, 192), op.mult)
-        tt(S("PD", 96, 288), S("PD", 96, 288), S("J", 192, 384), op.add)
-        cp(S("J2u"), S("PD", 96, 288))
-        tt(S("dJ2", 0, 96), S("PD", 96, 192), S("iw"), op.subtract)
-        tt(S("dJ2", 96, 192), S("PD", 192, 288), S("iw"), op.subtract)
+        ts(flag, flag, SIXTEEN, op.add, SIXTEEN, op.is_equal)
+        tt(flag, flag, S("o0k"), op.mult)
+        tt(t, flag, S("s5", 0, 96), op.mult)
+        tt(flag, flag, S("s5", 96, 192), op.mult)
+        tt(t, t, S("J", 192, 288), op.add)
+        tt(flag, flag, S("J", 288, 384), op.add)
+        cp(S("J2u", 0, 96), t)
+        cp(S("J2u", 96, 192), flag)
+        tt(S("dJ2", 0, 96), t, S("iw"), op.subtract)
+        tt(S("dJ2", 96, 192), flag, S("iw"), op.subtract)
 
-    def aims():
+    def aims(pa):
         for a, b in C3:
-            mm([(S("PD"), S("B8", parts=8), S("aims", a, b, parts=8), True, True)])
-            act(S("AM1", a, b), S("PD"), fn.Copy, scale=L1)
+            mm([(S(pa, a, b), S("B8", parts=8), S("aims", a, b, parts=8), True, True)])
+            act(S("AM", a, b), S(pa, a, b), fn.Copy)
 
-    def newton(two):
-        for k, (a, b) in enumerate(C3):
-            act(S(two[k % 2]), S("S1", a, b), fn.Copy)
-            tt(S("R0", a, b), S(two[k % 2]), S("R0", a, b), op.mult)
+    def newton():
+        for a, b in C3:
+            behind(len(calls) - 1, act, S("R0", a, b), S("K1", a, b), fn.Ln)
+        for a, b in C3:
+            behind(len(calls) - 1, act, S("R0", a, b), S("R0", a, b), fn.Exp, 0.6931472, -1.0)
+        act3("SQ", "R0", fn.Square, scale=0.5)
+        act3("R0", "R0", fn.Copy, scale=-1.0)
 
-    def shot(x):
-        lam, lb, v0, v0c, base = ((L1, "L1b", "v0s", "v0c", "V0b"), (L2, "L2b", "V0p", "CQ", "V0q"))[x]
-        v1, a2, am, y2, e1, vout = (("V1a", "A2a", "AM1", "Y2a", "E1a", "V0p"), ("V1b", "A2b", "AM2", "Y2b", "E1b", "Wn"))[x]
-        dl = 0.1875 * 16 * lam
+    def signed(chunks, spot):
+        for a, b in chunks:
+            y = spot(a, b)
+            mm([(y, S("IIb", 0, 128), S("DK1", a, b), True, False), (y, S("N8"), S("RK1", a, b), False, True)])
+            act(y, y, fn.Relu)
+            tt(y, y, S("K1", a, b), op.mult)
+            tt(S("KS", a, b), y, S("DQ1", a, b), op.mult)
 
-        def one(a, b):
-            tt(S("PB", a, b), S("KM", a, b), S("PB", a, b), op.mult)
+    def newton2(bank):
+        for a, b in C3:
+            put(S(bank), "IIb", S("K1", a, b))
+            tt(S("RR", a, b), S(bank), S("SQ", a, b), op.mult)
+        dma("pool", S("RR"), S("R0"), True)
 
-        def two(a, b):
-            tt(S("KS", a, b), S("PB", a, b), S("K1", a, b), op.mult)
+    def shot(x, pa, pb):
+        v0, ii, big, nbig, vg = (("v0s", "IIb", "IIb", "NIb", "QB"), ("V0p", "IIf", "IIf", "NIf", "VG"))[x]
+        v1, a2, y2, vout = (("V1a", "A2a", "Y2a", "V0p"), ("V1b", "A2b", "Y2b", "Wn"))[x]
 
-        def ee(a, b):
-            tt(S(e1, a, b), G(v0, "j1u", a, b), S(v0c, a, b), op.subtract)
-            act(S("PA", a, b), S(e1, a, b), fn.Sign)
+        def X(a, b):
+            return S("PD", 0, 256) if a == V else S(pa, a, b)
 
-        def hh(a, b):
-            tt(S("PA", a, b), S("PA", a, b), S("KS", a, b), op.mult)
-            act(S("PA", a, b), S("PA", a, b), fn.Relu, scale=-1.0)
+        def Y(a, b):
+            return S("PD", 256, 512) if a == V else S(pb, a, b)
 
-        def tv(a, b):
-            tt(S("PB", a, b), S("PA", a, b), S(e1, a, b), op.mult)
-
-        def vnew(a, b):
-            if a < V and OPT["q1pe"] & (1 << x):
-                tt(S(v1, a, b), S("PB", a, b), S(v0, a, b), op.add)
-                mm([(S("PB", a, b), S("IIf", 0, 128), S(v1, a, b), True, False), (S("PB", a, b), S(lb), S("q0s", a, b), False, True)])
-                return
-            out = S("V1v") if a == V else S(v1, a, b)
-            tt(out, S("PB", a, b), S(v0, a, b), op.add)
+        fast = x == 1 and OPT["fast"]
+        for a, b in CV:
+            if a == V and fast:
+                put(X(a, b), "IIf", S("KS", a, b))
+                act(S("CQ", a, b), S(v0, a, b), fn.Copy)
+            else:
+                put(X(a, b), big, S(v0, a, b), whole=b == V)
+        clear("PC")
+        shift("PC", ii, v0, V, False, start=False)
+        for a, b in CV:
+            if a < V or not fast:
+                differ(X(a, b), v0, "j1u", vg, nbig, a, b)
+        for c, (a, b) in enumerate(CV):
+            how = 2 if OPT["h1"] >> (4 * x + c) & 1 else OPT["fa1"] >> x & 1
+            if a == V and fast:
+                tt(S("tv"), G(v0, "j1u", a, b), S("CQ", a, b), op.subtract)
+                tt(X(a, b), X(a, b), S("tv"), op.mult)
+                if fast == 1:
+                    act(X(a, b), X(a, b), fn.Relu, scale=-1.0)
+                else:
+                    ts(X(a, b), X(a, b), -1.0, op.mult, 0.0, op.max)
+                tt(S("DL1", a, b), X(a, b), S("DQ1", a, b), op.mult)
+            elif x == 1 and OPT["ks"][c] != "-":
+                act(Y(a, b), X(a, b), fn.Sign)
+                tt(Y(a, b), Y(a, b), S("KS", a, b), op.mult)
+                act(S("KH1", a, b), Y(a, b), fn.Relu)
+            else:
+                hits(X(a, b), Y(a, b), "DQ1", "DK1", "RK1", "K1", S("KH1", a, b), how, a, b, Y(a, b))
             if a == V:
-                shift("PC", "IIf", "V1v", 0, False)
+                if not fast:
+                    tt(S("DL1", a, b), X(a, b), S("KH1", a, b), op.mult)
+                shift("PC", "NIf", "DL1", V, False, start=False)
                 act(S(("t1", "t3")[x]), S("PC", 0, 256), fn.Copy)
                 send(1 + 2 * x, nxt, S(("t1", "t3")[x]), S(v1, V, W))
-                mm([(S("PC", 256, 512), S(lb), S("K2", W, W + 256), True, True)])
+                if fast:
+                    act(X(a, b), S("tv"), fn.Sign)
+                    tt(X(a, b), X(a, b), S("KS", a, b), op.mult)
+                    act(S("KH1", a, b), X(a, b), fn.Relu, scale=-1.0)
+                put(Y(a, b), "Lb", S("K2", W, W + 256))
+            elif OPT["v1pe"] >> (4 * x + c) & 1:
+                tt(S("DL1", a, b), X(a, b), S("KH1", a, b), op.mult)
+                mm([(Y(a, b), S(ii, 0, 128), S(v0, a, b), True, False), (Y(a, b), S("NIf", 0, 128), S("DL1", a, b), False, True)])
+                act(S(v1, a, b), Y(a, b), fn.Copy)
+                put(X(a, b), "Lb", S("q0s", a, b))
+                tt(S("q1", a, b), X(a, b), S(v1, a, b), op.add)
             else:
-                mm([(S("PB", a, b), S(lb), S("q0s", a, b), True, True)])
-
-        def qnew(a, b):
-            if a < V and OPT["q1pe"] & (1 << x):
-                act(S("q1", a, b), S("PB", a, b), fn.Copy)
-                if OPT["cqdma"]:
+                tt(Y(a, b), X(a, b), S("KH1", a, b), op.mult)
+                act(S("DL1", a, b), Y(a, b), fn.Copy)
+                tt(S(v1, a, b), S(v0, a, b), Y(a, b), op.subtract)
+                put(X(a, b), "Lb", S("q0s", a, b))
+                if OPT["q1pe"] >> (4 * x + c) & 1:
+                    put(X(a, b), "IIf", S(v1, a, b), False)
+                    act(S("q1", a, b), X(a, b), fn.Copy)
+                else:
+                    tt(S("q1", a, b), X(a, b), S(v1, a, b), op.add)
+            if a < V:
+                if OPT["cqdma"] >> x & 1:
                     dma("sp", S("CQ", a, b), S("q1", a, b))
                 else:
-                    act(S("CQ", a, b), S("PB", a, b), fn.Copy)
-                return
-            tt(S("q1", a, b), S("PC", 256, 512) if a == V else S("PB", a, b), S(v1, a, b), op.add)
-            act(S("CQ", a, b), S("q1", a, b), fn.Copy)
-
+                    act(S("CQ", a, b), S("q1", a, b), fn.Copy)
         if x == 0:
-            one(*C3[2]); two(*C3[2]); one(*c0); hh(*cv); two(*c0); one(*c1); tv(*cv); hh(*c0); vnew(*cv)
-            two(*c1); hh(*c2); hh(*c1)
             lists2()
-            if not OPT["aqpe"]:
-                aims()
-        else:
-            ee(*cv); ee(*c0); hh(*cv); ee(*c1); tv(*cv); hh(*c0); vnew(*cv); ee(*c2); hh(*c1); hh(*c2)
-        stagger([tv, vnew], [c0, c1, c2], 0.5)
-        for a, b in C3:
-            act(S("KH1", a, b), S("PA", a, b), fn.Copy)
+            if "d" in OPT["p4"]:
+                aims(pa)
+        tt(S("q1", V, W), Y(V, W), S(v1, V, W), op.add)
+        tt(S("CQ", V, W), Y(V, W), S(v1, V, W), op.add)
+
+        if x == 0:
+            act3("DQ1", "DQ1", fn.Sign)
+            signed([(a, b) for c, (a, b) in enumerate(CV) if OPT["ks"][c] == "3"], lambda a, b: S(pa, a, b))
+        elif OPT["nw"] == 1:
+            newton2("PC")
         dma("sp", S("CP", 0, V), S(v1, 0, V))
-        for c in (c0, c1, c2):
-            qnew(*c)
-        for a, b in (c0, c1):
-            mm([(S("PA", a, b), S("NIf"), S("q1", a, b), True, False)])
-        if x == 0:
-            for a, b in C3:
-                mm([(S("PB", a, b), S("IIb", 0, 128), S("K1", a, b), True, True)])
-        elif OPT["rk"]:
-            newton(("PD", "PD"))
-        qnew(*cv)
         dma("sp", S("CP", V, W), S(v1, V, W))
-        mm([(S("PA", *C3[2]), S("NIf"), S("q1", *C3[2]), True, False)])
-
-        def fill2():
-            for a, b in C3:
-                if x == 0:
-                    tt(S("S1", a, b), S("PB", a, b), S("R0", a, b), op.mult)
-            spread_pre("K2")
-
-        decide("q1", "CQ", lam, "J2u", "dJ2", "j2u", None, OPT[("lea", "leb")[x]], fill2, lambda: None)
-        spread()
+        for k, (ab, ff, cnt) in enumerate((("AB0", "F0", "PC"), ("AB1", "F1", "PD"))):
+            for c, (a, b) in enumerate(C3):
+                src = S("DD", W * k + a, W * k + b)
+                tt(src, G("q1", "J2u", a, b, 96 * k), S("CQ", a, b), op.subtract)
+                act(S(ab, a, b), src, fn.Abs, scale=NEAR / L)
+                if OPT["ta2"] >> (3 * k + c) & 1:
+                    act(S(ff, a, b), S(ab, a, b), fn.Sign, bias=252.5 / 256, scale=-1.0)
+                else:
+                    ts(S(ff, a, b), S(ab, a, b), 252.5 / 256, op.is_lt, 0.5, op.subtract)
+                wrap2(cnt, "Zb", ff, a, b)
+        for a, b in C3:
+            put(S(pb, a, b), "IIb", S("K2", a, b))
+        choose(0.25, "dJ2", "j2u", None, True)
         for a, b in CL:
+            act(S("DQ2", a, b), G("DD", "selu", a, b), fn.Copy)
+            put(S(pa, a, b), "NIb", S("DQ2", a, b))
             tt(S("E2", a, b), G(v1, "j2u", a, b), S("CP", a, b), op.subtract)
-        for a, b in CL:
-            act(S("D0", a, b), G("q1", "j2u", a, b), fn.Copy)
-            mm([(S("PA", a, b), S("IIf", 0, 128), S("D0", a, b), False, True)])
-        for a, b in CL:
-            tt(S("D1", a, b), G("Wn", "j2u", a, b), S("io2", a, b), op.subtract)
-        for a, b in CL:
-            tt(S("PA", a, b), S("PA", a, b), S("E2", a, b), op.mult)
-            act(S("F0", a, b), S("PA", a, b), fn.Sign)
-            if OPT["fold"]:
-                act(S("D1", a, b), S("D1", a, b), fn.Abs)
-                mm([(S("PA", a, b), S("IIf", 0, 128), S("D1", a, b), True, False), (S("PA", a, b), S("IIb", 0, 128), S("F0", a, b), False, True)])
-                act(S("PA", a, b), S("PA", a, b), fn.Relu, scale=-1.0)
-                continue
-            partner_k(a, b)
-            mm([(S("PA", a, b), S("NIb"), S("F0", a, b), True, False), (S("PA", a, b), S("IIb", 0, 128), S("KM", a, b), False, True)])
-            act(S("PA", a, b), S("PA", a, b), fn.Relu, bias=-1.0)
-        if x == 0:
-            act3("S1", "S1", fn.Identity, bias=-2.0 / L2 ** 2, scale=1.0 / L2 ** 2)
-            if not OPT["v0pe"]:
-                act3("V0b", "v0s", fn.Copy, scale=L2 / 16)
-        else:
-            act3("V0q", "V0p", fn.Copy, scale=256.0)
+        partner(pb, "K2", "j2u", "DK2", "RK2", OPT["ra2"], CL)
+        for c, (a, b) in enumerate(CL):
+            xx, yy, how = S(pa, a, b), S(pb, a, b), OPT["p4"][c]
+            am = (xx, S("B8s", parts=8), S("aims", a, b, parts=8))
+            hits(xx, yy, "E2", "DK2", "RK2", "K2", yy, OPT["fa2"] >> c & 1, a, b, xx)
+            unit = 1.0
+            if how == "f":
+                put(xx, "Is", S(v1, a, b))
+                tt(S("Wn", a, b), yy, S("E2", a, b), op.mult)
+                mm([(xx, S("Is"), S("Wn", a, b), False, False), (xx, S("Is"), S("q1", a, b), False, False), am + (False, True)])
+            else:
+                tt(xx, yy, S("E2", a, b), op.mult)
+                tt(xx, xx, S(v1, a, b), op.add)
+                if how == "a":
+                    tt(S("Wn", a, b), xx, S("q1", a, b), op.add)
+                    mm([(xx, S("Is"), S("Wn", a, b), True, False), am + (False, True)])
+                else:
+                    tt(xx, xx, S("q1", a, b), op.add)
+                    tt(xx, xx, S("AM", a, b), op.add)
+                    unit = 1.0 / BIG
+            act(S("A", a, b), xx, fn.Copy, scale=unit)
+            if OPT["p5"][c] == "d":
+                act(S("CQ", a, b), xx, fn.Copy, scale=unit)
+            else:
+                if a == 1024:
+                    act(S("CQ", V, W), S(pa, V, W), fn.Copy, scale=unit)
+                if unit != 1.0:
+                    act(xx, xx, fn.Copy, scale=unit)
 
-        def aq(a, b):
-            if OPT["aqpe"]:
-                mm([(S("PA", a, b), S("IIf", 0, 128), S("DA", a, b), True, False),
-                    (S("PA", a, b), S(("B8a", "B8b")[x], parts=8), S("aims", a, b, parts=8), False, True)])
-                act(S("A", a, b), S("PA", a, b), fn.Copy)
-                act(S("CQ", a, b), S("PA", a, b), fn.Copy)
-                return
-            tt(S("A", a, b), S("PA", a, b), S(am, a, b), op.subtract)
-            act(S("CQ", a, b), S("A", a, b), fn.Copy)
-
-        stagger([lambda a, b: tt(S("PB", a, b), S("PA", a, b), S("K2", a, b), op.mult),
-                 lambda a, b: tt(S("PA", a, b), S("PB", a, b), S("E2", a, b), op.mult),
-                 lambda a, b: tt(S("PA", a, b), S("PA", a, b), S(v1, a, b), op.add),
-                 lambda a, b: tt(S("DA" if OPT["aqpe"] else "PA", a, b), S("PA", a, b), S("q1", a, b), op.add),
-                 aq], CV if OPT["c4"] & 2 else CL, OPT["st2"])
-
-        def da2(a, b):
-            tt(S("DA", a, b), G("A", "j2u", a, b), S("CQ", a, b), op.subtract)
-
-        def b1(a, b):
-            tt(S("PB", a, b), S("PB", a, b), S("DA", a, b), op.mult)
-
-        def b2(a, b):
-            tt(S("PA", a, b), S("PB", a, b), S("A", a, b), op.add)
-
-        def b3(a, b):
-            tt(S("A2v") if a == V else S(a2, a, b), S("PA", a, b), S("A", a, b), op.add)
+        clear("PC")
+        shift("PC", "IIf", "A", V, True, start=False)
+        for a, b in CV:
+            xx, yy = S(pa, a, b), S(pb, a, b)
+            if a == V or OPT["p5"][(a // 512 + 1) % 3] == "d":
+                tt(S("DA", a, b), G("A", "j2u", a, b), S("CQ", a, b), op.subtract)
+            else:
+                act(S("VG", a, b), G("A", "j2u", a, b), fn.Copy)
+                tt(S("DA", a, b), S("VG", a, b), xx, op.subtract)
             if a == V:
-                shift("PC", "IIf", "A2v", 0, True)
+                tt(S("tv"), yy, S("DA", a, b), op.mult)
+                shift("PC", "IIf", "tv", 0, True, start=False)
+                shift("PC", "IIf", "A", V, True, start=False)
                 act(S(("t2", "t4")[x]), S("PC", 0, 256), fn.Copy)
+                if x == 0:
+                    newton()
                 send(2 + 2 * x, prv, S(("t2", "t4")[x]), S(a2, V, W))
+                tt(S(y2, a, b), S("tv"), S("E2", a, b), op.mult)
             else:
-                dma("sp", S("CP", a, b), S(a2, a, b))
-                act(S("PA", a, W if b == V else b), S("KH1", a, W if b == V else b), fn.Copy)
-
-        def zz(a, b):
-            tt(S("Yv") if (a == V and x == 1) else S(y2, a, b), S("PB", a, b), S("E2", a, b), op.mult)
-
-        da2(*cv); da2(*c0); b1(*cv); da2(*c1); b2(*cv); b1(*c0); b3(*cv); da2(*c2)
-        if x == 1:
-            zz(*cv)
-            mm([(S("PD", 0, 128), S("IIf", 16, 144), S("Y2a", V, H), True, False),
-                (S("PD", 0, 128), S("IIf", 16, 144), S("Yv", 0, 128), False, True),
-                (S("PD", 128, 256), S("IIf", 64, 192), S("Y2a", H, W), True, False),
-                (S("PD", 128, 256), S("IIf", 64, 192), S("Yv", 128, 256), False, True)])
-            act(S("t5"), S("PD", 0, 256), fn.Copy)
-            send(5, prv, S("t5"), S("Y2b", V, W))
-        else:
-            if not OPT["aqpe"]:
-                act3("AM2", "AM1", fn.Copy, scale=L2 / L1)
-            act3("ZZ", "K1", fn.Square, scale=L2)
-        b1(*c1); b2(*c0); b1(*c2); b2(*c1); b3(*c0); b2(*c2); b3(*c1); b3(*c2)
-        for c in ((c0, c1, C3[2]) if x == 0 else (c0, c1, c2)):
-            zz(*c)
-        if x == 0 and not OPT["rk"]:
-            newton(("PD", "PC"))
-        act(S("CP", V, W), S(a2, V, W), fn.Copy)
-
-        sums = [S("PC"), S("PD"), S("PA", 1024, W)]
+                tt(yy, yy, S("DA", a, b), op.mult)
+                tt(xx, yy, S("A", a, b), op.add)
+                tt(S(a2, a, b), xx, S("A", a, b), op.add)
+                tt(S(y2, a, b), yy, S("E2", a, b), op.mult)
+            if a == V and x == 1:
+                mm([(S("PD", 256, 384), S("IIf", 16, 144), S("Y2a", V, H), True, False),
+                    (S("PD", 256, 384), S("IIf", 16, 144), S("Y2b", V, H), False, True),
+                    (S("PD", 384, 512), S("IIf", 64, 192), S("Y2a", H, W), True, False),
+                    (S("PD", 384, 512), S("IIf", 64, 192), S("Y2b", H, W), False, True)])
+                act(S("t5"), S("PD", 256, 512), fn.Copy)
+                send(5, prv, S("t5"), S("YL"))
+        if 2 * x == OPT["nw"]:
+            newton2(("PD", "PC")[x])
         if x == 0:
-            act3("ZZ", "ZZ", fn.Copy, scale=-1.0)
-            act3("Y2a", "Y2a", fn.Copy, scale=(L2 / L1) ** 2)
-            dma("pool", S("ZZ", 0, V), S("Y2a", 0, V), True)
-        else:
-            for (a, b), bank in list(zip(C3, sums))[:2]:
-                mm([(bank, S("IIf", 0, 128), S("ZZ", a, b), True, False)])
-                mm([(bank, S("IIf", 0, 128), S("Y2b", a, b), False, False)])
-        for a, b in C3:
-            tt(S("DA", a, b), G(a2, "j1u", a, b), S("CP", a, b), op.subtract)
-        for a, b in C3:
-            tt(S("PA", a, b), S("PA", a, b), S("DA", a, b), op.mult)
+            signed([(a, b) for c, (a, b) in enumerate(CV) if OPT["ks"][c] == "5"], lambda a, b: S("PD", 0, b - a))
+        dma("pool", S("ZZ", 0, V if x == 0 else 512), S(y2, 0, V if x == 0 else 512), True)
+
+        chunks = CN if OPT["c6"] else C3
+        last = x == 1 and OPT["yvacc"]
+        if last:
+            dma("sp", D("yv"), S("V0p"))
+
+        def spot(a, b):
+            if a < 512:
+                return S(pa, a, b)
+            return S("PC") if a < 1024 else S("PD", a - 1024, b - 1024)
+        for a, b in chunks:
+            if a < V:
+                put(S(pa, a, b), "IIf", S(a2, a, b), whole=b == V)
         if x == 1:
-            for (a, b), bank in zip(C3, sums):
-                tt(S("D1", a, b), S("PA", a, b), S("E1b", a, b), op.mult)
-                if a < 1024:
-                    mm([(bank, S("IIf", 0, 128), S("D1", a, b), False, True)])
-
-        def f1(a, b):
-            tt(S("PB", a, b), S("PA", a, b), S(a2, a, b), op.add)
-            if x == 0:
-                tt(S("D1", a, b), S("PA", a, b), S("E1a", a, b), op.mult)
-                act(S("D1", a, b), S("D1", a, b), fn.Copy, scale=(L2 / L1) ** 2)
-            elif a == 1024:
-                mm([(sums[2], S("IIf", 0, 128), S(z, a, b), z == "ZZ", z == "D1") for z in ("ZZ", "Y2b", "D1")])
-
-        def f3(a, b):
-            if x == 0 and OPT["v0pe"]:
-                mm([(S("PB", a, b), S("IIf", 0, 128), S("D0", a, b), True, False), (S("PB", a, b), S("N256"), S("v0s", a, b), False, True)])
-                act(S(vout, a, b), S("PB", a, b), fn.Copy, scale=-1.0)
-                act(S("CQ", a, b), S("PB", a, b), fn.Copy, scale=-1.0)
-                return
-            tt(S(vout, a, b), S(base, a, b), S("PB", a, b), op.subtract)
-            if x == 0:
-                act(S("CQ", a, b), S(vout, a, b), fn.Copy)
+            put(S("PC"), "IIf", S("ZZ", 512, 1024))
+            put(S("PC"), "IIf", S("Y2b", 512, 1024), False)
+            put(S("PD"), "IIf", S("ZZ", 1024, W))
+            put(S("PD", 0, 256), "IIf", S("Y2b", 1024, V), False)
+            put(S("PD", 256, 512), "IIf", S("YL"), False)
+        for a, b in chunks:
+            if a == V:
+                act(S("VG", a, b), G(a2, "j1u", a, b), fn.Copy)
+                mm([(S(pa, a, b), S("IIf", 0, 128), S(a2, a, b), True, False), (S(pa, a, b), S("NIf", 0, 128), S("VG", a, b), False, True)])
             else:
-                act(S(vout, a, b), S(vout, a, b), fn.Copy, scale=1.0 / (16 * L2))
-                dma("sp", D("yv", a, b), S(vout, a, b))
-
-        stagger([f1, lambda a, b: ts(S("D0" if x == 0 and OPT["v0pe"] else "PB", a, b), S("PB", a, b), dl, op.min, -dl, op.max), f3],
-                CV if x == 0 and OPT["c4"] & 1 else CL, OPT["st1"])
+                differ(S(pa, a, b), a2, "j1u", "VG", "NIf", a, b)
+        for a, b in chunks:
+            xx, yy = S(pa, a, b), S(pb, a, b)
+            tt(yy, xx, S("KH1", a, b), op.mult)
+            tt(xx if x == 1 and a == 0 else S("Y1", a, b), xx, S("DL1", a, b), op.mult)
+            tt(yy, yy, S(a2, a, b), op.subtract)
+            if last:
+                ts(S(vout, a, b), yy, 0.1875, op.min, -0.1875, op.max)
+                dma("pool", D("yv", a, b), S(vout, a, b), True)
+            else:
+                ts(yy, yy, 0.1875, op.min, -0.1875, op.max)
+                tt(S(vout, a, b), yy, S(v0, a, b), op.add)
+            if x == 1:
+                if not last:
+                    dma("sp", D("yv", a, b), S(vout, a, b))
+                bank = spot(a, b)
+                if a == 0:
+                    tt(bank, bank, S("ZZ", a, b), op.add)
+                else:
+                    put(bank, "IIf", S("Y1", a, b), False)
+                if b != V:
+                    a = a // 512 * 512
+                    tt(S("VG", a, b), spot(a, b), S("RR", a, b), op.mult)
+                    dma("act", D("yg", a, b), S("VG", a, b))
         if x == 0:
-            dma("pool", S("ZZ"), S("D1"), True)
-        else:
-            for (a, b), bank in zip(C3, sums):
-                tt(S("D0", a, b), bank, S("R0", a, b), op.mult)
-                dma("act", D("yg", a, b), S("D0", a, b))
+            dma("pool", S("ZZ"), S("Y1"), True)
 
-    shot(0)
-    shot(1)
+    act3("ZZ", "K1", fn.Square)
+    act3("ZZ", "ZZ", fn.Copy, scale=-1.0)
+    shot(0, "PA", "PB")
+    shot(1, "PB", "PA")
     issue()
 
     g.wait_ge(T.sem.sent, count["sent"])

@@ -10,9 +10,10 @@ TWO = 2.0 ** 24
 SIXTEEN = 1.5 * 2.0 ** 27
 NEAR = 0x150aaaa / 2.0 ** 24
 
-OPT = {"r0": "aaaaaa", "fast": 1, "q1pe": 0, "ra1": 15, "ra2": 7, "fa1": 3, "fa2": 7, "h1": 0, "dq1": "d", "p5": "dmm", "v1pe": 0, "p4": "fad",
-       "cqdma": 3, "ga2": 0, "ta2": 7, "nw": 1, "yvacc": 0, "c6": 1, "turns": 12, "span": 60, "moves": 2000, "warm": 1500, "free": 0.3, "soon": 1.0, "hint": 1.0, "seed": 12345, "ks": "3333", "look": 60, "heat": 300, "tries": 0}
-CASES = [(1.56, 0.45, 150, 4000), (1.9, 0.42, 200, 5000), (1.3, 0.6, 120, 3500)]
+OPT = {"r0": "daadaa", "fast": 1, "q1pe": 0, "ra1": 15, "ra2": 0, "fa1": 3, "fa2": 7, "h1": 0, "dq1": "dddd", "x23": 0, "p5": "ddm", "v1pe": 0, "p4": "fadd",
+       "b5": 0, "fine5": 0, "z0": 1, "oh": 1, "m6": 0x24, "m7": 4,
+       "cqdma": 3, "ga2": 0, "ta2": 3, "nw": 1, "yvacc": 1, "c6": 1, "turns": 9, "span": 80, "moves": 1200, "warm": 1500, "free": 0.3, "soon": 1.0, "hint": 1.0, "seed": 12345, "ks": "3333", "fine4": 12, "h2": 15, "kf": 1, "ln": 1, "wider": 20, "lead": 3, "up1": 2500, "up2": 0, "fresh": 100, "trans": 1, "each": 0, "look": 60, "heat": 300, "tries": 0}
+CASES = [(1.6, 0.46, 200, 3600), (1.3, 0.35, 145, 2700), (1.5, 0.6, 220, 4800)]
 KEPT = {}
 
 F, B, HF, I, U = "float32", "bfloat16", "float16", "int32", "uint16"
@@ -33,6 +34,7 @@ SCRATCH.update({
     "U2": ("sbuf", [128, 144], B), "C01": ("sbuf", [128, 128], B), "C23": ("sbuf", [128, 128], B),
     "Zb": ("sbuf", [128, 144], B), "Zh": ("sbuf", [128, 144], HF), "IIf": ("sbuf", [128, 256], F), "IIb": ("sbuf", [128, 256], B),
     "NIb": ("sbuf", [128, 128], B), "NIf": ("sbuf", [128, 256], F), "Lb": ("sbuf", [128, 128], B), "Zero": ("sbuf", [128, 128], B),
+    "Js": ("sbuf", [128, 128], F), "Ibs": ("sbuf", [128, 128], B), "GA": ("sbuf", [128, 256], B), "QV": ("sbuf", [128, 256], B),
     "Is": ("sbuf", [128, 128], F), "B8s": ("sbuf", [128, 128], B),
     "B8": ("sbuf", [128, 128], B), "B4": ("sbuf", [128, 128], B), "N8": ("sbuf", [128, 128], B),
     "iwr": ("sbuf", [128, 96], F), "iw": ("sbuf", [128, 96], F), "J": ("sbuf", [128, 384], F),
@@ -56,8 +58,9 @@ def rank_program(g, core, T, topo):
     n = len(T.cores)
     nxt, prv = T.cores[(rank + 1) % n], T.cores[(rank - 1) % n]
     Q = {"pe": g.tensor, "dve": g.vector, "act": g.scalar, "pool": g, "sp": g.sync}
-    count = {"pe": 0, "dve": 0, "act": 0, "pool": 0, "dma": 0, "sent": 0}
-    seen = {q: {} for q in Q}
+    count = {"pe": 0, "dve": 0, "act": 0, "pool": 0, "dma": 0, "sent": 0, "waits": 0}
+    KEPT["count"] = count
+    seen, known = {q: {} for q in Q}, {}
     hist = {}
     dmas = []
     opened = {}
@@ -87,11 +90,16 @@ def rank_program(g, core, T, topo):
                     if hit:
                         need[tok[0]] = max(need.get(tok[0], 0), tok[1])
         for s, c in need.items():
-            if seen[q].get(s, 0) < c:
+            if seen[q].get(s, 0) < c and not any(known.get(z, {}).get(s, 0) >= c for z in need.items()):
                 Q[q].wait_ge(T.sem[s], c)
-                seen[q][s] = c
+                count["waits"] += 1
+        for z in need.items():
+            for s, c in list(known.get(z, {}).items()) + [z]:
+                seen[q][s] = max(seen[q].get(s, 0), c)
 
     def note(q, reads, writes, tok):
+        if q in seen and OPT["trans"]:
+            known[tok] = dict(seen[q])
         for x in writes:
             hist[x[0]] = [h for h in hist.get(x[0], []) if not (x[1] <= h[0] and h[1] <= x[2])]
         for xs, wr in ((reads, False), (writes, True)):
@@ -100,6 +108,7 @@ def rank_program(g, core, T, topo):
 
     calls = []
 
+    fine = [0]
     gates, hints = [], []
 
     def urgent(up, f, *args):
@@ -127,12 +136,16 @@ def rank_program(g, core, T, topo):
     def price(out, a, m, more=0):
         if len(a) > 4:
             return (50, (out[2] - out[1]) * 0.83, 0)
-        return (max(64, (out[2] - out[1]) * m) * 0.83 + more, 0, 0)
+        return (max(64, (out[2] - out[1]) * m) * 0.83 + more + OPT["each"], 0, 0)
 
     def half(out, a):
         return 0.5 if size(out) == 2 and size(a) == 2 else 1
 
     def tt(out, a, b, o):
+        if fine[0] and out[2] - out[1] == 512 and len(a) == 4:
+            for k in (0, 256):
+                tt(*[S(x[0], x[1] + k, x[1] + k + 256) for x in (out, a, b)], o)
+            return
         both = SCRATCH[a[0]][0] == SCRATCH[b[0]][0]
         run("dve", lambda: g.vector.tensor_tensor(out[3], a[3], b[3], o), [a, b], [out], price(out, a, 2 if both else 1))
 
@@ -148,8 +161,9 @@ def rank_program(g, core, T, topo):
         run("dve", lambda: g.vector.tensor_copy(out[3], a[3]), [a], [out], price(out, a, half(out, a)))
 
     def act(out, a, f, bias=0.0, scale=1.0):
-        run("act", lambda: g.scalar.activation(out[3], a[3], f, bias=bias, scale=scale), [a], [out],
-            price(out, a, 1, 1400 if f in (fn.Ln, fn.Exp) and out[1] == 0 else 0))
+        col = [bias] if isinstance(bias, tuple) else []
+        run("act", lambda: g.scalar.activation(out[3], a[3], f, bias=bias[3] if col else bias, scale=scale), [a] + col, [out],
+            price(out, a, 1, 1450 if f in (fn.Ln, fn.Exp) and out[1] == 0 else 50))
 
     def act3(out, a, f, bias=0.0, scale=1.0):
         for k in range(0, W, 512):
@@ -401,13 +415,46 @@ def rank_program(g, core, T, topo):
                 part = [z for z in part if z in take] + [z for z in part if z not in take]
                 return o[:a] + (part[::-1] if back else part) + o[b + 1:]
 
+            def anew(case, part, fr, rank, look):
+                cost, late = case
+                fin, done, why = fr[0][:3]
+                lastq, lastb = list(fr[0][3]), list(fr[0][4])
+                inside = set(part)
+                left = {i: sum(j in inside for j in pred[i]) for i in part}
+                ready = {}
+
+                def admit(i):
+                    ready[i] = max([0.0] + [done[j] for j in hard[i]] + [fin[j] for j in soft[i]])
+                for i in part:
+                    if not left[i]:
+                        admit(i)
+                made = []
+                while ready:
+                    at = {i: max([t, fin[lastq[qn[i]]]] + [done[lastb[z]] for z in bn[i] if qn[lastb[z]] != qn[i]]) for i, t in ready.items()}
+                    k = min(at, key=at.get)
+                    i = max((z for z in at if qn[z] == qn[k] and at[z] <= at[k] + look), key=rank.get)
+                    del ready[i]
+                    made.append(i)
+                    fin[i] = at[i] + cost[i]
+                    done[i] = fin[i] + late[i]
+                    lastq[qn[i]] = i
+                    for z in bn[i]:
+                        lastb[z] = i
+                    for j in succ[i]:
+                        if j in inside:
+                            left[j] -= 1
+                            if not left[j]:
+                                admit(j)
+                return made
+
             def by_time(case, o):
                 state = [0.0] * (m + 1), [0.0] * (m + 1), [m] * (m + 1), [m] * len(Q), [m] * len(names)
                 lay(case, o, state)
                 return sorted(o, key=lambda i: state[0][i] - case[0][i])
 
-            order, span = top[1], OPT["span"]
+            order = top[1]
             for turn in range(OPT["turns"]):
+                span = OPT["span"] + (turn % 3) * OPT["wider"]
                 for a in range(-int(rnd() * span / 2), m - 10, span // 2):
                     order = by_time(cases[0], order)
                     a, b = max(a, 0), min(a + span, m)
@@ -415,6 +462,20 @@ def rank_program(g, core, T, topo):
                     part = order[a:b]
                     laid = [weigh(c, part, f) for c, f in zip(cases, frames)]
                     best = sum(z[0] for z in laid)
+                    rank, was = {}, None
+                    for i in reversed(part):
+                        rank[i] = cases[0][0][i] + max([frames[0][1][i]] + [rank[j] + cases[0][1][i] for j in succ[i] if j in rank])
+                    for it in range(OPT["fresh"]):
+                        r = dict(rank)
+                        for z in range(1 + int(rnd() * 6)):
+                            r[part[int(rnd() * (b - a))]] += 3000 * (rnd() - 0.5)
+                        o = anew(cases[0], part, frames[0], r, 400 * rnd() ** 2)
+                        new = [weigh(c, o, f) for c, f in zip(cases, frames)]
+                        s = sum(z[0] for z in new)
+                        if was is None or s <= was:
+                            rank, was = r, s
+                            if s < best:
+                                best, part, laid = s, o, new
                     keep = (best, part, laid)
                     for it in range(OPT["moves"]):
                         pairs = laid[int(rnd() * len(cases))][1]
@@ -468,7 +529,7 @@ def rank_program(g, core, T, topo):
     dma("sp", S("q0s"), D("q0"))
     dma("sp", S("K1"), D("kap"))
     dma("sp", S("v0s"), D("v0"))
-    if OPT["dq1"] == "d":
+    if "d" in OPT["dq1"]:
         dma("sp", S("q0c"), D("q0"))
     dma("sp", S("K2", 0, V), D("kap", 0, V))
     dma("sp", S("aims", parts=8), ("aim", 0, W, T.aim[:]))
@@ -486,6 +547,8 @@ def rank_program(g, core, T, topo):
     ts(S("v15"), S("vv", 0, 144), 15, op.bitwise_and)
     cp(S("col", 0, 1), S("pm", 0, 1))
     ts(S("col", 1, 2), S("pm", 0, 1), 2.0, op.mult)
+    if OPT["oh"]:
+        ts(S("col", 4, 5), S("pm", 0, 1), -2.0, op.mult)
     ts(S("col", 2, 3), S("pm", 0, 1), -1.0, op.mult, 143.0, op.add)
     ts(S("U0"), S("v15"), 0.0, op.is_equal)
     ts(S("U1"), S("v15"), 1.0, op.is_equal, EPS, op.mult)
@@ -503,7 +566,7 @@ def rank_program(g, core, T, topo):
     act(S("IIb"), S("IIb"), fn.Relu, bias=1.0, scale=-1.0)
     act(S("IIf"), S("IIb"), fn.Copy)
     act(S("NIf"), S("IIb"), fn.Copy, scale=-1.0)
-    for name, w in (("NIb", -1.0), ("Lb", L), ("Zero", 0.0), ("N8", -8.0), ("Is", 1.0 / BIG)):
+    for name, w in (("NIb", -1.0), ("Lb", L), ("Zero", 0.0), ("N8", -8.0), ("Is", 1.0 / BIG), ("Js", -1.0 / BIG), ("Ibs", 1.0 / BIG)):
         act(S(name), S("IIb", 0, 128), fn.Copy, scale=w)
     act(S("B4"), S("Bm"), fn.Copy, scale=0.25)
     ts(S("col", 3, 4), S("pc", 0, 1), 15.0, op.mult)
@@ -513,7 +576,11 @@ def rank_program(g, core, T, topo):
     spots = [("PA", 0), ("PA", 512), ("PA", 1024), ("PC", 0)]
     for k, (bk, o) in enumerate(spots):
         mm([(S(bk, o + 96 * s, o + 96 * s + 96), S("R", 128 * (4 * k + s), 128 * (4 * k + s) + 128), S("curh"), True, True) for s in range(4)])
-        ts(S("OH", 384 * k, 384 * k + 384), S(bk, o, o + 384), S("col", 1, 2), op.is_equal)
+        if k < OPT["oh"]:
+            act(S(bk, o, o + 384), S(bk, o, o + 384), fn.Abs, bias=S("col", 4, 5))
+            act(S("OH", 384 * k, 384 * k + 384), S(bk, o, o + 384), fn.Relu, bias=1.0, scale=-1.0)
+        else:
+            ts(S("OH", 384 * k, 384 * k + 384), S(bk, o, o + 384), S("col", 1, 2), op.is_equal)
 
     def unpack(src, rest, o, lists):
         if lists:
@@ -528,8 +595,6 @@ def rank_program(g, core, T, topo):
         put(S("PB", a, b), "C01", S("OH", a, b))
         tt(S("X", a, b), S("PB", a, b), S("cons", a, b), op.mult)
         wrap2("PD", "Zh", "X", a, b)
-    for a, b in C3:
-        put(S("PA", a, b), "C23", S("OH", a, b))
     unpack(S("PD", 0, 96), S("PD", 96, 192), 0, "Ju")
 
     urgent(9000, shift, "PC", "IIb", "K1", V, False)
@@ -579,19 +644,34 @@ def rank_program(g, core, T, topo):
             act(S("HB", a, b), x, fn.Sign)
             mm([(y, S("IIb", 0, 128), S(dq, a, b), True, False), (y, S("IIb", 0, 128), S("HB", a, b), False, True)])
             act(S("FH", a, b), y, fn.Abs)
+        elif how == 3:
+            least = 2.0
+            act(S("HB", a, b), S(dq, a, b), fn.Sign)
+            put(x, "IIb", S("HB", a, b), False)
+            act(S("FH", a, b), x, fn.Abs)
         elif how == 1:
             tt(h, x, S(dq, a, b), op.mult)
             act(S("FH", a, b), h, fn.Sign)
         else:
             tt(S("HB", a, b), x, S(dq, a, b), op.mult)
             ts(S("FH", a, b), S("HB", a, b), 0.0, op.is_gt)
+        if k is None:
+            mm([(y, S("IIf", 0, 128), S(dk, a, b), True, False), (y, S("N8"), S(rk, a, b), False, False)])
+            put(y, "IIb", S("FH", a, b), False)
+            act(kh, y, fn.Relu, bias=-least)
+            return
         mm([(y, S("IIb", 0, 128), S(dk, a, b), True, False), (y, S("N8"), S(rk, a, b), False, False),
             (y, S("IIb", 0, 128), S("FH", a, b), False, True)])
         act(y, y, fn.Relu, bias=-least)
         tt(kh, y, S(k, a, b), op.mult)
 
-    for a, b in C3:
-        tt(S("X", a, b), S("PA", a, b), S("cons", a, b), op.mult)
+    def rows23(late):
+        for c, (a, b) in enumerate(C3):
+            if (OPT["x23"] >> c & 1) == late:
+                put(S("PA", a, b), "C23", S("OH", a, b))
+                tt(S("X", a, b), S("PA", a, b), S("cons", a, b), op.mult)
+
+    rows23(0)
     for c, (a, b) in enumerate(C3):
         if "d" in OPT["r0"][c::3]:
             act(S("A", a, b), S("q0s", a, b), fn.Identity, bias=-0.25)
@@ -612,12 +692,13 @@ def rank_program(g, core, T, topo):
     for a, b in C3:
         put(S("PB", a, b), "IIb", S("K1", a, b))
     choose(8.5, "dJ", "j1u", "o0k", False)
+    rows23(1)
     spread = len(calls) + 4
     partner("PB", "K1", "j1u", "DK1", "RK1", OPT["ra1"], CV)
     behind(spread, wrap, "PC", "Zh", "X", ((0, W),), 288)
     unpack(S("PC", 288, 384), S("PC", 384, 480), 192, None)
-    for a, b in CV:
-        if OPT["dq1"] == "d":
+    for c, (a, b) in enumerate(CV):
+        if OPT["dq1"][c] == "d":
             tt(S("DQ1", a, b), G("q0s", "j1u", a, b), S("q0c", a, b), op.subtract)
         else:
             y = S("PD", 0, 256) if a == V else S("PB", a, b)
@@ -645,9 +726,12 @@ def rank_program(g, core, T, topo):
             mm([(S(pa, a, b), S("B8", parts=8), S("aims", a, b, parts=8), True, True)])
             act(S("AM", a, b), S(pa, a, b), fn.Copy)
 
-    def newton():
+    def newton(part):
         for a, b in C3:
-            behind(len(calls) - 1, act, S("R0", a, b), S("K1", a, b), fn.Ln)
+            if part & 1:
+                behind(len(calls) - 1, act, S("R0", a, b), S("K1", a, b), fn.Ln)
+        if not part & 2:
+            return
         for a, b in C3:
             behind(len(calls) - 1, act, S("R0", a, b), S("R0", a, b), fn.Exp, 0.6931472, -1.0)
         act3("SQ", "R0", fn.Square, scale=0.5)
@@ -678,19 +762,30 @@ def rank_program(g, core, T, topo):
             return S("PD", 256, 512) if a == V else S(pb, a, b)
 
         fast = x == 1 and OPT["fast"]
+        gone = x == 1 and OPT["lead"] & 1
         for a, b in CV:
-            if a == V and fast:
+            if a == V and gone:
+                put(Y(a, b), "Lb", S("K2", W, W + 256))
+            elif a == V and fast:
                 put(X(a, b), "IIf", S("KS", a, b))
                 act(S("CQ", a, b), S(v0, a, b), fn.Copy)
-            else:
+            elif not (x == 1 and OPT["m7"] >> (a // 512) & 1):
                 put(X(a, b), big, S(v0, a, b), whole=b == V)
-        clear("PC")
-        shift("PC", ii, v0, V, False, start=False)
+        if not gone:
+            clear("PC")
+            shift("PC", ii, v0, V, False, start=False)
         for a, b in CV:
-            if a < V or not fast:
+            if a < V and x == 1 and OPT["m7"] >> (a // 512) & 1:
+                act(S(vg, a, b), G(v0, "j1u", a, b), fn.Copy)
+                tt(X(a, b), X(a, b), S(vg, a, b), op.subtract)
+            elif a < V or not fast:
                 differ(X(a, b), v0, "j1u", vg, nbig, a, b)
+        if x == 0 and OPT["lead"] & 1:
+            act(S("QV"), S("QB", V, W), fn.Copy)
         for c, (a, b) in enumerate(CV):
             how = 2 if OPT["h1"] >> (4 * x + c) & 1 else OPT["fa1"] >> x & 1
+            if a == V and gone:
+                continue
             if a == V and fast:
                 tt(S("tv"), G(v0, "j1u", a, b), S("CQ", a, b), op.subtract)
                 tt(X(a, b), X(a, b), S("tv"), op.mult)
@@ -699,6 +794,11 @@ def rank_program(g, core, T, topo):
                 else:
                     ts(X(a, b), X(a, b), -1.0, op.mult, 0.0, op.max)
                 tt(S("DL1", a, b), X(a, b), S("DQ1", a, b), op.mult)
+            elif OPT["ks"][c] in "kK" and (x == 1 or OPT["ks"][c] == "k"):
+                if x == 0:
+                    put(Y(a, b), "IIb", S("DK1", a, b))
+                    tt(S("KS", a, b), Y(a, b), S("K1", a, b), op.mult)
+                hits(X(a, b), Y(a, b), "DQ1", "KS", "RK1", None, S("KH1", a, b), how if how == 2 else OPT["kf"], a, b, S("HB", a, b))
             elif x == 1 and OPT["ks"][c] != "-":
                 act(Y(a, b), X(a, b), fn.Sign)
                 tt(Y(a, b), Y(a, b), S("KS", a, b), op.mult)
@@ -710,6 +810,8 @@ def rank_program(g, core, T, topo):
                     tt(S("DL1", a, b), X(a, b), S("KH1", a, b), op.mult)
                 shift("PC", "NIf", "DL1", V, False, start=False)
                 act(S(("t1", "t3")[x]), S("PC", 0, 256), fn.Copy)
+                if x == 0:
+                    newton(OPT["ln"])
                 send(1 + 2 * x, nxt, S(("t1", "t3")[x]), S(v1, V, W))
                 if fast:
                     act(X(a, b), S("tv"), fn.Sign)
@@ -739,13 +841,17 @@ def rank_program(g, core, T, topo):
                     act(S("CQ", a, b), S("q1", a, b), fn.Copy)
         if x == 0:
             lists2()
-            if "d" in OPT["p4"]:
-                aims(pa)
+            aims(pa)
         tt(S("q1", V, W), Y(V, W), S(v1, V, W), op.add)
-        tt(S("CQ", V, W), Y(V, W), S(v1, V, W), op.add)
+        act(S("CQ", V, W), S("q1", V, W), fn.Copy)
 
         if x == 0:
-            act3("DQ1", "DQ1", fn.Sign)
+            for c, (a, b) in enumerate(CV):
+                if (OPT["ks"][c] in "35" or OPT["h1"] >> (4 + c) & 1) and OPT["dq1"][c] == "d":
+                    act(S("DQ1", a, b), S("DQ1", a, b), fn.Sign)
+                if OPT["ks"][c] == "K":
+                    put(S(pa, a, b), "IIb", S("DK1", a, b))
+                    tt(S("KS", a, b), S(pa, a, b), S("K1", a, b), op.mult)
             signed([(a, b) for c, (a, b) in enumerate(CV) if OPT["ks"][c] == "3"], lambda a, b: S(pa, a, b))
         elif OPT["nw"] == 1:
             newton2("PC")
@@ -764,16 +870,42 @@ def rank_program(g, core, T, topo):
         for a, b in C3:
             put(S(pb, a, b), "IIb", S("K2", a, b))
         choose(0.25, "dJ2", "j2u", None, True)
-        for a, b in CL:
-            act(S("DQ2", a, b), G("DD", "selu", a, b), fn.Copy)
-            put(S(pa, a, b), "NIb", S("DQ2", a, b))
+        ahead = OPT["lead"] & 2
+        C4, first = CV if ahead else CL, len(calls)
+        for a, b in C4:
+            act(S("DQ2", a, b), G("DD", "selu", a, b), fn.Sign)
             tt(S("E2", a, b), G(v1, "j2u", a, b), S("CP", a, b), op.subtract)
-        partner(pb, "K2", "j2u", "DK2", "RK2", OPT["ra2"], CL)
-        for c, (a, b) in enumerate(CL):
+        partner(pb, "K2", "j2u", "DK2", "RK2", OPT["ra2"], C4)
+
+        def back():
+            tt(S(pb, V, W), S(pb, V, W), S("DA", V, W), op.mult)
+            act(S("tv"), S(pb, V, W), fn.Copy)
+            shift("PC", "IIf", "tv", 0, True, start=False)
+            shift("PC", "IIf", "A", V, True, start=False)
+            act(S(("t2", "t4")[x]), S("PC", 0, 256), fn.Copy)
+            send(2 + 2 * x, prv, S(("t2", "t4")[x]), S(a2, V, W))
+            tt(S(y2, V, W), S(pb, V, W), S("E2", V, W), op.mult)
+            if x == 1:
+                mm([(S("PD", 256, 384), S("IIf", 16, 144), S("Y2a", V, H), True, False),
+                    (S("PD", 256, 384), S("IIf", 16, 144), S("Y2b", V, H), False, True),
+                    (S("PD", 384, 512), S("IIf", 64, 192), S("Y2a", H, W), True, False),
+                    (S("PD", 384, 512), S("IIf", 64, 192), S("Y2b", H, W), False, True)])
+                act(S("t5"), S("PD", 256, 512), fn.Copy)
+                send(5, prv, S("t5"), S("YL"))
+
+        mine = len(calls)
+        if ahead:
+            act(S("VG", 0, 256), G(v1, "j2u", V, W), fn.Copy)
+            act(S("VG", 256, 512), G("q1", "j2u", V, W), fn.Copy)
+            act(S("GA"), G("AM", "j2u", V, W), fn.Copy)
+            put(S("PD", 0, 256), "Is", S("VG", 0, 256))
+        for c, (a, b) in enumerate(C4):
             xx, yy, how = S(pa, a, b), S(pb, a, b), OPT["p4"][c]
+            put(xx, "NIb", S("DQ2", a, b), whole=b == V)
             am = (xx, S("B8s", parts=8), S("aims", a, b, parts=8))
-            hits(xx, yy, "E2", "DK2", "RK2", "K2", yy, OPT["fa2"] >> c & 1, a, b, xx)
+            hits(xx, yy, "E2", "DK2", "RK2", "K2", yy, 3 if OPT["h2"] >> c & 1 else OPT["fa2"] >> c & 1, a, b, xx)
             unit = 1.0
+            fine[0] = OPT["fine4"] >> c & 1
             if how == "f":
                 put(xx, "Is", S(v1, a, b))
                 tt(S("Wn", a, b), yy, S("E2", a, b), op.mult)
@@ -788,47 +920,59 @@ def rank_program(g, core, T, topo):
                     tt(xx, xx, S("q1", a, b), op.add)
                     tt(xx, xx, S("AM", a, b), op.add)
                     unit = 1.0 / BIG
+            fine[0] = 0
             act(S("A", a, b), xx, fn.Copy, scale=unit)
-            if OPT["p5"][c] == "d":
+            if a == V:
+                z = S("PD", 0, 256)
+                mm([(z, S("Js"), S("Wn", V, W), False, False), (z, S("Is"), S("VG", 256, 512), False, False), (z, S("Ibs"), S("GA"), False, True)])
+                clear("PC")
+                shift("PC", "IIf", "A", V, True, start=False)
+                tt(S("DA", V, W), z, S("A", V, W), op.subtract)
+                back()
+                for i in range(first, len(calls)):
+                    if i >= mine or calls[i][3][0][1:3] == (V, W):
+                        hints.append((i, i + 1, OPT["up2"]))
+            elif OPT["p5"][(a // 512 + 1) % 3] == "d":
                 act(S("CQ", a, b), xx, fn.Copy, scale=unit)
             else:
-                if a == 1024:
+                if b == W:
                     act(S("CQ", V, W), S(pa, V, W), fn.Copy, scale=unit)
                 if unit != 1.0:
                     act(xx, xx, fn.Copy, scale=unit)
 
-        clear("PC")
-        shift("PC", "IIf", "A", V, True, start=False)
-        for a, b in CV:
+        if not ahead:
+            clear("PC")
+            shift("PC", "IIf", "A", V, True, start=False)
+        for a, b in CV[1:] if ahead else CV:
             xx, yy = S(pa, a, b), S(pb, a, b)
             if a == V or OPT["p5"][(a // 512 + 1) % 3] == "d":
                 tt(S("DA", a, b), G("A", "j2u", a, b), S("CQ", a, b), op.subtract)
             else:
                 act(S("VG", a, b), G("A", "j2u", a, b), fn.Copy)
                 tt(S("DA", a, b), S("VG", a, b), xx, op.subtract)
+            if x == 0 and a == 0:
+                newton(3 - OPT["ln"])
             if a == V:
-                tt(S("tv"), yy, S("DA", a, b), op.mult)
-                shift("PC", "IIf", "tv", 0, True, start=False)
-                shift("PC", "IIf", "A", V, True, start=False)
-                act(S(("t2", "t4")[x]), S("PC", 0, 256), fn.Copy)
-                if x == 0:
-                    newton()
-                send(2 + 2 * x, prv, S(("t2", "t4")[x]), S(a2, V, W))
-                tt(S(y2, a, b), S("tv"), S("E2", a, b), op.mult)
+                back()
             else:
                 tt(yy, yy, S("DA", a, b), op.mult)
-                tt(xx, yy, S("A", a, b), op.add)
-                tt(S(a2, a, b), xx, S("A", a, b), op.add)
+                if OPT["b5"] >> (a // 512) & 1:
+                    put(xx, "IIf", S("A", a, b))
+                    act(S("DA", a, b), yy, fn.Copy)
+                    mm([(xx, S("IIf", 0, 128), S(z, a, b), False, True) for z in ("DA", "A")])
+                    act(S(a2, a, b), xx, fn.Copy)
+                else:
+                    fine[0] = OPT["fine5"]
+                    tt(xx, yy, S("A", a, b), op.add)
+                    if OPT["m6"] >> (3 * x + a // 512) & 1:
+                        tt(xx, xx, S("A", a, b), op.add)
+                        act(S(a2, a, b), xx, fn.Copy)
+                    else:
+                        tt(S(a2, a, b), xx, S("A", a, b), op.add)
+                    fine[0] = 0
                 tt(S(y2, a, b), yy, S("E2", a, b), op.mult)
-            if a == V and x == 1:
-                mm([(S("PD", 256, 384), S("IIf", 16, 144), S("Y2a", V, H), True, False),
-                    (S("PD", 256, 384), S("IIf", 16, 144), S("Y2b", V, H), False, True),
-                    (S("PD", 384, 512), S("IIf", 64, 192), S("Y2a", H, W), True, False),
-                    (S("PD", 384, 512), S("IIf", 64, 192), S("Y2b", H, W), False, True)])
-                act(S("t5"), S("PD", 256, 512), fn.Copy)
-                send(5, prv, S("t5"), S("YL"))
         if 2 * x == OPT["nw"]:
-            newton2(("PD", "PC")[x])
+            newton2("PC")
         if x == 0:
             signed([(a, b) for c, (a, b) in enumerate(CV) if OPT["ks"][c] == "5"], lambda a, b: S("PD", 0, b - a))
         dma("pool", S("ZZ", 0, V if x == 0 else 512), S(y2, 0, V if x == 0 else 512), True)
@@ -843,7 +987,7 @@ def rank_program(g, core, T, topo):
                 return S(pa, a, b)
             return S("PC") if a < 1024 else S("PD", a - 1024, b - 1024)
         for a, b in chunks:
-            if a < V:
+            if a < V and not OPT["m6"] >> (3 * x + a // 512) & 1:
                 put(S(pa, a, b), "IIf", S(a2, a, b), whole=b == V)
         if x == 1:
             put(S("PC"), "IIf", S("ZZ", 512, 1024))
@@ -851,28 +995,65 @@ def rank_program(g, core, T, topo):
             put(S("PD"), "IIf", S("ZZ", 1024, W))
             put(S("PD", 0, 256), "IIf", S("Y2b", 1024, V), False)
             put(S("PD", 256, 512), "IIf", S("YL"), False)
+        if x == 0 and OPT["lead"] & 1:
+            chunks, first = chunks[:3], len(calls)
+            xx, yy, zz = S("PD", 0, 256), S("PD", 256, 512), S(pb, V, W)
+            act(S("VG", V, W), G(a2, "j1u", V, W), fn.Copy)
+            put(xx, "IIf", S(a2, V, W))
+            put(xx, "NIf", S("VG", V, W), False)
+            tt(yy, xx, S("KH1", V, W), op.mult)
+            tt(zz, yy, S("VG", V, W), op.add)
+            tt(yy, yy, S(a2, V, W), op.subtract)
+            for z in (zz, yy):
+                ts(z, z, 0.1875, op.min, -0.1875, op.max)
+            tt(zz, S("QV"), zz, op.subtract)
+            tt(S("V0p", V, W), yy, S(v0, V, W), op.add)
+            tt(S("Y1", V, W), xx, S("DL1", V, W), op.mult)
+            tt(zz, zz, S("V0p", V, W), op.subtract)
+            tt(yy, zz, S("KS", V, W), op.mult)
+            act(yy, yy, fn.Relu, scale=-1.0)
+            tt(S("DL1", V, W), yy, S("DQ1", V, W), op.mult)
+            clear("PC")
+            shift("PC", "IIf", "V0p", V, False, start=False)
+            shift("PC", "NIf", "DL1", V, False, start=False)
+            act(S("t3"), S("PC", 0, 256), fn.Copy)
+            send(3, nxt, S("t3"), S("V1b", V, W))
+            hints.append((first, len(calls), OPT["up1"]))
+            act(yy, yy, fn.Sign)
+            tt(yy, yy, S("KS", V, W), op.mult)
+            act(S("KH1", V, W), yy, fn.Abs)
         for a, b in chunks:
             if a == V:
                 act(S("VG", a, b), G(a2, "j1u", a, b), fn.Copy)
                 mm([(S(pa, a, b), S("IIf", 0, 128), S(a2, a, b), True, False), (S(pa, a, b), S("NIf", 0, 128), S("VG", a, b), False, True)])
+            elif OPT["m6"] >> (3 * x + a // 512) & 1:
+                act(S("VG", a, b), G(a2, "j1u", a, b), fn.Copy)
+                tt(S(pa, a, b), S(pa, a, b), S("VG", a, b), op.subtract)
             else:
                 differ(S(pa, a, b), a2, "j1u", "VG", "NIf", a, b)
         for a, b in chunks:
             xx, yy = S(pa, a, b), S(pb, a, b)
             tt(yy, xx, S("KH1", a, b), op.mult)
-            tt(xx if x == 1 and a == 0 else S("Y1", a, b), xx, S("DL1", a, b), op.mult)
+            tt(xx if x == 1 and a == 0 and OPT["z0"] else S("Y1", a, b), xx, S("DL1", a, b), op.mult)
             tt(yy, yy, S(a2, a, b), op.subtract)
             if last:
                 ts(S(vout, a, b), yy, 0.1875, op.min, -0.1875, op.max)
                 dma("pool", D("yv", a, b), S(vout, a, b), True)
             else:
                 ts(yy, yy, 0.1875, op.min, -0.1875, op.max)
-                tt(S(vout, a, b), yy, S(v0, a, b), op.add)
+                if x == 0 and a < V and OPT["m7"] >> (a // 512) & 1:
+                    tt(yy, yy, S(v0, a, b), op.add)
+                    act(S(vout, a, b), yy, fn.Copy)
+                else:
+                    tt(S(vout, a, b), yy, S(v0, a, b), op.add)
             if x == 1:
                 if not last:
                     dma("sp", D("yv", a, b), S(vout, a, b))
                 bank = spot(a, b)
-                if a == 0:
+                if a == 0 and not OPT["z0"]:
+                    put(bank, "IIf", S("Y1", a, b))
+                    put(bank, "IIf", S("ZZ", a, b), False)
+                elif a == 0:
                     tt(bank, bank, S("ZZ", a, b), op.add)
                 else:
                     put(bank, "IIf", S("Y1", a, b), False)

from concourse.mybir import AluOpType, ActivationFunctionType

W, V = 1536, 1280
H = V + 128
L = 16.0
BIG = 16 * L
EPS = 2.0 ** -12
WHOLE = 1.5 * 2.0 ** 23
TWO = 2.0 ** 24
SIXTEEN = 1.5 * 2.0 ** 27
NEAR = 0x150aaaa / 2.0 ** 24

OPT = {"r0": "daadaa", "fast": 1, "q1pe": 0, "ra1": 15, "ra2": 0, "fa1": 3, "fa2": 7, "h1": 0, "dq1": "dddd", "x23": 0, "p5": "ddm", "v1pe": 0, "p4": "fadd",
       "b5": 0, "fine5": 0, "z0": 1, "oh": 1, "m6": 0x24, "m7": 4,
       "cqdma": 3, "ga2": 0, "ta2": 3, "nw": 1, "yvacc": 1, "c6": 1, "turns": 9, "span": 80, "moves": 1200, "warm": 1500, "free": 0.3, "soon": 1.0, "hint": 1.0, "seed": 12345, "ks": "3333", "fine4": 12, "h2": 15, "kf": 1, "ln": 1, "wider": 20, "lead": 3, "up1": 2500, "up2": 0, "fresh": 100, "trans": 1, "each": 0, "look": 60, "heat": 300, "tries": 0}
CASES = [(1.6, 0.46, 200, 3600), (1.3, 0.35, 145, 2700), (1.5, 0.6, 220, 4800)]
KEPT = {}

F, B, HF, I, U = "float32", "bfloat16", "float16", "int32", "uint16"
SAME = {"DA": "DD", "DQ2": "QB", "FH": "F0", "HB": "F1", "RK2": "AB0", "DK2": "AB1"}
SCRATCH = {}
for _n in ("V1a", "V1b", "q1", "CQ", "Wn", "io2", "A", "A2a", "A2b", "VG", "KH1", "E2", "DL1",
           "Y2a", "Y2b", "V0p", "ZZ", "R0", "RR", "Y1", "CP", "KS", "SQ"):
    SCRATCH[_n] = ("sbuf", [128, W], F)
for _n in ("q0s", "q0c", "v0s", "K1", "OH", "F0", "F1", "QB", "AM", "AB0", "AB1", "DK1", "RK1", "DQ1"):
    SCRATCH[_n] = ("sbuf", [128, W], B)
SCRATCH.update({
    "DD": ("sbuf", [128, 2 * W], F),
    "cons": ("sbuf", [128, W], I), "X": ("sbuf", [128, W], HF), "K2": ("sbuf", [128, W + 256], B),
    "aims": ("sbuf", [128, W], B), "curs": ("sbuf", [128, 96], I), "curh": ("sbuf", [128, 96], HF),
    "R": ("sbuf", [128, 2048], HF), "io3": ("sbuf", [128, 128], B), "vv": ("sbuf", [128, 256], I),
    "v15": ("sbuf", [128, 144], I), "pc": ("sbuf", [128, 4], I), "pm": ("sbuf", [128, 4], I),
    "col": ("sbuf", [128, 16], F), "Bm": ("sbuf", [128, 128], B), "U0": ("sbuf", [128, 144], B), "U1": ("sbuf", [128, 144], B),
    "U2": ("sbuf", [128, 144], B), "C01": ("sbuf", [128, 128], B), "C23": ("sbuf", [128, 128], B),
    "Zb": ("sbuf", [128, 144], B), "Zh": ("sbuf", [128, 144], HF), "IIf": ("sbuf", [128, 256], F), "IIb": ("sbuf", [128, 256], B),
    "NIb": ("sbuf", [128, 128], B), "NIf": ("sbuf", [128, 256], F), "Lb": ("sbuf", [128, 128], B), "Zero": ("sbuf", [128, 128], B),
    "Js": ("sbuf", [128, 128], F), "Ibs": ("sbuf", [128, 128], B), "GA": ("sbuf", [128, 256], B), "QV": ("sbuf", [128, 256], B),
    "Is": ("sbuf", [128, 128], F), "B8s": ("sbuf", [128, 128], B),
    "B8": ("sbuf", [128, 128], B), "B4": ("sbuf", [128, 128], B), "N8": ("sbuf", [128, 128], B),
    "iwr": ("sbuf", [128, 96], F), "iw": ("sbuf", [128, 96], F), "J": ("sbuf", [128, 384], F),
    "Ju": ("sbuf", [128, 192], U), "J2u": ("sbuf", [128, 192], U), "dJ": ("sbuf", [128, 192], F), "dJ2": ("sbuf", [128, 192], F),
    "o0k": ("sbuf", [128, 96], F), "s3": ("sbuf", [128, 96], F), "selu": ("sbuf", [128, 96], U),
    "s4": ("sbuf", [128, 96], F), "s5": ("sbuf", [128, 192], F), "jf": ("sbuf", [128, 96], F),
    "jh": ("sbuf", [128, 96], HF), "j1u": ("sbuf", [128, 96], U), "j2u": ("sbuf", [128, 96], U),
    "tv": ("sbuf", [128, 256], F), "YL": ("sbuf", [128, 256], F),
    "t0": ("sbuf", [128, 512], B), "t1": ("sbuf", [128, 256], F), "t2": ("sbuf", [128, 256], F),
    "t3": ("sbuf", [128, 256], F), "t4": ("sbuf", [128, 256], F), "t5": ("sbuf", [128, 256], F),
    "PA": ("psum", [128, W], F), "PB": ("psum", [128, W], F), "PC": ("psum", [128, 512], F), "PD": ("psum", [128, 512], F),
})
SEMAPHORES = ["pe", "dve", "act", "pool", "sent"] + ["d%d" % _i for _i in range(40)] + ["r%d" % _i for _i in range(6)]


def rank_program(g, core, T, topo):
    rank = T.rank_of(core)
    if rank is None:
        return
    op, fn = AluOpType, ActivationFunctionType
    n = len(T.cores)
    nxt, prv = T.cores[(rank + 1) % n], T.cores[(rank - 1) % n]
    Q = {"pe": g.tensor, "dve": g.vector, "act": g.scalar, "pool": g, "sp": g.sync}
    count = {"pe": 0, "dve": 0, "act": 0, "pool": 0, "dma": 0, "sent": 0, "waits": 0}
    KEPT["count"] = count
    seen, known = {q: {} for q in Q}, {}
    hist = {}
    dmas = []
    opened = {}

    def S(name, a=0, b=None, step=1, parts=128):
        name = SAME.get(name, name)
        b = T[name].shape[1] if b is None else b
        ap = T[name][0:parts, a:b:step] if step > 1 else T[name][0:parts, a:b]
        return (name, a, b, ap)

    def G(win, off, a, b, o=0):
        w = T[win].shape[1]
        return (win, 0, w, T[win][:, 0:w].indirect(T[off][:, o + a // 16:o + b // 16]), (off, o + a // 16, o + b // 16, None))

    def deps(q, reads, writes):
        need = {}
        for xs, wr in ((reads, False), (writes, True)):
            for x in xs:
                ps = SCRATCH.get(x[0], ("",))[0] == "psum"
                for lo, hi, q2, tok, w2 in hist.get(x[0], []):
                    if q == "pe" and q2 == "pe":
                        continue
                    if ps and q2 != q:
                        hit = lo // 512 <= (x[2] - 1) // 512 and x[1] // 512 <= (hi - 1) // 512
                    else:
                        hit = (wr or w2) and lo < x[2] and x[1] < hi
                    if hit:
                        need[tok[0]] = max(need.get(tok[0], 0), tok[1])
        for s, c in need.items():
            if seen[q].get(s, 0) < c and not any(known.get(z, {}).get(s, 0) >= c for z in need.items()):
                Q[q].wait_ge(T.sem[s], c)
                count["waits"] += 1
        for z in need.items():
            for s, c in list(known.get(z, {}).items()) + [z]:
                seen[q][s] = max(seen[q].get(s, 0), c)

    def note(q, reads, writes, tok):
        if q in seen and OPT["trans"]:
            known[tok] = dict(seen[q])
        for x in writes:
            hist[x[0]] = [h for h in hist.get(x[0], []) if not (x[1] <= h[0] and h[1] <= x[2])]
        for xs, wr in ((reads, False), (writes, True)):
            for x in xs:
                hist.setdefault(x[0], []).append((x[1], x[2], q, tok, wr))

    calls = []

    fine = [0]
    gates, hints = [], []

    def urgent(up, f, *args):
        a = len(calls)
        f(*args)
        hints.append((a, len(calls), up * OPT["hint"]))

    def behind(j, f, *args):
        gates.append((len(calls), j))
        f(*args)

    def run(q, make, reads, writes, cost):
        reads = list(reads) + [x[4] for x in reads if len(x) > 4]

        def emit():
            deps(q, reads, writes)
            count[q] += 1
            make().then_inc(T.sem[q], 1)
            note(q, reads, writes, (q, count[q]))
        calls.append((q, emit, reads, writes, cost, "lat"))

    def size(x):
        return int(SCRATCH[x[0]][2][-2:]) // 8 if x[0] in SCRATCH else 4

    def price(out, a, m, more=0):
        if len(a) > 4:
            return (50, (out[2] - out[1]) * 0.83, 0)
        return (max(64, (out[2] - out[1]) * m) * 0.83 + more + OPT["each"], 0, 0)

    def half(out, a):
        return 0.5 if size(out) == 2 and size(a) == 2 else 1

    def tt(out, a, b, o):
        if fine[0] and out[2] - out[1] == 512 and len(a) == 4:
            for k in (0, 256):
                tt(*[S(x[0], x[1] + k, x[1] + k + 256) for x in (out, a, b)], o)
            return
        both = SCRATCH[a[0]][0] == SCRATCH[b[0]][0]
        run("dve", lambda: g.vector.tensor_tensor(out[3], a[3], b[3], o), [a, b], [out], price(out, a, 2 if both else 1))

    def ts(out, a, s1, o0, s2=None, o1=None):
        cols = [s for s in (s1, s2) if isinstance(s, tuple)]
        x1, x2 = [s[3] if isinstance(s, tuple) else s for s in (s1, s2)]
        if o1 is None:
            run("dve", lambda: g.vector.tensor_scalar(out[3], a[3], x1, None, o0), [a] + cols, [out], price(out, a, half(out, a)))
        else:
            run("dve", lambda: g.vector.tensor_scalar(out[3], a[3], x1, x2, o0, o1), [a] + cols, [out], price(out, a, half(out, a)))

    def cp(out, a):
        run("dve", lambda: g.vector.tensor_copy(out[3], a[3]), [a], [out], price(out, a, half(out, a)))

    def act(out, a, f, bias=0.0, scale=1.0):
        col = [bias] if isinstance(bias, tuple) else []
        run("act", lambda: g.scalar.activation(out[3], a[3], f, bias=bias[3] if col else bias, scale=scale), [a] + col, [out],
            price(out, a, 1, 1450 if f in (fn.Ln, fn.Exp) and out[1] == 0 else 50))

    def act3(out, a, f, bias=0.0, scale=1.0):
        for k in range(0, W, 512):
            act(S(out, k, k + 512), S(a, k, k + 512), f, bias, scale)

    def mm(items, wide=None, more=()):
        items = [list(it) for it in items]
        for it in items:
            key = (it[0][0], it[0][1] // 512)
            if not it[3]:
                opened[key][4] = False
            opened[key] = it

        def make():
            for o, l, r, s0, s1 in items:
                ins = g.tensor.matmul(o[3], l[3], r[3], s0, s1)
            return ins
        cost = (0, 0, sum(max(64, wide or it[0][2] - it[0][1]) * (4 if size(it[2]) == 4 else 1) for it in items))
        run("pe", make, [x for it in items for x in it[1:3]], [it[0] for it in items] + list(more), cost)

    def iota(out, pat, base, cm, small=True):
        cost = (130 + 1.66 * (out[2] - out[1]), 0, 0)
        if small:
            run("pool", lambda: g.iota(out[3], pat, base, cm, allow_small_or_imprecise_dtypes=True), [], [out], cost)
        else:
            run("pool", lambda: g.iota(out[3], pat, base, cm), [], [out], cost)

    def dma(q, out, a, add=False):
        def emit():
            deps(q, [a], [out])
            s = "d%d" % count["dma"]
            count["dma"] += 1
            ins = g.dma_start(out[3], a[3], accum_op=op.add) if add else Q[q].dma_start(out[3], a[3])
            ins.then_inc(T.sem[s], 16)
            note("dma", [a], [out], (s, 16))
            dmas.append(s)
        calls.append((q, emit, [a], [out], (1000 if add else 60, 0, 0), 2000 + (out[2] - out[1]) * size(out) * (0.5 if add else 0.25)))

    def D(name, a=0, b=W):
        return (name, a, b, T[name][:, a:b])

    def send(k, dst, src, land):
        def emit():
            deps("pool", [src], [])
            eng = topo.engines(core, dst)[:8]
            rid, pid, _ = topo.addr(dst)
            g.remote_dma(land[3], src[3], T.sem["r%d" % k], T.sem.sent, pid, rid, sum(1 << e for e in eng))
            count["sent"] += len(eng)
            other = prv if dst == nxt else nxt
            note("dma", [], [land], ("r%d" % k, len(topo.engines(other, core)[:8])))
        calls.append(("pool", emit, [src], [land], (500, 0, 0), "rem"))

    def banks(x):
        return [(x[0], k) for k in range(x[1] // 512, (x[2] - 1) // 512 + 1)] if SCRATCH.get(x[0], ("",))[0] == "psum" else []

    def issue():
        m = len(calls)
        pred = [set() for _ in range(m)]
        log, lastpe = {}, {}
        for i, (q, _, reads, writes, _, _) in enumerate(calls):
            for xs, wr in ((reads, False), (writes, True)):
                for x in xs:
                    for lo, hi, j, w2 in log.get(x[0], []):
                        if (wr or w2) and lo < x[2] and x[1] < hi and j != i:
                            pred[i].add(j)
            for x in writes:
                log[x[0]] = [h for h in log.get(x[0], []) if not (x[1] <= h[0] and h[1] <= x[2])]
                if q == "pe":
                    for bk in banks(x):
                        if lastpe.get(bk, i) != i:
                            pred[i].add(lastpe[bk])
                        lastpe[bk] = i
            for xs, wr in ((reads, False), (writes, True)):
                for x in xs:
                    log.setdefault(x[0], []).append((x[1], x[2], i, wr))
        for i, j in gates:
            pred[i].add(j)
        succ = [[] for _ in range(m)]
        for i in range(m):
            for j in pred[i]:
                succ[j].append(i)
        qs = [c[0] for c in calls]
        bk = [list(set(b for x in c[2] + c[3] for b in banks(x))) for c in calls]
        cases = []
        for gat, pe, lat, rem in CASES:
            cases.append(([c[4][0] + c[4][1] * gat + c[4][2] * pe for c in calls], [{"lat": lat, "rem": rem}.get(c[5], c[5]) for c in calls]))

        def walk(case, order=None, rank_of=None):
            cost, late = case
            left = [len(p) for p in pred]
            at = [0.0] * m
            free = {q: 0.0 for q in Q}
            held = {}
            ready = {q: [i for i in range(m) if not left[i] and qs[i] == q] for q in Q}
            made, end = [], 0.0

            def start(i, q):
                t = max(at[i], free[q])
                for b in bk[i]:
                    if b in held and held[b][0] != q and held[b][1] > t:
                        t = held[b][1]
                return t
            for step in range(m):
                if order:
                    i = order[step]
                    q = qs[i]
                    t = start(i, q)
                else:
                    t0 = 1e18
                    for z in Q:
                        if ready[z] and free[z] < t0:
                            ts0 = [(start(i, z), i) for i in ready[z]]
                            t1 = min(ts0)[0]
                            if t1 < t0:
                                t0, q, pick = t1, z, ts0
                    t, i = max((z for z in pick if z[0] <= t0 + OPT["look"]), key=lambda z: rank_of[z[1]])
                    ready[q].remove(i)
                    made.append(i)
                free[q] = t + cost[i]
                done = free[q] + late[i]
                end = max(end, done)
                for b in bk[i]:
                    held[b] = (q, done)
                for j in succ[i]:
                    d = free[q] if q == "pe" and qs[j] == "pe" else done
                    if d > at[j]:
                        at[j] = d
                    left[j] -= 1
                    if not left[j] and not order:
                        ready[qs[j]].append(j)
            return made, end

        if "order" not in KEPT:
            rest = [0.0] * m
            for i in range(m - 1, -1, -1):
                rest[i] = cases[0][0][i] + cases[0][1][i] + max([rest[j] for j in succ[i]] + [0.0])
            for a, b, up in hints:
                for i in range(a, b):
                    rest[i] += up
            seed = [OPT["seed"]]

            def rnd():
                seed[0] = (seed[0] * 1103515245 + 12345) % 2 ** 31
                return seed[0] / 2.0 ** 31

            def score(r):
                o, e = walk(cases[0], rank_of=r)
                return e + sum(walk(c, o)[1] for c in cases[1:]), o
            best, order = score(rest)
            top = (best, order)
            for it in range(OPT["tries"]):
                r = list(rest)
                k = int(rnd() * m)
                amp = 300 + 2500 * rnd() ** 2
                if rnd() < 0.5:
                    for i in order[k:k + 2 + int(rnd() * 14)]:
                        r[i] += amp * (rnd() - 0.5)
                else:
                    up, c = amp * (rnd() - 0.5) * 2, calls[order[k]][3][0][1] // 512
                    for i in order[k:k + 5 + int(rnd() * 50)]:
                        if calls[i][3][0][1] // 512 == c:
                            r[i] += up
                s, o = score(r)
                if s <= best + OPT["heat"] * (1 - it / OPT["tries"]) ** 2 * rnd() ** 3:
                    best, order, rest = s, o, r
                    if s < top[0]:
                        top = (s, o)
            qn = [list(Q).index(q) for q in qs]
            names = sorted(set(b for x in bk for b in x))
            bn = [[names.index(b) for b in x] for x in bk]
            soft = [[j for j in pred[i] if qs[i] == "pe" and qs[j] == "pe"] for i in range(m)]
            hard = [[j for j in pred[i] if j not in soft[i]] for i in range(m)]

            qn.append(-1)

            def frame(case, o, a, b):
                cost, late = case
                state = [0.0] * (m + 1), [0.0] * (m + 1), [m] * (m + 1), [m] * len(Q), [m] * len(names)
                lay(case, o[:a], state)
                tail, nextq, nextb = [0.0] * (m + 1), [m] * len(Q), [m] * len(names)
                for i in reversed(o[b:]):
                    t = max([late[i], tail[nextq[qn[i]]]] + [tail[j] + (0 if i in soft[j] else late[i]) for j in succ[i]]
                            + [tail[nextb[z]] + late[i] for z in bn[i] if qn[nextb[z]] != qn[i]])
                    tail[i] = t + cost[i]
                    nextq[qn[i]] = i
                    for z in bn[i]:
                        nextb[z] = i
                after = [max([late[i]] + [tail[j] + (0 if i in soft[j] else late[i]) for j in succ[i]]) for i in range(m)]
                least = max([0.0] + [state[0][i] + after[i] for i in o[:a]])
                return state, after, tail, nextq, nextb, least

            def weigh(case, part, fr):
                state, after, tail, nextq, nextb, end = fr
                fin, done, why, lastq, lastb = state[0], state[1], state[2], list(state[3]), list(state[4])
                lay(case, part, (fin, done, why, lastq, lastb))
                last, total = m, 0.0
                for i in part:
                    total += fin[i]
                    if fin[i] + after[i] > end:
                        end, last = fin[i] + after[i], i
                for i, j in zip(lastq, nextq):
                    if fin[i] + tail[j] > end:
                        end, last = fin[i] + tail[j], i
                for i, j in zip(lastb, nextb):
                    if qn[i] != qn[j] and done[i] + tail[j] > end:
                        end, last = done[i] + tail[j], i
                pairs, inside = [], set(part)
                while last in inside:
                    if why[last] in inside and why[last] not in pred[last]:
                        pairs.append((last, why[last]))
                    last = why[last]
                return end + OPT["soon"] * total / m, pairs, end

            def lay(case, o, state):
                cost, late = case
                fin, done, why, lastq, lastb = state
                for i in o:
                    q = qn[i]
                    w = lastq[q]
                    t = fin[w]
                    for j in hard[i]:
                        if done[j] > t:
                            t, w = done[j], j
                    for j in soft[i]:
                        if fin[j] > t:
                            t, w = fin[j], j
                    for b in bn[i]:
                        j = lastb[b]
                        if done[j] > t and qn[j] != q:
                            t, w = done[j], j
                        lastb[b] = i
                    why[i] = w
                    lastq[q] = i
                    fin[i] = t = t + cost[i]
                    done[i] = t + late[i]

            def moved(o, i, j):
                a, b = o.index(j), o.index(i)
                part, link = o[a:b + 1], pred
                back = rnd() < 0.5
                if back:
                    part, link, i, j = part[::-1], succ, j, i
                take = {i}
                for z in reversed(part):
                    if z in take:
                        take.update(link[z])
                if j in take:
                    return None
                part = [z for z in part if z in take] + [z for z in part if z not in take]
                return o[:a] + (part[::-1] if back else part) + o[b + 1:]

            def anew(case, part, fr, rank, look):
                cost, late = case
                fin, done, why = fr[0][:3]
                lastq, lastb = list(fr[0][3]), list(fr[0][4])
                inside = set(part)
                left = {i: sum(j in inside for j in pred[i]) for i in part}
                ready = {}

                def admit(i):
                    ready[i] = max([0.0] + [done[j] for j in hard[i]] + [fin[j] for j in soft[i]])
                for i in part:
                    if not left[i]:
                        admit(i)
                made = []
                while ready:
                    at = {i: max([t, fin[lastq[qn[i]]]] + [done[lastb[z]] for z in bn[i] if qn[lastb[z]] != qn[i]]) for i, t in ready.items()}
                    k = min(at, key=at.get)
                    i = max((z for z in at if qn[z] == qn[k] and at[z] <= at[k] + look), key=rank.get)
                    del ready[i]
                    made.append(i)
                    fin[i] = at[i] + cost[i]
                    done[i] = fin[i] + late[i]
                    lastq[qn[i]] = i
                    for z in bn[i]:
                        lastb[z] = i
                    for j in succ[i]:
                        if j in inside:
                            left[j] -= 1
                            if not left[j]:
                                admit(j)
                return made

            def by_time(case, o):
                state = [0.0] * (m + 1), [0.0] * (m + 1), [m] * (m + 1), [m] * len(Q), [m] * len(names)
                lay(case, o, state)
                return sorted(o, key=lambda i: state[0][i] - case[0][i])

            order = top[1]
            for turn in range(OPT["turns"]):
                span = OPT["span"] + (turn % 3) * OPT["wider"]
                for a in range(-int(rnd() * span / 2), m - 10, span // 2):
                    order = by_time(cases[0], order)
                    a, b = max(a, 0), min(a + span, m)
                    frames = [frame(c, order, a, b) for c in cases]
                    part = order[a:b]
                    laid = [weigh(c, part, f) for c, f in zip(cases, frames)]
                    best = sum(z[0] for z in laid)
                    rank, was = {}, None
                    for i in reversed(part):
                        rank[i] = cases[0][0][i] + max([frames[0][1][i]] + [rank[j] + cases[0][1][i] for j in succ[i] if j in rank])
                    for it in range(OPT["fresh"]):
                        r = dict(rank)
                        for z in range(1 + int(rnd() * 6)):
                            r[part[int(rnd() * (b - a))]] += 3000 * (rnd() - 0.5)
                        o = anew(cases[0], part, frames[0], r, 400 * rnd() ** 2)
                        new = [weigh(c, o, f) for c, f in zip(cases, frames)]
                        s = sum(z[0] for z in new)
                        if was is None or s <= was:
                            rank, was = r, s
                            if s < best:
                                best, part, laid = s, o, new
                    keep = (best, part, laid)
                    for it in range(OPT["moves"]):
                        pairs = laid[int(rnd() * len(cases))][1]
                        if rnd() < OPT["free"] or not pairs:
                            k = int(rnd() * (b - a - 1))
                            near = [z for z in part[k:k + 40] if qs[z] == qs[part[k]]][:2 + int(rnd() * 5)]
                            i, j = near[-1], near[0]
                        else:
                            i, j = pairs[int(rnd() * len(pairs))]
                        o = moved(part, i, j) if i != j else None
                        if o:
                            new = [weigh(c, o, f) for c, f in zip(cases, frames)]
                            s = sum(z[0] for z in new)
                            if s <= best + OPT["warm"] * (1 - it / OPT["moves"]) ** 2 * rnd() ** 2:
                                best, part, laid = s, o, new
                                if s < keep[0]:
                                    keep = (s, o, new)
                    order = order[:a] + keep[1] + order[b:]
                top = (sum(z[2] for z in keep[2]), order)
            KEPT["order"], KEPT["best"] = top[1], top[0] / len(cases)
        for i in list(range(loads)) + [i for i in KEPT["order"] if i >= loads]:
            calls[i][1]()

    C3 = [(0, 512), (512, 1024), (1024, W)]
    CL = [C3[2], C3[0], C3[1]]
    CV = [(V, W), (0, 512), (512, 1024), (1024, V)]
    CN = [(1024, V), (0, 512), (512, 1024), (V, W)]

    def wrap(bank, z, src, chunks=((0, W),), o=0):
        for a, b in chunks:
            mm([(S(bank, o + a // 16, o + b // 16), S(z, 15 - l, 143 - l), S(src, a + l, b, 16), l == 0, l == 15) for l in range(16)])

    def wrap2(bank, z, src, a, b):
        if b >= 1024:
            wrap(bank, z, src, [(0, 1024) if b == 1024 else (a, b)])

    def shift(bank, ii, src, a, back, o=0, start=True):
        k = 16 if back else 112
        mm([(S(bank, o, o + 128), S(ii, k, k + 128), S(src, a, a + 128), start, True),
            (S(bank, o + 128, o + 256), S(ii, 64, 192), S(src, a + 128, a + 256), start, True)])

    def clear(bank):
        mm([(S(bank), S("Zero"), S("OH", 0, 512), True, True)])

    def put(out, w, src, start=True, whole=False):
        mm([(out, S(w, 0, 128), src, start, True)], more=[S(out[0], out[2], out[1] // 512 * 512 + 512)] if whole else [])

    dma("sp", S("curs"), ("cur", 0, W, T.cur[:]))
    for a, b in C3:
        dma("sp", S("cons", a, b), D("con", a, b))
    dma("sp", S("q0s"), D("q0"))
    dma("sp", S("K1"), D("kap"))
    dma("sp", S("v0s"), D("v0"))
    if "d" in OPT["dq1"]:
        dma("sp", S("q0c"), D("q0"))
    dma("sp", S("K2", 0, V), D("kap", 0, V))
    dma("sp", S("aims", parts=8), ("aim", 0, W, T.aim[:]))
    loads = len(calls)
    for i in range(loads):
        calls[i] = calls[i][:5] + (2000 + sum((c[3][0][2] - c[3][0][1]) * size(c[3][0]) * 0.22 for c in calls[:i + 1]),)

    iota(S("io3"), [[16, 8], [0, 16]], 0, -1)
    iota(S("pc", 0, 1), [[0, 1]], 0, 1, False)
    iota(S("vv", 0, 144), [[1, 144]], 128, -1, False)
    iota(S("iwr"), [[16, 96]], 0, 0)
    for l in range(16):
        ts(S("R", 128 * l, 128 * l + 128), S("io3"), float(-l), op.is_equal, 2.0, op.mult)
    ts(S("pm", 0, 1), S("pc", 0, 1), 15, op.bitwise_and)
    ts(S("v15"), S("vv", 0, 144), 15, op.bitwise_and)
    cp(S("col", 0, 1), S("pm", 0, 1))
    ts(S("col", 1, 2), S("pm", 0, 1), 2.0, op.mult)
    if OPT["oh"]:
        ts(S("col", 4, 5), S("pm", 0, 1), -2.0, op.mult)
    ts(S("col", 2, 3), S("pm", 0, 1), -1.0, op.mult, 143.0, op.add)
    ts(S("U0"), S("v15"), 0.0, op.is_equal)
    ts(S("U1"), S("v15"), 1.0, op.is_equal, EPS, op.mult)
    ts(S("Bm"), S("io3"), S("col", 0, 1), op.add, 0.0, op.is_equal)
    tt(S("U2"), S("U0"), S("U1"), op.add)
    ts(S("Zh"), S("vv", 0, 144), S("col", 2, 3), op.is_equal)
    cp(S("curh"), S("curs"))
    tt(S("C01"), S("Bm"), S("U2", 0, 128), op.mult)
    ts(S("Zb"), S("vv", 0, 144), S("col", 2, 3), op.is_equal)
    tt(S("C23"), S("Bm"), S("U2", 14, 142), op.mult)
    ts(S("iw"), S("iwr"), S("col", 0, 1), op.add)
    iota(S("IIb"), [[0, 2], [1, 128]], 0, -1)
    iota(S("io2"), [[2, W]], 0, 0)
    act(S("IIb"), S("IIb"), fn.Abs)
    act(S("IIb"), S("IIb"), fn.Relu, bias=1.0, scale=-1.0)
    act(S("IIf"), S("IIb"), fn.Copy)
    act(S("NIf"), S("IIb"), fn.Copy, scale=-1.0)
    for name, w in (("NIb", -1.0), ("Lb", L), ("Zero", 0.0), ("N8", -8.0), ("Is", 1.0 / BIG), ("Js", -1.0 / BIG), ("Ibs", 1.0 / BIG)):
        act(S(name), S("IIb", 0, 128), fn.Copy, scale=w)
    act(S("B4"), S("Bm"), fn.Copy, scale=0.25)
    ts(S("col", 3, 4), S("pc", 0, 1), 15.0, op.mult)
    ts(S("B8", parts=8), S("io3", parts=8), S("col", 3, 4, parts=8), op.is_equal, -L, op.mult)
    act(S("B8s", parts=8), S("B8", parts=8), fn.Copy, scale=1.0 / BIG)

    spots = [("PA", 0), ("PA", 512), ("PA", 1024), ("PC", 0)]
    for k, (bk, o) in enumerate(spots):
        mm([(S(bk, o + 96 * s, o + 96 * s + 96), S("R", 128 * (4 * k + s), 128 * (4 * k + s) + 128), S("curh"), True, True) for s in range(4)])
        if k < OPT["oh"]:
            act(S(bk, o, o + 384), S(bk, o, o + 384), fn.Abs, bias=S("col", 4, 5))
            act(S("OH", 384 * k, 384 * k + 384), S(bk, o, o + 384), fn.Relu, bias=1.0, scale=-1.0)
        else:
            ts(S("OH", 384 * k, 384 * k + 384), S(bk, o, o + 384), S("col", 1, 2), op.is_equal)

    def unpack(src, rest, o, lists):
        if lists:
            ts(S(lists, 0, 96), src, WHOLE, op.add, WHOLE, op.subtract)
        ts(S("J", o, o + 96), src, WHOLE, op.add, WHOLE, op.subtract)
        tt(rest, src, S("J", o, o + 96), op.subtract)
        if lists:
            ts(S(lists, 96, 192), rest, 1.0 / EPS, op.mult)
        ts(S("J", o + 96, o + 192), rest, 1.0 / EPS, op.mult)

    for a, b in C3:
        put(S("PB", a, b), "C01", S("OH", a, b))
        tt(S("X", a, b), S("PB", a, b), S("cons", a, b), op.mult)
        wrap2("PD", "Zh", "X", a, b)
    unpack(S("PD", 0, 96), S("PD", 96, 192), 0, "Ju")

    urgent(9000, shift, "PC", "IIb", "K1", V, False)
    urgent(9000, shift, "PC", "IIb", "q0s", V, False, 256)
    urgent(9000, act, S("t0"), S("PC"), fn.Copy)
    send(0, nxt, S("t0"), S("K2", V, W + 256))

    def choose(least, dj, ju, o0, sel):
        p1, p2, p3 = S("PC", 96, 192), S("PC", 192, 288), S("PD", 96, 192)
        if o0:
            ts(S(o0), S("PC", 0, 96), least, op.is_ge)
        ts(p1, S("PC", 0, 96), least, op.is_ge)
        ts(p2, S("PC", 0, 96), least, op.is_lt)
        if sel:
            p4 = S("PC", 288, 384)
            ts(p4, S("PC", 0, 96), least, op.is_lt, float(W), op.mult)
            tt(p4, p4, S("iw"), op.add)
            cp(S("selu"), p4)
        tt(p1, p1, S(dj, 0, 96), op.mult)
        tt(S("s3"), p2, S(dj, 96, 192), op.mult)
        tt(S("s4"), p1, S("iw"), op.add)
        ts(p3, S("PD", 0, 96), least, op.is_ge)
        tt(p3, p3, S("s3"), op.mult)
        urgent(2000, tt, S("jh"), p3, S("s4"), op.add)
        tt(S("jf"), p3, S("s4"), op.add)
        cp(S(ju), S("jf"))

    def partner(bank, k, ju, dk, rk, ract, chunks):
        for a, b in C3:
            urgent(2000, mm, [(S(bank, a + l, b, 16), S("R", 128 * l, 128 * l + 128), S("jh", a // 16, b // 16), False, l == 15) for l in range(16)], 32)
            urgent(2000, act, S("Wn", a, b), S(bank, a, b), fn.Copy)
        for c, (a, b) in enumerate(chunks):
            tt(S(dk, a, b), G("Wn", ju, a, b), S("io2", a, b), op.subtract)
            if ract >> c & 1:
                act(S(rk, a, b), S(dk, a, b), fn.Relu, bias=-1.0)
            else:
                ts(S(rk, a, b), S(dk, a, b), 1.0, op.subtract, 0.0, op.max)

    def differ(x, win, ju, to, w, a, b):
        act(S(to, a, b), G(win, ju, a, b), fn.Copy)
        put(x, w, S(to, a, b), False)

    def hits(x, y, dq, dk, rk, k, kh, how, a, b, h):
        least = 1.0
        if how == 2:
            least = 2.0
            act(S("HB", a, b), x, fn.Sign)
            mm([(y, S("IIb", 0, 128), S(dq, a, b), True, False), (y, S("IIb", 0, 128), S("HB", a, b), False, True)])
            act(S("FH", a, b), y, fn.Abs)
        elif how == 3:
            least = 2.0
            act(S("HB", a, b), S(dq, a, b), fn.Sign)
            put(x, "IIb", S("HB", a, b), False)
            act(S("FH", a, b), x, fn.Abs)
        elif how == 1:
            tt(h, x, S(dq, a, b), op.mult)
            act(S("FH", a, b), h, fn.Sign)
        else:
            tt(S("HB", a, b), x, S(dq, a, b), op.mult)
            ts(S("FH", a, b), S("HB", a, b), 0.0, op.is_gt)
        if k is None:
            mm([(y, S("IIf", 0, 128), S(dk, a, b), True, False), (y, S("N8"), S(rk, a, b), False, False)])
            put(y, "IIb", S("FH", a, b), False)
            act(kh, y, fn.Relu, bias=-least)
            return
        mm([(y, S("IIb", 0, 128), S(dk, a, b), True, False), (y, S("N8"), S(rk, a, b), False, False),
            (y, S("IIb", 0, 128), S("FH", a, b), False, True)])
        act(y, y, fn.Relu, bias=-least)
        tt(kh, y, S(k, a, b), op.mult)

    def rows23(late):
        for c, (a, b) in enumerate(C3):
            if (OPT["x23"] >> c & 1) == late:
                put(S("PA", a, b), "C23", S("OH", a, b))
                tt(S("X", a, b), S("PA", a, b), S("cons", a, b), op.mult)

    rows23(0)
    for c, (a, b) in enumerate(C3):
        if "d" in OPT["r0"][c::3]:
            act(S("A", a, b), S("q0s", a, b), fn.Identity, bias=-0.25)
    for k, (bank, ff, cnt, qb) in enumerate((("PB", "F0", "PC", "QB"), ("PA", "F1", "PD", "HB"))):
        for c, (a, b) in enumerate(C3):
            if OPT["r0"][3 * k + c] == "d":
                src = S("DD", W * k + a, W * k + b)
                tt(src, G("q0s", "Ju", a, b, 96 * k), S("A", a, b), op.subtract)
            else:
                src = S(bank, a, b)
                mm([(src, S("NIb"), S("q0s", a, b), True, False), (src, S("B4"), S("OH", a, b), False, False)])
                act(S(qb, a, b), G("q0s", "Ju", a, b, 96 * k), fn.Copy)
                put(src, "IIb", S(qb, a, b), False)
            ts(S(ff, a, b), src, TWO, op.add, TWO, op.is_equal)
            wrap2(cnt, "Zb", ff, a, b)
    tt(S("dJ", 0, 96), S("J", 0, 96), S("iw"), op.subtract)
    tt(S("dJ", 96, 192), S("J", 96, 192), S("iw"), op.subtract)
    for a, b in C3:
        put(S("PB", a, b), "IIb", S("K1", a, b))
    choose(8.5, "dJ", "j1u", "o0k", False)
    rows23(1)
    spread = len(calls) + 4
    partner("PB", "K1", "j1u", "DK1", "RK1", OPT["ra1"], CV)
    behind(spread, wrap, "PC", "Zh", "X", ((0, W),), 288)
    unpack(S("PC", 288, 384), S("PC", 384, 480), 192, None)
    for c, (a, b) in enumerate(CV):
        if OPT["dq1"][c] == "d":
            tt(S("DQ1", a, b), G("q0s", "j1u", a, b), S("q0c", a, b), op.subtract)
        else:
            y = S("PD", 0, 256) if a == V else S("PB", a, b)
            put(y, "NIb", S("q0s", a, b))
            differ(y, "q0s", "j1u", "AB0", "IIb", a, b)
            act(S("DQ1", a, b), y, fn.Sign)

    def lists2():
        flag, t = S("PC", 256, 352), S("PC", 352, 448)
        wrap("PC", "Zb", "DK1", o=256)
        tt(S("s5"), S("J", 96, 288), S("J", 192, 384), op.subtract)
        ts(flag, flag, SIXTEEN, op.add, SIXTEEN, op.is_equal)
        tt(flag, flag, S("o0k"), op.mult)
        tt(t, flag, S("s5", 0, 96), op.mult)
        tt(flag, flag, S("s5", 96, 192), op.mult)
        tt(t, t, S("J", 192, 288), op.add)
        tt(flag, flag, S("J", 288, 384), op.add)
        cp(S("J2u", 0, 96), t)
        cp(S("J2u", 96, 192), flag)
        tt(S("dJ2", 0, 96), t, S("iw"), op.subtract)
        tt(S("dJ2", 96, 192), flag, S("iw"), op.subtract)

    def aims(pa):
        for a, b in C3:
            mm([(S(pa, a, b), S("B8", parts=8), S("aims", a, b, parts=8), True, True)])
            act(S("AM", a, b), S(pa, a, b), fn.Copy)

    def newton(part):
        for a, b in C3:
            if part & 1:
                behind(len(calls) - 1, act, S("R0", a, b), S("K1", a, b), fn.Ln)
        if not part & 2:
            return
        for a, b in C3:
            behind(len(calls) - 1, act, S("R0", a, b), S("R0", a, b), fn.Exp, 0.6931472, -1.0)
        act3("SQ", "R0", fn.Square, scale=0.5)
        act3("R0", "R0", fn.Copy, scale=-1.0)

    def signed(chunks, spot):
        for a, b in chunks:
            y = spot(a, b)
            mm([(y, S("IIb", 0, 128), S("DK1", a, b), True, False), (y, S("N8"), S("RK1", a, b), False, True)])
            act(y, y, fn.Relu)
            tt(y, y, S("K1", a, b), op.mult)
            tt(S("KS", a, b), y, S("DQ1", a, b), op.mult)

    def newton2(bank):
        for a, b in C3:
            put(S(bank), "IIb", S("K1", a, b))
            tt(S("RR", a, b), S(bank), S("SQ", a, b), op.mult)
        dma("pool", S("RR"), S("R0"), True)

    def shot(x, pa, pb):
        v0, ii, big, nbig, vg = (("v0s", "IIb", "IIb", "NIb", "QB"), ("V0p", "IIf", "IIf", "NIf", "VG"))[x]
        v1, a2, y2, vout = (("V1a", "A2a", "Y2a", "V0p"), ("V1b", "A2b", "Y2b", "Wn"))[x]

        def X(a, b):
            return S("PD", 0, 256) if a == V else S(pa, a, b)

        def Y(a, b):
            return S("PD", 256, 512) if a == V else S(pb, a, b)

        fast = x == 1 and OPT["fast"]
        gone = x == 1 and OPT["lead"] & 1
        for a, b in CV:
            if a == V and gone:
                put(Y(a, b), "Lb", S("K2", W, W + 256))
            elif a == V and fast:
                put(X(a, b), "IIf", S("KS", a, b))
                act(S("CQ", a, b), S(v0, a, b), fn.Copy)
            elif not (x == 1 and OPT["m7"] >> (a // 512) & 1):
                put(X(a, b), big, S(v0, a, b), whole=b == V)
        if not gone:
            clear("PC")
            shift("PC", ii, v0, V, False, start=False)
        for a, b in CV:
            if a < V and x == 1 and OPT["m7"] >> (a // 512) & 1:
                act(S(vg, a, b), G(v0, "j1u", a, b), fn.Copy)
                tt(X(a, b), X(a, b), S(vg, a, b), op.subtract)
            elif a < V or not fast:
                differ(X(a, b), v0, "j1u", vg, nbig, a, b)
        if x == 0 and OPT["lead"] & 1:
            act(S("QV"), S("QB", V, W), fn.Copy)
        for c, (a, b) in enumerate(CV):
            how = 2 if OPT["h1"] >> (4 * x + c) & 1 else OPT["fa1"] >> x & 1
            if a == V and gone:
                continue
            if a == V and fast:
                tt(S("tv"), G(v0, "j1u", a, b), S("CQ", a, b), op.subtract)
                tt(X(a, b), X(a, b), S("tv"), op.mult)
                if fast == 1:
                    act(X(a, b), X(a, b), fn.Relu, scale=-1.0)
                else:
                    ts(X(a, b), X(a, b), -1.0, op.mult, 0.0, op.max)
                tt(S("DL1", a, b), X(a, b), S("DQ1", a, b), op.mult)
            elif OPT["ks"][c] in "kK" and (x == 1 or OPT["ks"][c] == "k"):
                if x == 0:
                    put(Y(a, b), "IIb", S("DK1", a, b))
                    tt(S("KS", a, b), Y(a, b), S("K1", a, b), op.mult)
                hits(X(a, b), Y(a, b), "DQ1", "KS", "RK1", None, S("KH1", a, b), how if how == 2 else OPT["kf"], a, b, S("HB", a, b))
            elif x == 1 and OPT["ks"][c] != "-":
                act(Y(a, b), X(a, b), fn.Sign)
                tt(Y(a, b), Y(a, b), S("KS", a, b), op.mult)
                act(S("KH1", a, b), Y(a, b), fn.Relu)
            else:
                hits(X(a, b), Y(a, b), "DQ1", "DK1", "RK1", "K1", S("KH1", a, b), how, a, b, Y(a, b))
            if a == V:
                if not fast:
                    tt(S("DL1", a, b), X(a, b), S("KH1", a, b), op.mult)
                shift("PC", "NIf", "DL1", V, False, start=False)
                act(S(("t1", "t3")[x]), S("PC", 0, 256), fn.Copy)
                if x == 0:
                    newton(OPT["ln"])
                send(1 + 2 * x, nxt, S(("t1", "t3")[x]), S(v1, V, W))
                if fast:
                    act(X(a, b), S("tv"), fn.Sign)
                    tt(X(a, b), X(a, b), S("KS", a, b), op.mult)
                    act(S("KH1", a, b), X(a, b), fn.Relu, scale=-1.0)
                put(Y(a, b), "Lb", S("K2", W, W + 256))
            elif OPT["v1pe"] >> (4 * x + c) & 1:
                tt(S("DL1", a, b), X(a, b), S("KH1", a, b), op.mult)
                mm([(Y(a, b), S(ii, 0, 128), S(v0, a, b), True, False), (Y(a, b), S("NIf", 0, 128), S("DL1", a, b), False, True)])
                act(S(v1, a, b), Y(a, b), fn.Copy)
                put(X(a, b), "Lb", S("q0s", a, b))
                tt(S("q1", a, b), X(a, b), S(v1, a, b), op.add)
            else:
                tt(Y(a, b), X(a, b), S("KH1", a, b), op.mult)
                act(S("DL1", a, b), Y(a, b), fn.Copy)
                tt(S(v1, a, b), S(v0, a, b), Y(a, b), op.subtract)
                put(X(a, b), "Lb", S("q0s", a, b))
                if OPT["q1pe"] >> (4 * x + c) & 1:
                    put(X(a, b), "IIf", S(v1, a, b), False)
                    act(S("q1", a, b), X(a, b), fn.Copy)
                else:
                    tt(S("q1", a, b), X(a, b), S(v1, a, b), op.add)
            if a < V:
                if OPT["cqdma"] >> x & 1:
                    dma("sp", S("CQ", a, b), S("q1", a, b))
                else:
                    act(S("CQ", a, b), S("q1", a, b), fn.Copy)
        if x == 0:
            lists2()
            aims(pa)
        tt(S("q1", V, W), Y(V, W), S(v1, V, W), op.add)
        act(S("CQ", V, W), S("q1", V, W), fn.Copy)

        if x == 0:
            for c, (a, b) in enumerate(CV):
                if (OPT["ks"][c] in "35" or OPT["h1"] >> (4 + c) & 1) and OPT["dq1"][c] == "d":
                    act(S("DQ1", a, b), S("DQ1", a, b), fn.Sign)
                if OPT["ks"][c] == "K":
                    put(S(pa, a, b), "IIb", S("DK1", a, b))
                    tt(S("KS", a, b), S(pa, a, b), S("K1", a, b), op.mult)
            signed([(a, b) for c, (a, b) in enumerate(CV) if OPT["ks"][c] == "3"], lambda a, b: S(pa, a, b))
        elif OPT["nw"] == 1:
            newton2("PC")
        dma("sp", S("CP", 0, V), S(v1, 0, V))
        dma("sp", S("CP", V, W), S(v1, V, W))
        for k, (ab, ff, cnt) in enumerate((("AB0", "F0", "PC"), ("AB1", "F1", "PD"))):
            for c, (a, b) in enumerate(C3):
                src = S("DD", W * k + a, W * k + b)
                tt(src, G("q1", "J2u", a, b, 96 * k), S("CQ", a, b), op.subtract)
                act(S(ab, a, b), src, fn.Abs, scale=NEAR / L)
                if OPT["ta2"] >> (3 * k + c) & 1:
                    act(S(ff, a, b), S(ab, a, b), fn.Sign, bias=252.5 / 256, scale=-1.0)
                else:
                    ts(S(ff, a, b), S(ab, a, b), 252.5 / 256, op.is_lt, 0.5, op.subtract)
                wrap2(cnt, "Zb", ff, a, b)
        for a, b in C3:
            put(S(pb, a, b), "IIb", S("K2", a, b))
        choose(0.25, "dJ2", "j2u", None, True)
        ahead = OPT["lead"] & 2
        C4, first = CV if ahead else CL, len(calls)
        for a, b in C4:
            act(S("DQ2", a, b), G("DD", "selu", a, b), fn.Sign)
            tt(S("E2", a, b), G(v1, "j2u", a, b), S("CP", a, b), op.subtract)
        partner(pb, "K2", "j2u", "DK2", "RK2", OPT["ra2"], C4)

        def back():
            tt(S(pb, V, W), S(pb, V, W), S("DA", V, W), op.mult)
            act(S("tv"), S(pb, V, W), fn.Copy)
            shift("PC", "IIf", "tv", 0, True, start=False)
            shift("PC", "IIf", "A", V, True, start=False)
            act(S(("t2", "t4")[x]), S("PC", 0, 256), fn.Copy)
            send(2 + 2 * x, prv, S(("t2", "t4")[x]), S(a2, V, W))
            tt(S(y2, V, W), S(pb, V, W), S("E2", V, W), op.mult)
            if x == 1:
                mm([(S("PD", 256, 384), S("IIf", 16, 144), S("Y2a", V, H), True, False),
                    (S("PD", 256, 384), S("IIf", 16, 144), S("Y2b", V, H), False, True),
                    (S("PD", 384, 512), S("IIf", 64, 192), S("Y2a", H, W), True, False),
                    (S("PD", 384, 512), S("IIf", 64, 192), S("Y2b", H, W), False, True)])
                act(S("t5"), S("PD", 256, 512), fn.Copy)
                send(5, prv, S("t5"), S("YL"))

        mine = len(calls)
        if ahead:
            act(S("VG", 0, 256), G(v1, "j2u", V, W), fn.Copy)
            act(S("VG", 256, 512), G("q1", "j2u", V, W), fn.Copy)
            act(S("GA"), G("AM", "j2u", V, W), fn.Copy)
            put(S("PD", 0, 256), "Is", S("VG", 0, 256))
        for c, (a, b) in enumerate(C4):
            xx, yy, how = S(pa, a, b), S(pb, a, b), OPT["p4"][c]
            put(xx, "NIb", S("DQ2", a, b), whole=b == V)
            am = (xx, S("B8s", parts=8), S("aims", a, b, parts=8))
            hits(xx, yy, "E2", "DK2", "RK2", "K2", yy, 3 if OPT["h2"] >> c & 1 else OPT["fa2"] >> c & 1, a, b, xx)
            unit = 1.0
            fine[0] = OPT["fine4"] >> c & 1
            if how == "f":
                put(xx, "Is", S(v1, a, b))
                tt(S("Wn", a, b), yy, S("E2", a, b), op.mult)
                mm([(xx, S("Is"), S("Wn", a, b), False, False), (xx, S("Is"), S("q1", a, b), False, False), am + (False, True)])
            else:
                tt(xx, yy, S("E2", a, b), op.mult)
                tt(xx, xx, S(v1, a, b), op.add)
                if how == "a":
                    tt(S("Wn", a, b), xx, S("q1", a, b), op.add)
                    mm([(xx, S("Is"), S("Wn", a, b), True, False), am + (False, True)])
                else:
                    tt(xx, xx, S("q1", a, b), op.add)
                    tt(xx, xx, S("AM", a, b), op.add)
                    unit = 1.0 / BIG
            fine[0] = 0
            act(S("A", a, b), xx, fn.Copy, scale=unit)
            if a == V:
                z = S("PD", 0, 256)
                mm([(z, S("Js"), S("Wn", V, W), False, False), (z, S("Is"), S("VG", 256, 512), False, False), (z, S("Ibs"), S("GA"), False, True)])
                clear("PC")
                shift("PC", "IIf", "A", V, True, start=False)
                tt(S("DA", V, W), z, S("A", V, W), op.subtract)
                back()
                for i in range(first, len(calls)):
                    if i >= mine or calls[i][3][0][1:3] == (V, W):
                        hints.append((i, i + 1, OPT["up2"]))
            elif OPT["p5"][(a // 512 + 1) % 3] == "d":
                act(S("CQ", a, b), xx, fn.Copy, scale=unit)
            else:
                if b == W:
                    act(S("CQ", V, W), S(pa, V, W), fn.Copy, scale=unit)
                if unit != 1.0:
                    act(xx, xx, fn.Copy, scale=unit)

        if not ahead:
            clear("PC")
            shift("PC", "IIf", "A", V, True, start=False)
        for a, b in CV[1:] if ahead else CV:
            xx, yy = S(pa, a, b), S(pb, a, b)
            if a == V or OPT["p5"][(a // 512 + 1) % 3] == "d":
                tt(S("DA", a, b), G("A", "j2u", a, b), S("CQ", a, b), op.subtract)
            else:
                act(S("VG", a, b), G("A", "j2u", a, b), fn.Copy)
                tt(S("DA", a, b), S("VG", a, b), xx, op.subtract)
            if x == 0 and a == 0:
                newton(3 - OPT["ln"])
            if a == V:
                back()
            else:
                tt(yy, yy, S("DA", a, b), op.mult)
                if OPT["b5"] >> (a // 512) & 1:
                    put(xx, "IIf", S("A", a, b))
                    act(S("DA", a, b), yy, fn.Copy)
                    mm([(xx, S("IIf", 0, 128), S(z, a, b), False, True) for z in ("DA", "A")])
                    act(S(a2, a, b), xx, fn.Copy)
                else:
                    fine[0] = OPT["fine5"]
                    tt(xx, yy, S("A", a, b), op.add)
                    if OPT["m6"] >> (3 * x + a // 512) & 1:
                        tt(xx, xx, S("A", a, b), op.add)
                        act(S(a2, a, b), xx, fn.Copy)
                    else:
                        tt(S(a2, a, b), xx, S("A", a, b), op.add)
                    fine[0] = 0
                tt(S(y2, a, b), yy, S("E2", a, b), op.mult)
        if 2 * x == OPT["nw"]:
            newton2("PC")
        if x == 0:
            signed([(a, b) for c, (a, b) in enumerate(CV) if OPT["ks"][c] == "5"], lambda a, b: S("PD", 0, b - a))
        dma("pool", S("ZZ", 0, V if x == 0 else 512), S(y2, 0, V if x == 0 else 512), True)

        chunks = CN if OPT["c6"] else C3
        last = x == 1 and OPT["yvacc"]
        if last:
            dma("sp", D("yv"), S("V0p"))

        def spot(a, b):
            if a < 512:
                return S(pa, a, b)
            return S("PC") if a < 1024 else S("PD", a - 1024, b - 1024)
        for a, b in chunks:
            if a < V and not OPT["m6"] >> (3 * x + a // 512) & 1:
                put(S(pa, a, b), "IIf", S(a2, a, b), whole=b == V)
        if x == 1:
            put(S("PC"), "IIf", S("ZZ", 512, 1024))
            put(S("PC"), "IIf", S("Y2b", 512, 1024), False)
            put(S("PD"), "IIf", S("ZZ", 1024, W))
            put(S("PD", 0, 256), "IIf", S("Y2b", 1024, V), False)
            put(S("PD", 256, 512), "IIf", S("YL"), False)
        if x == 0 and OPT["lead"] & 1:
            chunks, first = chunks[:3], len(calls)
            xx, yy, zz = S("PD", 0, 256), S("PD", 256, 512), S(pb, V, W)
            act(S("VG", V, W), G(a2, "j1u", V, W), fn.Copy)
            put(xx, "IIf", S(a2, V, W))
            put(xx, "NIf", S("VG", V, W), False)
            tt(yy, xx, S("KH1", V, W), op.mult)
            tt(zz, yy, S("VG", V, W), op.add)
            tt(yy, yy, S(a2, V, W), op.subtract)
            for z in (zz, yy):
                ts(z, z, 0.1875, op.min, -0.1875, op.max)
            tt(zz, S("QV"), zz, op.subtract)
            tt(S("V0p", V, W), yy, S(v0, V, W), op.add)
            tt(S("Y1", V, W), xx, S("DL1", V, W), op.mult)
            tt(zz, zz, S("V0p", V, W), op.subtract)
            tt(yy, zz, S("KS", V, W), op.mult)
            act(yy, yy, fn.Relu, scale=-1.0)
            tt(S("DL1", V, W), yy, S("DQ1", V, W), op.mult)
            clear("PC")
            shift("PC", "IIf", "V0p", V, False, start=False)
            shift("PC", "NIf", "DL1", V, False, start=False)
            act(S("t3"), S("PC", 0, 256), fn.Copy)
            send(3, nxt, S("t3"), S("V1b", V, W))
            hints.append((first, len(calls), OPT["up1"]))
            act(yy, yy, fn.Sign)
            tt(yy, yy, S("KS", V, W), op.mult)
            act(S("KH1", V, W), yy, fn.Abs)
        for a, b in chunks:
            if a == V:
                act(S("VG", a, b), G(a2, "j1u", a, b), fn.Copy)
                mm([(S(pa, a, b), S("IIf", 0, 128), S(a2, a, b), True, False), (S(pa, a, b), S("NIf", 0, 128), S("VG", a, b), False, True)])
            elif OPT["m6"] >> (3 * x + a // 512) & 1:
                act(S("VG", a, b), G(a2, "j1u", a, b), fn.Copy)
                tt(S(pa, a, b), S(pa, a, b), S("VG", a, b), op.subtract)
            else:
                differ(S(pa, a, b), a2, "j1u", "VG", "NIf", a, b)
        for a, b in chunks:
            xx, yy = S(pa, a, b), S(pb, a, b)
            tt(yy, xx, S("KH1", a, b), op.mult)
            tt(xx if x == 1 and a == 0 and OPT["z0"] else S("Y1", a, b), xx, S("DL1", a, b), op.mult)
            tt(yy, yy, S(a2, a, b), op.subtract)
            if last:
                ts(S(vout, a, b), yy, 0.1875, op.min, -0.1875, op.max)
                dma("pool", D("yv", a, b), S(vout, a, b), True)
            else:
                ts(yy, yy, 0.1875, op.min, -0.1875, op.max)
                if x == 0 and a < V and OPT["m7"] >> (a // 512) & 1:
                    tt(yy, yy, S(v0, a, b), op.add)
                    act(S(vout, a, b), yy, fn.Copy)
                else:
                    tt(S(vout, a, b), yy, S(v0, a, b), op.add)
            if x == 1:
                if not last:
                    dma("sp", D("yv", a, b), S(vout, a, b))
                bank = spot(a, b)
                if a == 0 and not OPT["z0"]:
                    put(bank, "IIf", S("Y1", a, b))
                    put(bank, "IIf", S("ZZ", a, b), False)
                elif a == 0:
                    tt(bank, bank, S("ZZ", a, b), op.add)
                else:
                    put(bank, "IIf", S("Y1", a, b), False)
                if b != V:
                    a = a // 512 * 512
                    tt(S("VG", a, b), spot(a, b), S("RR", a, b), op.mult)
                    dma("act", D("yg", a, b), S("VG", a, b))
        if x == 0:
            dma("pool", S("ZZ"), S("Y1"), True)

    act3("ZZ", "K1", fn.Square)
    act3("ZZ", "ZZ", fn.Copy, scale=-1.0)
    shot(0, "PA", "PB")
    shot(1, "PB", "PA")
    issue()

    g.wait_ge(T.sem.sent, count["sent"])
    for q in ("pe", "dve", "act", "pool"):
        g.wait_ge(T.sem[q], count[q])
    for s in dmas:
        g.wait_ge(T.sem[s], 16)
